import numpy as np, ml_dtypes
CORES = [2,6,10,14,18,22,26,30]
N = 8
import mx_ref
BF = ml_dtypes.bfloat16
def entries(a):
    return np.ascontiguousarray(a.T).reshape(-1)
def table(e):
    return np.ascontiguousarray(np.reshape(e, (-1, 16)).T).astype(np.int32)
def pick(q, e):
    c = np.concatenate([q[0].reshape(128, -1, 4), np.zeros((128, 1, 4), np.uint8)], axis=1); s = np.concatenate([q[1], np.ones((16, 1), np.uint8)], axis=1)
    return (np.ascontiguousarray(c[:, e].reshape(128, -1)), np.ascontiguousarray(s[:, e]))
def join(*qs):
    return (np.concatenate([q[0] for q in qs], axis=1), np.concatenate([q[1] for q in qs], axis=1))
def put(q, e, v):
    c, s = q[0].reshape(128, -1, 4).copy(), q[1].copy(); c[:, e] = v[0].reshape(128, -1, 4); s[:, e] = v[1]
    return (c.reshape(128, -1), s)
def pk(c, s):
    return (np.ascontiguousarray(c), mx_ref.live(s))
def emit(q):
    return q[0], q[1]
def decode(q):
    o = []
    for b in range(4):
        e = np.zeros((128, 128, 4), np.float32); e[np.arange(128), np.arange(128), b] = 1
        o.append(mx_ref.matmul(mx_ref.quantize(e.reshape(128, 512).astype(BF)), q))
    return np.stack(o, axis=2).reshape(128, -1)
def f(rng, *shape):
    return mx_ref.flush((rng.standard_normal(shape, dtype=np.float32) * np.exp2(rng.integers(-2, 3, shape[:-1] + (1,)))).astype(BF))
def wide(rng, *shape, cols=0):
    v = rng.standard_normal(shape, dtype=np.float32) * np.exp2(rng.integers(-12, 13, shape)).astype(np.float32)
    if cols: v *= np.repeat(np.exp2(rng.integers(-cols, cols + 1, shape[:-2] + (1, shape[-1] // 4))) * (rng.random(shape[:-2] + (1, shape[-1] // 4)) > 0.0625), 4, axis=-1).astype(np.float32)
    return mx_ref.flush(v.astype(BF))
M, K, J, R = 256, 64, 3, 3
def unpack(q):
    c = q[0].reshape(16, 8, -1, 4).astype(int)
    s = np.broadcast_to(q[1].astype(int)[:, None, :, None], c.shape)
    k = np.unique(q[1]).astype(int)
    k = np.concatenate([k, np.ones(4 + k.size % 2, int)])
    here = np.zeros((256, 256), np.uint8)
    here[s, c] = c
    z = np.zeros((128, k.size, 4), np.uint8)
    z[:64] = here[k].reshape(-1, 64, 4).transpose(1, 0, 2)
    v = decode((z.reshape(128, -1), np.repeat(k[None], 16, axis=0).astype(np.uint8)))
    held = np.zeros((256, 256), np.float32)
    held[k] = v.reshape(128, -1, 4)[:64].transpose(1, 0, 2).reshape(-1, 256)
    return held[s, c].reshape(128, -1)
def big(v):
    v = np.array(v)
    v[np.abs(v.astype(np.float32)) < np.float32(2.0 ** -16)] = 0
    return v
def bf(v):
    return np.asarray(v, np.float32).astype(BF)
def parts(t):
    return t.reshape(N, 128, -1, 4)
def store(e):
    return np.stack([table(v.T) for v in e.reshape(N, M, J)])
def setup_inputs(rng):
    return {"x": big(f(rng, N, 128, 4 * M)), "u": np.array(f(rng, N, 128, 512)), "w": np.array(f(rng, N, 128, 512)), "nb": store(rng.integers(0, N * M, (N * M, J)))}
def setup_inputs_chain(rng):
    d, n = setup_inputs(rng), N * M
    at = rng.permutation(n)
    e = at[rng.integers(0, np.arange(1, n + 1)[:, None], (n, J))]
    j = np.arange(n - 1)
    e[j, rng.integers(0, J, n - 1)] = at[j + 1]
    nb, h = np.zeros((n, J), int), np.zeros(n, int)
    nb[at], h[at] = e, np.arange(n)
    x, u = parts(d["x"]), parts(d["u"])
    x[:, :16] = 0
    u[:, :, :R] = 0
    for k in range(12):
        x[:, 4 * (k // 4), :, k % 4] = bf((h >> k & 1).reshape(N, M))
        u[:, 4 * (k // 4), :R, k % 4] = 2.0 ** k
    return {"x": x.reshape(N, 128, -1), "u": u.reshape(N, 128, -1), "w": d["w"], "nb": store(nb)}
def setup_inputs_deep(rng):
    d, n = setup_inputs(rng), N * M
    at = np.sort(rng.permutation(n).reshape(-1, 4), axis=1)
    nb, low = np.zeros((n, J), int), np.zeros(n)
    for k in range(4): nb[at[:, k]] = at[:, [min(k + i, 3) for i in (1, 2, 3)]]
    low[at[1::2]] = 11
    x, u = parts(d["x"]), parts(d["u"])
    u[:, :, :R] = 0
    for t, k in enumerate(rng.permutation(R)):
        v = np.zeros(n)
        v[at] = [(4, 4, 4, 7), (4, 7, 4, 6), (7, 7, 5, 5)][k]
        x[:, 40 * t:40 * t + 40] = bf((v - low).reshape(N, 1, M, 1) * 2.0 ** 27)
        u[:, 40 * t:40 * t + 40, t] = 2.0 ** 30
    return {"x": x.reshape(N, 128, -1), "u": u.reshape(N, 128, -1), "w": d["w"], "nb": store(rng.permuted(nb, axis=1))}
def setup_inputs_peaks(rng):
    d, n = setup_inputs(rng), N * M
    who = rng.permutation(N)
    peaks = [M * who[t] + rng.permutation(M)[:K] for t in range(R)]
    lone = np.zeros(n, bool)
    lone[np.concatenate(peaks)] = True
    lone[M * who[R]:M * who[R] + M] = True
    m = np.flatnonzero(~lone)
    nb = np.repeat(np.arange(n)[:, None], J, axis=1)
    x, u = parts(d["x"]), parts(d["u"])
    u[:, :, :R] = mx_ref.flush(bf(u[:, :, :R].astype(np.float32) * np.float32(2.0 ** -6)))
    for t in range(R):
        nb[m, t] = rng.permutation(np.concatenate([peaks[t], peaks[t], rng.choice(peaks[t], m.size - 2 * K)]))
        level = rng.integers(1, 4, n)
        level[peaks[t]] = 7
        x[:, 32 * t:32 * t + 16] = 0
        u[:, 32 * t:32 * t + 16, :R] = 0
        x[:, 32 * t, :, 0] = bf(level.reshape(N, M))
        u[:, 32 * t, t, 0] = 1024
    return {"x": x.reshape(N, 128, -1), "u": u.reshape(N, 128, -1), "w": d["w"], "nb": store(rng.permuted(nb, axis=1))}
def setup_inputs_spread(rng):
    return {**setup_inputs(rng), "x": big(wide(rng, N, 128, 4 * M, cols=6))}
def setup_inputs_ties(rng):
    d = setup_inputs(rng)
    x, u = parts(d["x"]), parts(d["u"])
    x[:, :16] = 0
    x[:, 0, :, 0] = 4
    u[:, :, :R] = 0
    u[:, 0, :R, 0] = -2.0 ** 30
    for t in range(R):
        p = 32 * t + 32
        x[:, p:p + 16] = 0
        x[:, p, :, 0] = bf(rng.integers(4, 8, (N, M)))
        u[:, p, t, 0] = 1024
    return {"x": x.reshape(N, 128, -1), "u": u.reshape(N, 128, -1), "w": d["w"], "nb": d["nb"]}
def check_inputs(d):
    b = []
    for k in ("x", "u", "w"):
        v = np.abs(d[k].astype(np.float32))
        if not (np.isfinite(v).all() and ((v == 0) | (v >= 2.0 ** -30) & (v <= 2.0 ** 30)).all()): b.append("a value of " + k)
    if d["nb"].min() < 0 or d["nb"].max() >= N * M: b.append("nb")
    return b
def reference(x, u, w, nb):
    node = np.arange(N * M)
    near = np.concatenate([entries(nb[r]).reshape(J, M).T for r in range(N)])
    near = np.sort(np.concatenate([node[:, None], near], axis=1), axis=1)
    state = join(*[mx_ref.quantize(np.ascontiguousarray(x[r])) for r in range(N)])
    own = node.reshape(N, M)
    pieces = [np.concatenate([own[r], np.full(-M % 128, -1)]).reshape(-1, 128) for r in range(N)]
    qu = [mx_ref.quantize(np.ascontiguousarray(u[r][:, :16])) for r in range(N)]
    y, rt = np.zeros((N, 128, M), np.float32), np.zeros((N, 1, R * M), np.float32)
    oc, osc = np.zeros((N, 128, 4 * M), np.uint8), np.zeros((N, 16, M), np.uint8)
    for t in range(R):
        h = np.concatenate([np.concatenate([mx_ref.matmul(pick(state, e), qu[r])[:, t] for e in pieces[r]])[:M] for r in range(N)]) + np.float32(0)
        root = near[node, np.argmax(h[near], axis=1)]
        while (root[root] != root).any(): root = root[root]
        size = np.bincount(root, minlength=N * M)
        chosen = np.argsort(-size, kind="stable")[:K]
        m = np.flatnonzero(np.isin(root, chosen) & (root != node))
        if m.size:
            v = unpack(state).reshape(128, N * M, 4)
            v = (v[:, m] + v[:, root[m]]) * np.float32(0.5)
            v = np.concatenate([v, np.zeros((128, -m.size % 4, 4), np.float32)], axis=1)
            new = mx_ref.quantize(np.ascontiguousarray(v.reshape(128, -1).astype(BF)))
            state = put(state, m, pick(new, np.arange(m.size)))
        rt[:, 0, t * M:t * M + M] = root.reshape(N, M)
    for r in range(N):
        y[r] = mx_ref.matmul(mx_ref.quantize(np.ascontiguousarray(w[r])), pick(state, own[r]))
        oc[r], osc[r] = emit(pick(state, own[r]))
    return {"y": y, "oc": oc, "osc": osc, "rt": rt}

@@ -1,0 +1,625 @@
+from concourse.bass import DstId, RemoteDMATransfer
+from concourse.mybir import dt, AluOpType, AxisListType, ActivationFunctionType
+
+N, M, K, J, R = 8, 256, 64, 3, 3
+F32, I32, U16, BF, CODE, PLANE = "float32", "int32", "uint16", "bfloat16", "float8_e4m3fn_x4", "uint8"
+NA = 7
+ND = 16 - NA
+CA = 320
+DUMMY = 2200
+
+SCRATCH = {}
+
+
+def _sb(name, n, d):
+    SCRATCH[name] = ("sbuf", [128, n], d)
+
+
+for _n, _w, _d in [
+    ("xs", 1024, BF), ("us", 512, BF), ("ws", 512, BF), ("nbs", 48, I32), ("nbo", 16, U16), ("nbl", 48, U16),
+    ("qu", 128, CODE), ("su", 128, PLANE), ("qw", 128, CODE), ("sw", 128, PLANE),
+    ("et", 2048, BF), ("qe", 512, CODE), ("se", 512, PLANE), ("io512", 512, F32),
+    ("ci", 32, I32), ("cf", 32, F32), ("jr", 48, I32), ("tmpi", 128, I32), ("lst", 160, U16),
+    ("iot16", 256, F32), ("iot32", 64, F32), ("rst", 768, F32), ("sv", 256, F32), ("tri", 64, F32), ("kk", 64, F32),
+    ("nbi", 48, I32), ("nhi", 48, I32), ("nlo", 48, I32), ("qn", 160, F32), ("on", 48, U16), ("mt", 768, F32), ("mf", 768, F32),
+    ("hs", 8, F32), ("q", 160, F32), ("xx", 96, F32), ("wt", 128, F32), ("oo", 16, U16), ("d1", 256, F32),
+    ("gm", 768, F32), ("tt", 768, F32), ("ss", 768, F32), ("mk", 256, F32), ("hi", 16, I32), ("lof", 16, F32),
+    ("sm", 160, F32), ("p2", 16, F32), ("q2", 16, F32), ("rb", 256, F32), ("rf", 256, F32),
+    ("ja", 256 * (NA + 1), BF), ("acc", 24, F32),
+    ("rti", 256, I32), ("rta", 256, F32), ("rtb", 256, F32), ("rto", 768, F32),
+    ("r2", 16, F32), ("r2i", 48, I32), ("r2f", 128, F32), ("o3", 16, U16), ("mk3", 256, F32),
+    ("s1", 64, F32), ("sz", 16, F32), ("yb", 512, BF), ("yt", 512, BF), ("jy", 512, BF), ("cc", 16, F32),
+    ("bb", 64, F32), ("bt", 64, F32), ("fl", 48, F32), ("sc", 32, F32), ("tm", 64, F32), ("pf", 16, F32),
+    ("bs", 96, F32), ("vo", 16, U16), ("lw", 2480, F32), ("lt", 160, F32), ("zz", 32, F32), ("zs", 16, F32),
+    ("cht", 64, F32), ("pl", 80, U16), ("ht", 1024, BF), ("yo", 256, F32),
+]:
+    _sb(_n, _w, _d)
+ALIAS = {}
+for _b, _d, _names in (("kc", F32, [("thx", 16), ("th", 16), ("c128", 32), ("ones", 32), ("mym", 16), ("dum", 16)]),
+                       ("wk", F32, [("cor", 16), ("cs", 8), ("rr", 8), ("vv", 16), ("ch", 16)]),
+                       ("wb", BF, [("zb", 256), ("ob", 256), ("jd", 256 * ND), ("js", 256 * ND)])):
+    _o = 0
+    for _n, _w in _names:
+        ALIAS[_n] = (_b, _o, _w)
+        _o += _w
+    _sb(_b, _o, _d)
+for _t in range(R):
+    _sb("qh%d" % _t, 160, F32)
+    _sb("hl%d" % _t, 128, BF)
+    for _s in "abc":
+        _sb("c%s%d" % (_s, _t), 128, CODE)
+        _sb("p%s%d" % (_s, _t), 128, PLANE)
+    _sb("cr%d" % _t, 256, CODE)
+    _sb("pr%d" % _t, 256, PLANE)
+for _t in range(R + 1):
+    _sb("ct%d" % _t, 512, CODE)
+    _sb("pt%d" % _t, 512, PLANE)
+SCRATCH["psh"] = ("psum", [128, 1024], F32)
+SCRATCH["psd"] = ("psum", [128, 2048], F32)
+SCRATCH["psy"] = ("psum", [128, 512], F32)
+
+SEMAPHORES = ["kv", "ka", "kt", "kg", "ls", "dx", "du", "dw", "dn", "dout", "an"] + \
+    ["%s%d" % (_s, _t) for _s in ("ah", "az", "aa", "ab", "ac") for _t in range(R)]
+
+OP = AluOpType
+ACT = ActivationFunctionType
+
+
+def rank_program(g, core, T, topo):
+    rank = T.rank_of(core)
+    if rank is None:
+        return
+    cores = list(T.cores)
+    queues = {"v": g.vector, "a": g.scalar, "t": g.tensor, "g": g, "s": g.sync}
+    own_sem = {"v": "kv", "a": "ka", "t": "kt", "g": "kg"}
+    count = {s: 0 for s in SEMAPHORES}
+    known = {q: {} for q in queues}
+    hist = {}
+
+    def V(name, c0=0, c1=None, s=1, p0=0, p1=128):
+        if name in ALIAS:
+            b, o, w = ALIAS[name]
+            return (b, o + c0, o + (w if c1 is None else c1), s, p0, p1)
+        return (name, c0, SCRATCH[name][1][1] if c1 is None else c1, s, p0, p1)
+
+    def IND(win, off):
+        return ("*", win, off)
+
+    def ap(x):
+        if not isinstance(x, tuple):
+            return x
+        if x[0] == "*":
+            return ap(x[1]).indirect(ap(x[2]))
+        name, c0, c1, s, p0, p1 = x
+        return T[name][p0:p1, c0:c1] if s == 1 else T[name][p0:p1, c0:c1:s]
+
+    def flat(xs):
+        o = []
+        for x in xs:
+            if isinstance(x, tuple):
+                o += [x[1], x[2]] if x[0] == "*" else [x]
+        return o
+
+    def meet(a, b):
+        if a[2] <= b[1] or b[2] <= a[1] or a[5] <= b[4] or b[5] <= a[4]:
+            return False
+        return not (a[3] > 1 and a[3] == b[3] and (a[1] - b[1]) % a[3] != 0)
+
+    def wait(q, sem, val):
+        if known[q].get(sem, 0) < val:
+            queues[q].wait_ge(T.sem[sem], val)
+            known[q][sem] = val
+
+    def order(q, outs, ins, skip=None):
+        need = {}
+        for regs, wr in ((ins, False), (outs, True)):
+            for x in regs:
+                for (y, yw, sem), val in hist.get(x[0], {}).items():
+                    if (wr or yw) and sem != skip and meet(x, y):
+                        need[sem] = max(need.get(sem, 0), val)
+        for sem, val in need.items():
+            wait(q, sem, val)
+
+    def note(outs, ins, sem, val):
+        for regs, wr in ((ins, False), (outs, True)):
+            for x in regs:
+                hist.setdefault(x[0], {})[(x, wr, sem)] = val
+
+    def emit(q, call, outs, ins, skip=None):
+        outs, ins = flat(outs), flat(ins)
+        order(q, outs, ins, skip)
+        sem = own_sem[q]
+        call().then_inc(T.sem[sem], 1)
+        count[sem] += 1
+        note(outs, ins, sem, count[sem])
+
+    def cp(out, in_, q="v"):
+        if q == "v":
+            emit("v", lambda: g.vector.tensor_copy(ap(out), ap(in_)), [out], [in_])
+        else:
+            emit("a", lambda: g.scalar.activation(ap(out), ap(in_), ACT.Copy), [out], [in_])
+
+    def tt(out, a, b, op):
+        emit("v", lambda: g.vector.tensor_tensor(ap(out), ap(a), ap(b), op), [out], [a, b])
+
+    def ts(out, a, s1, op0, s2=None, op1=None):
+        if op1 is None:
+            emit("v", lambda: g.vector.tensor_scalar(ap(out), ap(a), ap(s1), None, op0), [out], [a, s1])
+        else:
+            emit("v", lambda: g.vector.tensor_scalar(ap(out), ap(a), ap(s1), ap(s2), op0, op1), [out], [a, s1, s2])
+
+    def red(out, a, op):
+        emit("v", lambda: g.vector.tensor_reduce(ap(out), ap(a), AxisListType.X, op), [out], [a])
+
+    def scan(out, d0, d1, op0, op1):
+        emit("v", lambda: g.vector.tensor_tensor_scan(ap(out), ap(d0), ap(d1), 0.0, op0, op1), [out], [d0, d1])
+
+    def tr(out, a):
+        emit("v", lambda: g.vector.transpose(ap(out), ap(a)), [out], [a])
+
+    def fill(out, c):
+        emit("v", lambda: g.vector.memset(ap(out), c), [out], [])
+
+    def sign(out, a, bias, accum):
+        emit("a", lambda: g.scalar.activation(ap(out), ap(a), ACT.Sign, bias=ap(bias), accum_out=ap(accum)), [out, accum], [a, bias])
+
+    def iota(out, pattern, base, mult):
+        if SCRATCH[out[0]][2] == I32:
+            emit("g", lambda: g.iota(ap(out), pattern, base, mult), [out], [])
+        else:
+            emit("g", lambda: g.iota(ap(out), pattern, base, mult, allow_small_or_imprecise_dtypes=True), [out], [])
+
+    def quant(c, s, a):
+        emit("v", lambda: g.vector.quantize_mx(ap(c), ap(s), ap(a)), [c, s], [a])
+
+    def mm(out, lc, ls_, rc, rs, start, stop):
+        emit("t", lambda: g.tensor.matmul_mx(ap(out), ap(lc), ap(ls_), ap(rc), ap(rs), start, stop), [out], [lc, ls_, rc, rs],
+             skip=None if start else "kt")
+
+    def pick(oc_, op_, wc, wp, off):
+        emit("v", lambda: g.vector.tensor_copy(ap(oc_).bitcast(dt.uint32), ap(wc).bitcast(dt.uint32).indirect(ap(off))), [oc_], [wc, off])
+        cp(op_, IND(wp, off), "a")
+
+    def dma(q, out, in_, sem, outs=(), ins=(), total=None):
+        order(q, list(outs), list(ins))
+        queues[q].dma_start(out, in_).then_inc(T.sem[sem], 16)
+        count[sem] += 16
+        note(list(outs), [], sem, total or count[sem])
+
+    def bits(m):
+        return bin(m).count("1")
+
+    def dst(c):
+        rid, pid, _ = topo.addr(c)
+        return DstId(rid=rid, pnc=pid)
+
+    def split(src):
+        i0 = cores.index(src)
+        others = [cores[(i0 + k) % N] for k in range(1, N)]
+        near = [c for c in others if topo.chip(c) == topo.chip(src)]
+        far = [c for c in others if topo.chip(c) != topo.chip(src)]
+        mf_ = topo.mask(src, far[0])
+        for c in far:
+            mf_ &= topo.mask(src, c)
+        mn = topo.mask(src, near[0]) & ~mf_
+        return near, far, mn, mf_
+
+    def allgather(src, buf, w, sem):
+        near, far, mn, mf_ = split(core)
+        land = ap(V(buf, w * rank, w * rank + w))
+        order("g", [], [src])
+        g.remote_dma_fused([RemoteDMATransfer(dst_ids=[dst(c) for c in cs_], dma_engine_mask=m, remote_sem=T.sem[sem],
+                                              srcs=[ap(src)], dsts=[land for _ in cs_]) for cs_, m in ((far, mf_), (near, mn))],
+                           local_sem=T.sem.ls)
+        count["ls"] += bits(mf_) + bits(mn)
+        for c in cores:
+            if c != core:
+                n2, f2, mn2, mf2 = split(c)
+                count[sem] += bits(mn2) if core in n2 else bits(mf2)
+        note([V(buf, 0, w * N)], [], sem, count[sem])
+
+    def swap(peer, cb, pb, sem):
+        rid, pid, _ = topo.addr(peer)
+        m = topo.mask(core, peer)
+        order("g", [], [V(cb, 0, K)])
+        g.remote_dma(ap(V(cb, K, 2 * K)).bitcast(dt.uint8), ap(V(cb, 0, K)).bitcast(dt.uint8), T.sem[sem], T.sem.ls, pid, rid, m)
+        order("g", [], [V(pb, 0, K)])
+        g.remote_dma(ap(V(pb, K, 2 * K)), ap(V(pb, 0, K)), T.sem[sem], T.sem.ls, pid, rid, m)
+        count["ls"] += 2 * bits(m)
+        count[sem] += 2 * bits(topo.mask(peer, core))
+        note([V(cb, K, 2 * K), V(pb, K, 2 * K)], [], sem, count[sem])
+
+    me = topo.chip(core)
+    peer_a = [c for c in cores if c != core and topo.chip(c) == me][0]
+    peer_b = [c for c in cores if topo.mates(topo.chip(c), me) and topo.die(c) == topo.die(core)][0]
+    peer_c = [c for c in cores if topo.same_plane(topo.chip(c), me) and topo.die(c) == topo.die(core)][0]
+    set_a = [cores.index(peer_a)]
+    set_b = [k for k in range(N) if topo.chip(cores[k]) == topo.chip(peer_b)]
+    set_c = [k for k in range(N) if topo.chip(cores[k]) not in (me, topo.chip(peer_b))]
+    for s_ in (set_a, set_b, set_c):
+        assert s_ == list(range(s_[0], s_[0] + len(s_)))
+
+    def shift_one(buf, w):
+        for a in range(4):
+            b = (a + 1) % 4
+            cp(V(buf, w, 2 * w, 1, 32 * b, 32 * b + 32), V(buf, 0, w, 1, 32 * a, 32 * a + 32), "a" if a % 2 else "v")
+
+    def shift_two(buf, w):
+        cp(V(buf, 2 * w, 4 * w, 1, 64, 128), V(buf, 0, 2 * w, 1, 0, 64), "v")
+        cp(V(buf, 2 * w, 4 * w, 1, 0, 64), V(buf, 0, 2 * w, 1, 64, 128), "a")
+
+    def shift_all(buf, w):
+        shift_one(buf, w)
+        shift_two(buf, w)
+
+    def cross(buf):
+        tr(V("xx", 16, 80), V(buf, 0, 64))
+        tr(V(buf, 64, 160), V("xx"))
+
+    dma("a", T.nbs[0:16, :], T.nb[:], "dn", [V("nbs", p1=16)], total=32)
+    dma("a", T.nbs[16:32, :], T.nb[:], "dn", [V("nbs", p0=16, p1=32)], total=32)
+    dma("s", T.xs[:], T.x[:], "dx", [V("xs")])
+    dma("s", T.us[:], T.u[:], "du", [V("us")])
+    dma("s", T.ws[:], T.w[:], "dw", [V("ws")])
+
+    CI = {n: V("ci", k, k + 1) for k, n in enumerate(
+        ["p", "i", "g", "hs", "as", "i0", "i1", "i12", "i3", "i123", "q", "ne", "hoff", "nh", "d", "t0", "t1", "t2", "t3", "t4", "t5", "t6"])}
+    CF = {n: V("cf", k, k + 1) for k, n in enumerate(
+        ["p", "i", "g", "hs", "as", "q", "m128i", "noff", "top", "o4096", "sW", "sO", "p4", "ba", "bd", "g256", "k0"])}
+    LNB, LW, LO, LP2, LO2, LR2, LA, LCH = V("lst", 0, 1), V("lst", 2, 10), V("lst", 10, 13), V("lst", 14, 15), V("lst", 16, 17), V("lst", 18, 19), V("lst", 20, 21), V("lst", 22, 23)
+    LO1 = V("lst", 10, 11)
+    LI, LF, LB2 = V("lst", 24, 27), V("lst", 28, 44), V("lst", 44, 76)
+
+    def LB(a, b):
+        return V("lst", 80 + a, 80 + b)
+
+    AND, SHR = OP.bitwise_and, OP.logical_shift_right
+    iota(CI["p"], [[0, 1]], 0, 1)
+    iota(V("jr"), [[1, 48]], 0, 0)
+    iota(V("iot16"), [[0, 16], [1, 16]], 0, 0)
+    iota(V("thx"), [[2, 16]], 0, 64)
+    iota(V("tri"), [[0, 2], [1, 32]], 0, 0)
+    P = CI["p"]
+    ts(CI["i"], P, 15, AND)
+    ts(CI["g"], P, 4, SHR)
+    ts(CI["t0"], CI["i"], 5.0, OP.min, 8.0, OP.mult)
+    tt(CI["t1"], CI["t0"], CI["g"], OP.add)
+    cp(LNB, CI["t1"])
+    cp(V("nbs", p0=32, p1=64), V("nbs", p1=32))
+    cp(V("nbs", p0=64), V("nbs", p1=64))
+    cp(V("nbo"), IND(V("nbs"), LNB))
+    allgather(V("nbo", 0, 6), "nbl", 6, "an")
+    quant(V("ct0", 0, M), V("pt0", 0, M), V("xs"))
+    quant(V("qu"), V("su"), V("us"))
+
+    def heights(t):
+        for u in range(2):
+            mm(V("psh", 512 * u, 512 * u + 128), V("ct%d" % t, 128 * u, 128 * u + 128), V("pt%d" % t, 128 * u, 128 * u + 128), V("qu"), V("su"), True, True)
+        cp(V("hs", 2 * t, 2 * t + 2), V("psh", t, 1024, 512))
+        allgather(V("hs", 2 * t, 2 * t + 2), "qh%d" % t, 2, "ah%d" % t)
+
+    heights(0)
+    iota(V("sv"), [[1, 16], [16, 16]], 1, 0)
+    iota(V("io512"), [[1, 512]], 0, 0)
+
+    ts(CI["hs"], P, 4, SHR, 1, AND)
+    ts(CI["as"], P, 5, SHR)
+    ts(CI["i0"], P, 1, AND)
+    ts(CI["i1"], P, 1, SHR, 1, AND)
+    ts(CI["i12"], P, 1, SHR, 3, AND)
+    ts(CI["i3"], P, 3, SHR, 1, AND)
+    ts(CI["i123"], P, 1, SHR, 7, AND)
+    ts(CI["q"], P, 31, AND)
+    fill(V("xx"), 0.0)
+    fill(V("qn", 48, 64), 0.0)
+    cp(V("cf", 0, 5), V("ci", 0, 5))
+    cp(CF["q"], CI["q"])
+    tt(CI["ne"], CI["i0"], CI["hs"], OP.not_equal)
+    ts(CI["hoff"], CI["hs"], -32.0, OP.mult, 96.0, OP.add)
+    tt(CI["t2"], CI["as"], CI["i12"], OP.subtract)
+    ts(CI["t3"], CI["i123"], 2.0, OP.mult, CF["hs"], OP.add)
+    tt(CI["nh"], CI["ne"], CI["hoff"], OP.mult)
+    ts(CI["d"], CI["t2"], 3, AND)
+    cp(LB(0, 48), V("jr"))
+    tt(CF["sO"], CI["t3"], CI["nh"], OP.add)
+    tt(CI["t4"], CI["i3"], CI["nh"], OP.add)
+    ts(CI["t5"], CI["d"], 16.0, OP.mult)
+    ts(LO, V("jr", 0, 3), 16.0, OP.mult, CF["sO"], OP.add)
+    tt(CF["sW"], CI["t4"], CI["t5"], OP.add)
+    ts(LI, V("jr", 0, 3), 0.0, OP.mult, CF["i"], OP.add)
+    ts(LW, V("jr", 0, 8), 2.0, OP.mult, CF["sW"], OP.add)
+    ts(CF["m128i"], CF["i"], -128.0, OP.mult)
+    ts(CF["noff"], CF["i"], 128.0, OP.mult, -1920.0, OP.add)
+    ts(CF["top"], CF["i"], -128.0, OP.mult, 2176.0, OP.add)
+    ts(CF["k0"], CF["i"], -1.0 / 32, OP.mult, 256.0, OP.add)
+    for k in range(3):
+        ts(V("rst", 256 * k, 256 * k + 256), V("iot16"), 0.0, OP.not_equal)
+    ts(V("iot32"), V("iot16", 0, 64), 1.0 / 32, OP.mult)
+    fill(V("d1"), 2048.0)
+    ts(V("tmpi", 0, 16), V("jr", 0, 16), -8.0, OP.mult, CF["g"], OP.subtract)
+    ts(V("kk", 48, 64), V("tmpi", 0, 16), CF["k0"], OP.add)
+
+    def late_constants():
+        ts(CI["t0"], CI["i1"], float(2 * rank), OP.add)
+        ts(LO2, CI["i1"], 2.0, OP.mult, CF["hs"], OP.add)
+        ts(CI["t2"], CI["d"], 4.0, OP.mult)
+        ts(CI["t3"], CI["i3"], 2.0, OP.mult)
+        ts(CI["t4"], CI["i123"], 2.0, OP.mult)
+        ts(CI["t5"], CI["hs"], -1.0, OP.mult, 3.0, OP.add)
+        tt(CI["t1"], CI["t0"], CI["nh"], OP.add)
+        tt(CI["t6"], CI["t2"], CI["t3"], OP.add)
+        tt(CI["t4"], CI["t4"], CI["ne"], OP.add)
+        tt(CI["t5"], CI["t5"], CI["ne"], OP.mult)
+        cp(LP2, CI["t1"])
+        tt(CI["t6"], CI["t6"], CI["ne"], OP.add)
+        cp(LA, CI["t4"])
+        tt(CI["t5"], CI["t5"], CI["i1"], OP.add)
+        cp(LR2, CI["t6"])
+        ts(V("tmpi", 16, 32), V("jr", 0, 16), 1, SHR, 3, AND)
+        cp(LCH, CI["t5"])
+        ts(V("tmpi", 32, 48), V("jr", 0, 16), 3, SHR)
+        ts(V("tmpi", 48, 64), V("tmpi", 16, 32), -1.0, OP.mult, CF["as"], OP.add)
+        ts(V("tmpi", 32, 48), V("tmpi", 32, 48), 2.0, OP.mult, CF["hs"], OP.add)
+        ts(V("tmpi", 48, 64), V("tmpi", 48, 64), 3, AND)
+        ts(V("tmpi", 64, 96), V("jr", 0, 32), 1, SHR)
+        ts(V("tmpi", 48, 64), V("tmpi", 48, 64), 4.0, OP.mult)
+        cp(LB2, V("tmpi", 64, 96))
+        tt(V("tmpi", 48, 64), V("tmpi", 48, 64), V("tmpi", 32, 48), OP.add)
+        ts(V("th"), V("thx"), -1.0, OP.add, -1.0 / 64, OP.mult)
+        cp(LF, V("tmpi", 48, 64))
+        fill(V("ob"), 1.0)
+
+    def later_constants():
+        ts(CF["o4096"], CF["i"], -4096.0, OP.mult, 61440.0, OP.add)
+        ts(CF["ba"], CF["q"], -2.0, OP.mult, -3.0, OP.add)
+        ts(CF["bd"], CF["q"], 2.0, OP.mult, 4.0, OP.add)
+        ts(CF["g256"], CF["g"], 256.0, OP.mult)
+        ts(CF["p4"], P, 4.0, OP.mult)
+        ts(V("tri"), V("tri"), CF["q"], OP.is_lt)
+        fill(V("c128"), 128.0)
+        fill(V("ones"), 1.0)
+        fill(V("cc", 8, 9), float(4 * CA))
+        fill(V("pf"), 0.0)
+        fill(V("zz"), 0.0)
+        ts(V("sv"), V("sv"), CF["g256"], OP.add)
+        ts(V("tmpi", 96, 112), V("jr", 0, 16), 1, AND)
+        ts(V("dum"), V("jr", 0, 16), 16.0, OP.mult, CF["i"], OP.add)
+        tt(V("tmpi", 112, 128), V("jr", 0, 16), V("tmpi", 96, 112), OP.subtract)
+        ts(V("tmpi", 96, 112), V("tmpi", 96, 112), CF["hs"], OP.not_equal)
+        ts(V("dum"), V("dum"), float(DUMMY), OP.add)
+        tt(V("tmpi", 96, 112), V("tmpi", 96, 112), V("tmpi", 112, 128), OP.add)
+        ts(V("mym"), V("tmpi", 96, 112), 16.0, OP.mult, CF["i"], OP.add)
+
+    def unpackers():
+        for b in range(4):
+            ts(V("et", 512 * b, 512 * b + 512), V("io512"), CF["p4"], OP.subtract, float(b), OP.is_equal)
+        quant(V("qe"), V("se"), V("et"))
+
+    late_constants()
+
+    cp(V("nbl", 6 * rank, 6 * rank + 6), V("nbo", 0, 6))
+    for j in range(J):
+        for u in range(2):
+            cp(V("nbi", 16 * j + u, 16 * j + 16, 2), V("nbl", 2 * j + u, 48, 6))
+    ts(V("nhi"), V("nbi"), 4, SHR)
+    ts(V("nlo"), V("nbi"), 15, AND)
+    cp(V("qn", 0, 48), V("nhi"))
+    ts(V("sm", 0, 48), V("nlo"), -1.0 / 32, OP.mult, 256.0, OP.add)
+    cross("qn")
+    tt(V("kk", 0, 48), V("sm", 0, 48), V("nhi"), OP.subtract)
+    cp(V("on"), IND(V("qn"), LO))
+    tt(V("mt", 0, 256), IND(V("nlo"), LB(0, 16)), V("iot16"), OP.is_equal)
+    tt(V("mt", 256, 512), IND(V("nlo"), LB(16, 32)), V("iot16"), OP.is_equal)
+    tt(V("mt", 512, 768), IND(V("nlo"), LB(32, 48)), V("iot16"), OP.is_equal)
+    tr(V("mf"), V("mt"))
+
+    def in_range(out, tmp, x, ranks, base):
+        ts(out, x, float(M * ranks[0] + base), OP.is_ge, float(K), OP.mult)
+        ts(tmp, x, float(M * (ranks[-1] + 1) + base), OP.is_lt)
+        tt(out, out, tmp, OP.mult)
+
+    for t in range(R):
+        ct, pt, qh, hl = "ct%d" % t, "pt%d" % t, "qh%d" % t, "hl%d" % t
+        cp(V(qh, 2 * rank, 2 * rank + 2), V("hs", 2 * t, 2 * t + 2))
+        shift_all(qh, 16)
+        cross(qh)
+        cp(V("wt"), IND(V(qh), LW))
+        tt(V("gm"), IND(V("wt"), V("on")), V("mf"), OP.mult)
+        tr(V("tt"), V("gm"))
+        scan(V("ss"), V("rst"), V("tt"), OP.mult, OP.add)
+        tt(V("sm", 0, 16), V("ss", 15, 256, 16), V("ss", 271, 512, 16), OP.max)
+        tt(V("sm", 16, 32), V("ss", 527, 768, 16), V(qh, 0, 16), OP.max)
+        tt(V("sm", 32, 48), V("sm", 0, 16), V("sm", 16, 32), OP.max)
+        tt(V("sm", 64, 112), IND(V("sm", 32, 48), LI), V("ss", 15, 768, 16), OP.is_equal)
+        tt(V("sm", 112, 128), V("sm", 32, 48), V(qh, 0, 16), OP.is_equal)
+        tt(V("sm", 64, 128), V("sm", 64, 128), V("kk"), OP.mult)
+        tt(V("sm", 128, 160), V("sm", 64, 96), V("sm", 96, 128), OP.max)
+        tt(V("sm", 0, 16), V("sm", 128, 144), V("sm", 144, 160), OP.max)
+        ts(V("q", 0, 16), V("sm", 0, 16), -1.0, OP.mult, CF["top"], OP.add)
+        for step in range(10):
+            shift_one("q", 16)
+            if step < 9:
+                cp(V("hi"), V("q", 0, 16))
+            shift_two("q", 16)
+            if step < 9:
+                tt(V("lof"), V("q", 0, 16), V("hi"), OP.subtract)
+            tr(V("xx", 16, 80), V("q", 0, 64))
+            if step < 9:
+                ts(V("d1", 0, 256, 16), V("lof"), -65536.0, OP.mult)
+            tr(V("q", 64, 160), V("xx"))
+            cp(V("wt"), IND(V("q"), LW), "a")
+            if step == 9:
+                break
+            ts(V("oo"), IND(V("q"), LO1), CF["noff"], OP.add)
+            scan(V("mk"), V("rst", 0, 256), V("d1"), OP.mult, OP.add)
+            ts(V("cor"), V("lof"), 4096.0, OP.mult, CF["m128i"], OP.add)
+            for h in range(2):
+                cp(V("gm", 128 * h, 128 * h + 128), IND(V("wt"), V("oo", 8 * h, 8 * h + 8)), "a")
+            tr(V("tt", 0, 128), V("gm", 0, 128))
+            scan(V("ss", 0, 128), V("mk", 0, 128), V("tt", 0, 128), OP.min, OP.max)
+            tr(V("tt", 128, 256), V("gm", 128, 256))
+            scan(V("ss", 128, 256), V("mk", 128, 256), V("tt", 128, 256), OP.min, OP.max)
+            tt(V("q", 0, 16), V("ss", 15, 256, 16), V("cor"), OP.add)
+        ts(V("p2"), IND(V("q"), LP2), CF["noff"], OP.add)
+        for step in range(3):
+            cp(V("oo"), IND(V("p2"), LO2))
+            cp(V("hi", 0, 4), V("p2", 0, 4))
+            cp(V("gm", 0, 64), IND(V("wt"), V("oo", 0, 4)), "a")
+            tt(V("lof", 0, 4), V("p2", 0, 4), V("hi", 0, 4), OP.subtract)
+            tt(V("mk", 0, 64), IND(V("lof"), LB(0, 4)), V("iot32"), OP.not_equal)
+            tr(V("tt", 0, 64), V("gm", 0, 64))
+            ts(V("cor", 0, 4), V("lof", 0, 4), 4096.0, OP.mult, -1920.0, OP.add)
+            scan(V("ss", 0, 64), V("mk", 0, 64), V("tt", 0, 64), OP.mult, OP.max)
+            tt(V("p2" if step < 2 else "q2", 0, 4), V("ss", 15, 64, 16), V("cor", 0, 4), OP.add)
+        shift_all("q2", 4)
+        cp(V("rb", 0, 128), IND(V("q2"), V("lst", 28, 36)), "v")
+        cp(V("rb", 128, 256), IND(V("q2"), V("lst", 36, 44)), "a")
+        tr(V("rf"), V("rb"))
+        ts(V("zb"), V("rf"), CF["p"], OP.subtract)
+        for k in range(NA + 1):
+            sign(V("ja", 256 * k, 256 * k + 256), V("rf"), V("th", k, k + 1), V("acc", k, k + 1))
+        for k in range(ND):
+            ts(V("jd", 256 * k, 256 * k + 256), V("zb"), (NA + k) / 32.0, OP.is_equal, 2.0, OP.mult)
+        for k in range(ND):
+            scan(V("js", 256 * k, 256 * k + 256), V("ob"), V("jd", 256 * k, 256 * k + 256), OP.mult, OP.add)
+        cp(V(hl, 16 * rank + NA, 16 * rank + 16), V("js", 255, 256 * ND, 256))
+        tt(V(hl, 16 * rank, 16 * rank + NA), V("acc", 0, NA), V("acc", 1, NA + 1), OP.subtract)
+        allgather(V(hl, 16 * rank, 16 * rank + 16), hl, 16, "az%d" % t)
+        if t == 0:
+            later_constants()
+        fill(V("lw", 0, 96), 0.0)
+        cp(V("r2"), IND(V("q2"), LR2))
+        cp(V("rti", p1=1), V("rf", p1=1))
+        cp(V("r2i", 0, 16), V("r2"))
+        ts(V("rta", p1=1), V("rf", p1=1), 32.0, OP.mult)
+        tt(V("r2f", 0, 16), V("r2"), V("r2i", 0, 16), OP.subtract)
+        ts(V("r2i", 16, 32), V("r2i", 0, 16), 15, AND)
+        ts(V("r2i", 32, 48), V("r2i", 0, 16), 4, SHR)
+        ts(V("rtb", p1=1), V("rti", p1=1), 16.0, OP.mult)
+        ts(V("r2f", 16, 32), V("r2f", 0, 16), 256.0, OP.mult)
+        ts(V("r2f", 32, 48), V("r2"), 32.0, OP.mult)
+        ts(V("r2f", 48, 64), V("r2i", 0, 16), 16.0, OP.mult)
+        tt(V("rto", M * t, M * t + M, p1=1), V("rta", p1=1), V("rtb", p1=1), OP.subtract)
+        tt(V("r2f", 16, 32), V("r2f", 16, 32), V("r2i", 32, 48), OP.add)
+        tt(V("r2f", 32, 48), V("r2f", 32, 48), V("r2f", 48, 64), OP.subtract)
+        dma("s", T.rt[0:1, M * t:M * t + M], ap(V("rto", M * t, M * t + M, p1=1)), "dout", ins=[V("rto", M * t, M * t + M, p1=1)])
+        cp(V("o3"), V("r2f", 16, 32))
+        tt(V("mk3"), IND(V("r2i", 16, 32), LB(0, 16)), V("iot16"), OP.not_equal)
+        ts(V("r2f", 64, 80), V("r2i", 16, 32), 4096.0, OP.mult, -61440.0, OP.add)
+        in_range(V("r2f", 80, 96), V("r2f", 96, 112), V("r2f", 32, 48), set_c, 0)
+        ts(V("r2f", 48, 64), V("r2f", 32, 48), float(-M * rank), OP.add)
+        tt(V("r2f", 112, 128), V("r2f", 48, 64), V("mym"), OP.not_equal)
+        tt(V("s1"), V(hl, 0, 64), V(hl, 64, 128), OP.add)
+        tt(V("s1", 0, 32), V("s1", 0, 32), V("s1", 32, 64), OP.add)
+        tt(V("sz"), V("s1", 0, 16), V("s1", 16, 32), OP.add)
+        cp(V("yb", 0, 256), IND(V("sz"), V("lst", 44, 60)), "a")
+        cp(V("yb", 256, 512), IND(V("sz"), V("lst", 60, 76)), "v")
+        tr(V("yt"), V("yb"))
+        sign(V("jy", 0, CA), V("yt", 0, CA), CF["ba"], V("cc", 0, 1))
+        ts(V("jy", CA, 512), V("yt", CA, 512), CF["bd"], OP.is_ge, 2.0, OP.mult)
+        red(V("cc", 1, 2), V("jy", CA, 512), OP.add)
+        shift_all("cc", 2)
+        red(V("cs", 0, 1), V("cc", 0, 9), OP.add)
+        ts(V("bb", 0, 32), V("c128"), V("cs", 0, 1), OP.is_le, 2.0, OP.mult)
+        ts(V("bb", 32, 64), V("c128"), V("cs", 0, 1), OP.is_gt, V("cs", 0, 1), OP.mult)
+        tr(V("bt"), V("bb"))
+        red(V("cs", 1, 2), V("bt", 0, 32), OP.add)
+        red(V("cs", 2, 3), V("bt", 32, 64), OP.max)
+        ts(V("fl", 0, 16), V("sz"), -2.0, OP.add, V("cs", 1, 2), OP.is_gt)
+        ts(V("fl", 16, 32), V("sz"), -2.0, OP.add, V("cs", 1, 2), OP.is_equal)
+        ts(V("fl", 32, 48), V("sz"), -2.0, OP.add, V("cs", 1, 2), OP.is_lt)
+        scan(V("sc"), V("rst", 0, 32), V("fl", 0, 32), OP.mult, OP.add)
+        ts(V("pf", 9, 10), V("cs", 2, 3), 0.5, OP.mult)
+        ts(V("bb", 0, 32), V("ones"), V("sc", 15, 16), OP.mult)
+        ts(V("bb", 32, 64), V("ones"), V("sc", 31, 32), OP.mult)
+        tt(V("bs", 32, 48), V("fl", 32, 48), V("dum"), OP.mult)
+        tr(V("bt"), V("bb"))
+        tt(V("bs", 0, 32), V("sc"), V("fl", 0, 32), OP.mult)
+        red(V("rr", 0, 1), V("bt", 0, 32), OP.add)
+        red(V("rr", 1, 2), V("bt", 32, 64), OP.add)
+        tt(V("tm"), V("bt"), V("tri"), OP.mult)
+        cp(V("pf", 2, 4, 1, 32, 64), V("rr", 0, 2, 1, 0, 32), "a")
+        cp(V("pf", 2, 4, 1, 64, 96), V("rr", 0, 2, 1, 32, 64), "a")
+        cp(V("pf", 2, 4, 1, 96, 128), V("rr", 0, 2, 1, 64, 96), "a")
+        cp(V("pf", 4, 6, 1, 64, 128), V("rr", 0, 2, 1, 0, 64), "v")
+        cp(V("pf", 6, 8, 1, 96, 128), V("rr", 0, 2, 1, 0, 32), "v")
+        red(V("pf", 0, 1), V("tm", 0, 32), OP.add)
+        red(V("pf", 1, 2), V("tm", 32, 64), OP.add)
+        tt(V("bs", 48, 64), V("bs", 0, 16), V("bs", 16, 32), OP.add)
+        ts(V("bs", 32, 48), V("bs", 32, 48), 15.0, OP.add)
+        red(V("rr", 2, 3), V("pf", 0, 10, 2), OP.add)
+        red(V("rr", 3, 4), V("pf", 1, 10, 2), OP.add)
+        tt(V("bs", 48, 64), V("bs", 48, 64), V("bs", 32, 48), OP.add)
+        ts(V("bs", 64, 80), V("fl", 0, 16), V("rr", 2, 3), OP.mult)
+        ts(V("bs", 80, 96), V("fl", 16, 32), V("rr", 3, 4), OP.mult)
+        tt(V("bs", 64, 80), V("bs", 64, 80), V("bs", 48, 64), OP.add)
+        tt(V("vv"), V("bs", 64, 80), V("bs", 80, 96), OP.add)
+        cp(V("vo"), V("vv"))
+        emit("v", lambda: g.vector.tensor_copy(ap(IND(V("lw"), V("vo"))), ap(V("sv"))), [V("lw")], [V("sv"), V("vo")])
+        tr(V("lt", 0, 64), V("lw", 16, 80))
+        tr(V("lt", 64, 160), V("lw", 0, 96))
+        tt(V("zz", 0, 5), V("lt", 0, 160, 32), V("lt", 16, 160, 32), OP.add)
+        shift_all("zz", 8)
+        tt(V("zs"), V("zz", 0, 16), V("zz", 16, 32), OP.add)
+        tt(V("zs", 0, 8), V("zs", 0, 8), V("zs", 8, 16), OP.add)
+        ts(V("pl", 0, 16), IND(V("zs", 0, 8), LCH), float(-1 - M * rank), OP.add, float(M - 1), OP.min)
+        ca, pa, cb, pb, cc_, pc_ = ["%s%s%d" % (x, s_, t) for s_ in "abc" for x in "cp"]
+        pick(V(ca, 0, K), V(pa, 0, K), V(ct, 0, M), V(pt, 0, M), V("pl", 0, 4))
+        swap(peer_a, ca, pa, "aa%d" % t)
+        cp(V("ch"), IND(V("zs", 0, 8), LCH))
+        ts(V("q", 0, 16), V("vv"), CF["o4096"], OP.add)
+        in_range(V("cht", 0, 4), V("cht", 4, 8), V("ch", 0, 4), set_a, 1)
+        in_range(V("cht", 8, 12), V("cht", 12, 16), V("ch", 0, 4), set_b, 1)
+        tt(V("cht", 0, 4), V("cht", 0, 4), V("dum", 0, 4), OP.add)
+        tt(V("cht", 8, 12), V("cht", 8, 12), V("dum", 0, 4), OP.add)
+        ts(V("pl", 16, 20), V("cht", 0, 4), float(-DUMMY), OP.add)
+        ts(V("pl", 20, 24), V("cht", 8, 12), float(-DUMMY), OP.add)
+        shift_all("q", 16)
+        cross("q")
+        cp(V("wt"), IND(V("q"), LW), "a")
+        pick(V(cb, 0, K), V(pb, 0, K), V(ca), V(pa), V("pl", 16, 20))
+        swap(peer_b, cb, pb, "ab%d" % t)
+        cp(V("gm", 0, 256), IND(V("wt"), V("o3")), "a")
+        tr(V("tt", 0, 256), V("gm", 0, 256))
+        scan(V("ss", 0, 256), V("mk3"), V("tt", 0, 256), OP.mult, OP.max)
+        tt(V("cht", 16, 32), V("ss", 15, 256, 16), V("r2f", 64, 80), OP.add)
+        ts(V("cht", 32, 48), V("cht", 16, 32), -16.0, OP.add, float(K - 1), OP.min)
+        ts(V("cht", 48, 64), V("cht", 16, 32), 79.5, OP.is_lt, float(M), OP.mult)
+        tt(V("cht", 32, 48), V("cht", 32, 48), V("r2f", 80, 96), OP.add)
+        tt(V("cht", 48, 64), V("cht", 48, 64), V("r2f", 112, 128), OP.mult)
+        cp(V("pl", 32, 48), IND(V("cht", 32, 48), LA))
+        tt(V("cht", 48, 64), V("cht", 48, 64), V("mym"), OP.add)
+        cp(V("pl", 48, 64), IND(V("cht", 48, 64), LA))
+        pick(V(cc_, 0, K), V(pc_, 0, K), V(cb), V(pb), V("pl", 20, 24))
+        swap(peer_c, cc_, pc_, "ac%d" % t)
+        if t == 0:
+            unpackers()
+        if t == 1:
+            quant(V("qw"), V("sw"), V("ws"))
+        for b in range(4):
+            mm(V("psd", 512 * b, 512 * b + M), V("qe", 128 * b, 128 * b + 128), V("se", 128 * b, 128 * b + 128), V(ct, 0, M), V(pt, 0, M), True, False)
+        cr, pr = "cr%d" % t, "pr%d" % t
+        pick(V(cr), V(pr), V(cc_), V(pc_), V("pl", 32, 48))
+        for b in range(4):
+            mm(V("psd", 512 * b, 512 * b + M), V("qe", 128 * b, 128 * b + 128), V("se", 128 * b, 128 * b + 128), V(cr), V(pr), False, True)
+        for b in range(4):
+            o, i_ = V("ht", b, 1024, 4), V("psd", 512 * b, 512 * b + M)
+            if b % 2:
+                ts(o, i_, 0.5, OP.mult)
+            else:
+                emit("a", lambda: g.scalar.activation(ap(o), ap(i_), ACT.Copy, scale=0.5), [o], [i_])
+        quant(V(ct, M, 2 * M), V(pt, M, 2 * M), V("ht"))
+        pick(V("ct%d" % (t + 1), 0, M), V("pt%d" % (t + 1), 0, M), V(ct), V(pt), V("pl", 48, 64))
+        if t + 1 < R:
+            heights(t + 1)
+
+    ct, pt = "ct%d" % R, "pt%d" % R
+    mm(V("psy", 0, M), V("qw"), V("sw"), V(ct, 0, M), V(pt, 0, M), True, True)
+    dma("s", T.oc[:], ap(V(ct, 0, M)).bitcast(dt.uint8), "dout", ins=[V(ct, 0, M)])
+    for k in range(4):
+        dma("a", T.osc[4 * k:4 * k + 4, :], T[pt][32 * k:32 * k + 4, 0:M], "dout", ins=[V(pt, 0, M)])
+    cp(V("yo"), V("psy", 0, M))
+    dma("s", T.y[:], T.yo[:], "dout", ins=[V("yo")])
+    for s_ in SEMAPHORES:
+        if count[s_]:
+            wait("g", s_, count[s_])

@@ -3,9 +3,10 @@ from concourse.mybir import dt, AluOpType, AxisListType, ActivationFunctionType
 
 N, M, K, J, R = 8, 256, 64, 3, 3
 F32, I32, U16, BF, CODE, PLANE = "float32", "int32", "uint16", "bfloat16", "float8_e4m3fn_x4", "uint8"
-NA = 7
+NA = 8
 ND = 16 - NA
-CA = 320
+CA = 384
+GA = 160
 DUMMY = 2200
 
 SCRATCH = {}
@@ -20,24 +21,24 @@ for _n, _w, _d in [
     ("qu", 128, CODE), ("su", 128, PLANE), ("qw", 128, CODE), ("sw", 128, PLANE),
     ("et", 2048, BF), ("qe", 512, CODE), ("se", 512, PLANE), ("io512", 512, F32),
     ("ci", 32, I32), ("cf", 32, F32), ("jr", 48, I32), ("tmpi", 128, I32), ("lst", 160, U16),
-    ("iot16", 256, F32), ("iot32", 64, F32), ("rst", 768, F32), ("sv", 256, F32), ("tri", 64, F32), ("kk", 64, F32),
+    ("iot16", 256, F32), ("iot32", 64, F32), ("rst", 256, F32), ("rs8", 128, F32), ("sv", 256, F32), ("tri", 64, F32), ("kk", 64, F32),
     ("nbi", 48, I32), ("nhi", 48, I32), ("nlo", 48, I32), ("qn", 160, F32), ("on", 48, U16), ("mt", 768, F32), ("mf", 768, F32),
-    ("hs", 8, F32), ("q", 160, F32), ("xx", 96, F32), ("wt", 128, F32), ("oo", 16, U16), ("d1", 256, F32),
-    ("gm", 768, F32), ("tt", 768, F32), ("ss", 768, F32), ("mk", 256, F32), ("hi", 16, I32), ("lof", 16, F32),
+    ("hs", 12, F32), ("q", 160, F32), ("xx", 96, F32), ("wt", 128, F32), ("oo", 16, U16), ("d1", 256, BF),
+    ("gm", 768, F32), ("tt", 768, F32), ("ss", 768, F32), ("mk", 256, BF), ("hi", 16, I32), ("lof", 16, F32),
     ("sm", 160, F32), ("p2", 16, F32), ("q2", 16, F32), ("rb", 256, F32), ("rf", 256, F32),
     ("ja", 256 * (NA + 1), BF), ("acc", 24, F32),
     ("rti", 256, I32), ("rta", 256, F32), ("rtb", 256, F32), ("rto", 768, F32),
     ("r2", 16, F32), ("r2i", 48, I32), ("r2f", 128, F32), ("o3", 16, U16), ("mk3", 256, F32),
-    ("s1", 64, F32), ("sz", 16, F32), ("yb", 512, BF), ("yt", 512, BF), ("jy", 512, BF), ("cc", 16, F32),
+    ("s1", 128, F32), ("sz", 128, F32), ("yb", 512, BF), ("yt", 512, BF), ("jy", 512, BF), ("cc", 16, F32),
     ("bb", 64, F32), ("bt", 64, F32), ("fl", 48, F32), ("sc", 32, F32), ("tm", 64, F32), ("pf", 16, F32),
-    ("bs", 96, F32), ("vo", 16, U16), ("lw", 2480, F32), ("lt", 160, F32), ("zz", 32, F32), ("zs", 16, F32),
+    ("bs", 64, F32), ("vo", 16, U16), ("lw", 2480, F32), ("lt", 160, F32), ("zz", 40, F32),
     ("cht", 64, F32), ("pl", 80, U16), ("ht", 1024, BF), ("yo", 256, F32),
 ]:
     _sb(_n, _w, _d)
 ALIAS = {}
-for _b, _d, _names in (("kc", F32, [("thx", 16), ("th", 16), ("c128", 32), ("ones", 32), ("mym", 16), ("dum", 16)]),
-                       ("wk", F32, [("cor", 16), ("cs", 8), ("rr", 8), ("vv", 16), ("ch", 16)]),
-                       ("wb", BF, [("zb", 256), ("ob", 256), ("jd", 256 * ND), ("js", 256 * ND)])):
+for _b, _d, _names in (("kc", F32, [("thx", 16), ("th", 16), ("c128", 32), ("ones", 32), ("mym", 16), ("dum", 16), ("rs3", 48)]),
+                       ("wk", F32, [("cor", 16), ("cs", 8), ("rr", 8), ("ch", 16), ("v3", 48), ("v3s", 48), ("ff", 16), ("nf", 4), ("ho", 4), ("zs", 40)]),
+                       ("wb", BF, [("zb", 256), ("ob", 256), ("rsb", 256), ("jd", 256 * ND), ("js", 256 * ND)])):
     _o = 0
     for _n, _w in _names:
         ALIAS[_n] = (_b, _o, _w)
@@ -58,7 +59,7 @@ SCRATCH["psh"] = ("psum", [128, 1024], F32)
 SCRATCH["psd"] = ("psum", [128, 2048], F32)
 SCRATCH["psy"] = ("psum", [128, 512], F32)
 
-SEMAPHORES = ["kv", "ka", "kt", "kg", "ls", "dx", "du", "dw", "dn", "dout", "an"] + \
+SEMAPHORES = ["kv", "ka", "kt", "kg", "ls", "dx", "du", "dw", "dn", "dh", "dout", "an"] + \
     ["%s%d" % (_s, _t) for _s in ("ah", "az", "aa", "ab", "ac") for _t in range(R)]
 
 OP = AluOpType
@@ -181,7 +182,7 @@ def rank_program(g, core, T, topo):
         cp(op_, IND(wp, off), "a")
 
     def dma(q, out, in_, sem, outs=(), ins=(), total=None):
-        order(q, list(outs), list(ins))
+        order(q, [], list(ins))
         queues[q].dma_start(out, in_).then_inc(T.sem[sem], 16)
         count[sem] += 16
         note(list(outs), [], sem, total or count[sem])
@@ -248,9 +249,16 @@ def rank_program(g, core, T, topo):
         cp(V(buf, 2 * w, 4 * w, 1, 64, 128), V(buf, 0, 2 * w, 1, 0, 64), "v")
         cp(V(buf, 2 * w, 4 * w, 1, 0, 64), V(buf, 0, 2 * w, 1, 64, 128), "a")
 
-    def shift_all(buf, w):
-        shift_one(buf, w)
-        shift_two(buf, w)
+    def shift_at_once(dst_, src):
+        cp(dst_(2, 64, 128), src(0, 64), "v")
+        cp(dst_(2, 0, 64), src(64, 128), "a")
+        for m in (1, 3):
+            for a in range(4):
+                b = (a + m) % 4
+                cp(dst_(m, 32 * b, 32 * b + 32), src(32 * a, 32 * a + 32), "a" if a % 2 else "v")
+
+    def shift_now(buf, w):
+        shift_at_once(lambda m, a, b: V(buf, m * w, m * w + w, 1, a, b), lambda a, b: V(buf, 0, w, 1, a, b))
 
     def cross(buf):
         tr(V("xx", 16, 80), V(buf, 0, 64))
@@ -265,10 +273,11 @@ def rank_program(g, core, T, topo):
     CI = {n: V("ci", k, k + 1) for k, n in enumerate(
         ["p", "i", "g", "hs", "as", "i0", "i1", "i12", "i3", "i123", "q", "ne", "hoff", "nh", "d", "t0", "t1", "t2", "t3", "t4", "t5", "t6"])}
     CF = {n: V("cf", k, k + 1) for k, n in enumerate(
-        ["p", "i", "g", "hs", "as", "q", "m128i", "noff", "top", "o4096", "sW", "sO", "p4", "ba", "bd", "g256", "k0"])}
+        ["p", "i", "g", "hs", "as", "q", "m128i", "noff", "top", "o4096", "sW", "sO", "p4", "ba", "bd", "g256", "k0", "sZ"])}
     LNB, LW, LO, LP2, LO2, LR2, LA, LCH = V("lst", 0, 1), V("lst", 2, 10), V("lst", 10, 13), V("lst", 14, 15), V("lst", 16, 17), V("lst", 18, 19), V("lst", 20, 21), V("lst", 22, 23)
     LO1 = V("lst", 10, 11)
     LI, LF, LB2 = V("lst", 24, 27), V("lst", 28, 44), V("lst", 44, 76)
+    LH, LZ = V("lst", 128, 129), V("lst", 130, 138)
 
     def LB(a, b):
         return V("lst", 80 + a, 80 + b)
@@ -292,14 +301,27 @@ def rank_program(g, core, T, topo):
     quant(V("ct0", 0, M), V("pt0", 0, M), V("xs"))
     quant(V("qu"), V("su"), V("us"))
 
-    def heights(t):
+    def products(t, c0):
         for u in range(2):
-            mm(V("psh", 512 * u, 512 * u + 128), V("ct%d" % t, 128 * u, 128 * u + 128), V("pt%d" % t, 128 * u, 128 * u + 128), V("qu"), V("su"), True, True)
-        cp(V("hs", 2 * t, 2 * t + 2), V("psh", t, 1024, 512))
-        allgather(V("hs", 2 * t, 2 * t + 2), "qh%d" % t, 2, "ah%d" % t)
+            mm(V("psh", 512 * u, 512 * u + 128), V("ct%d" % t, c0 + 128 * u, c0 + 128 * u + 128), V("pt%d" % t, c0 + 128 * u, c0 + 128 * u + 128),
+               V("qu"), V("su"), True, True)
+
+    def heights(t):
+        if t == 0:
+            products(0, 0)
+            cp(V("hs", 0, 2), V("psh", 0, 1024, 512))
+        else:
+            products(t - 1, M)
+            for u in range(2):
+                ts(V("hs", 4 * t + u, 4 * t + u + 1), V("psh", 512 * u + t, 512 * u + t + 1), V("ff", u, u + 1), OP.mult, V("ho", u, u + 1), OP.add)
+        mine, own = V("hs", 4 * t, 4 * t + 2), V("qh%d" % t, 2 * rank, 2 * rank + 2)
+        allgather(mine, "qh%d" % t, 2, "ah%d" % t)
+        dma("s", ap(own), ap(mine), "dh", [own], [mine])
 
     heights(0)
     iota(V("sv"), [[1, 16], [16, 16]], 1, 0)
+    iota(V("rs8"), [[0, 16], [1, 8]], 0, 0)
+    iota(V("rs3"), [[0, 16], [1, 3]], 0, 0)
     iota(V("io512"), [[1, 512]], 0, 0)
 
     ts(CI["hs"], P, 4, SHR, 1, AND)
@@ -332,10 +354,10 @@ def rank_program(g, core, T, topo):
     ts(CF["noff"], CF["i"], 128.0, OP.mult, -1920.0, OP.add)
     ts(CF["top"], CF["i"], -128.0, OP.mult, 2176.0, OP.add)
     ts(CF["k0"], CF["i"], -1.0 / 32, OP.mult, 256.0, OP.add)
-    for k in range(3):
-        ts(V("rst", 256 * k, 256 * k + 256), V("iot16"), 0.0, OP.not_equal)
+    ts(V("rst"), V("iot16"), 0.0, OP.not_equal)
     ts(V("iot32"), V("iot16", 0, 64), 1.0 / 32, OP.mult)
     fill(V("d1"), 2048.0)
+    cp(V("rsb"), V("rst"))
     ts(V("tmpi", 0, 16), V("jr", 0, 16), -8.0, OP.mult, CF["g"], OP.subtract)
     ts(V("kk", 48, 64), V("tmpi", 0, 16), CF["k0"], OP.add)
 
@@ -356,14 +378,14 @@ def rank_program(g, core, T, topo):
         tt(CI["t5"], CI["t5"], CI["i1"], OP.add)
         cp(LR2, CI["t6"])
         ts(V("tmpi", 16, 32), V("jr", 0, 16), 1, SHR, 3, AND)
-        cp(LCH, CI["t5"])
+        ts(LCH, CI["t5"], 8.0, OP.mult, 7.0, OP.add)
         ts(V("tmpi", 32, 48), V("jr", 0, 16), 3, SHR)
         ts(V("tmpi", 48, 64), V("tmpi", 16, 32), -1.0, OP.mult, CF["as"], OP.add)
         ts(V("tmpi", 32, 48), V("tmpi", 32, 48), 2.0, OP.mult, CF["hs"], OP.add)
         ts(V("tmpi", 48, 64), V("tmpi", 48, 64), 3, AND)
         ts(V("tmpi", 64, 96), V("jr", 0, 32), 1, SHR)
         ts(V("tmpi", 48, 64), V("tmpi", 48, 64), 4.0, OP.mult)
-        cp(LB2, V("tmpi", 64, 96))
+        ts(LB2, V("tmpi", 64, 96), 8.0, OP.mult, 7.0, OP.add)
         tt(V("tmpi", 48, 64), V("tmpi", 48, 64), V("tmpi", 32, 48), OP.add)
         ts(V("th"), V("thx"), -1.0, OP.add, -1.0 / 64, OP.mult)
         cp(LF, V("tmpi", 48, 64))
@@ -380,11 +402,18 @@ def rank_program(g, core, T, topo):
         fill(V("ones"), 1.0)
         fill(V("cc", 8, 9), float(4 * CA))
         fill(V("pf"), 0.0)
-        fill(V("zz"), 0.0)
+        ts(V("rs8"), V("rs8"), 0.0, OP.not_equal)
+        ts(V("rs3"), V("rs3"), 0.0, OP.not_equal)
+        ts(CI["t0"], P, 7, AND)
+        ts(CI["t1"], CI["i0"], 4.0, OP.mult, CF["as"], OP.add)
         ts(V("sv"), V("sv"), CF["g256"], OP.add)
+        ts(CI["t0"], CI["t0"], 16.0, OP.mult)
+        ts(LH, CI["t1"], 2.0, OP.mult)
         ts(V("tmpi", 96, 112), V("jr", 0, 16), 1, AND)
+        tt(CF["sZ"], CI["t0"], CI["i3"], OP.add)
         ts(V("dum"), V("jr", 0, 16), 16.0, OP.mult, CF["i"], OP.add)
         tt(V("tmpi", 112, 128), V("jr", 0, 16), V("tmpi", 96, 112), OP.subtract)
+        ts(LZ, V("jr", 0, 8), 2.0, OP.mult, CF["sZ"], OP.add)
         ts(V("tmpi", 96, 112), V("tmpi", 96, 112), CF["hs"], OP.not_equal)
         ts(V("dum"), V("dum"), float(DUMMY), OP.add)
         tt(V("tmpi", 96, 112), V("tmpi", 96, 112), V("tmpi", 112, 128), OP.add)
@@ -420,13 +449,16 @@ def rank_program(g, core, T, topo):
 
     for t in range(R):
         ct, pt, qh, hl = "ct%d" % t, "pt%d" % t, "qh%d" % t, "hl%d" % t
-        cp(V(qh, 2 * rank, 2 * rank + 2), V("hs", 2 * t, 2 * t + 2))
-        shift_all(qh, 16)
+        shift_now(qh, 16)
         cross(qh)
-        cp(V("wt"), IND(V(qh), LW))
-        tt(V("gm"), IND(V("wt"), V("on")), V("mf"), OP.mult)
-        tr(V("tt"), V("gm"))
-        scan(V("ss"), V("rst"), V("tt"), OP.mult, OP.add)
+        cp(V("wt", 0, 64), IND(V(qh), V("lst", 2, 6)), "a")
+        cp(V("wt", 64, 128), IND(V(qh), V("lst", 6, 10)), "v")
+        for j in range(J):
+            tt(V("gm", 256 * j, 256 * j + 256), IND(V("wt"), V("on", 16 * j, 16 * j + 16)), V("mf", 256 * j, 256 * j + 256), OP.mult)
+        for j in range(J):
+            tr(V("tt", 256 * j, 256 * j + 256), V("gm", 256 * j, 256 * j + 256))
+        for j in range(J):
+            scan(V("ss", 256 * j, 256 * j + 256), V("rst"), V("tt", 256 * j, 256 * j + 256), OP.mult, OP.add)
         tt(V("sm", 0, 16), V("ss", 15, 256, 16), V("ss", 271, 512, 16), OP.max)
         tt(V("sm", 16, 32), V("ss", 527, 768, 16), V(qh, 0, 16), OP.max)
         tt(V("sm", 32, 48), V("sm", 0, 16), V("sm", 16, 32), OP.max)
@@ -451,14 +483,14 @@ def rank_program(g, core, T, topo):
             if step == 9:
                 break
             ts(V("oo"), IND(V("q"), LO1), CF["noff"], OP.add)
-            scan(V("mk"), V("rst", 0, 256), V("d1"), OP.mult, OP.add)
+            scan(V("mk"), V("rsb"), V("d1"), OP.mult, OP.add)
             ts(V("cor"), V("lof"), 4096.0, OP.mult, CF["m128i"], OP.add)
-            for h in range(2):
-                cp(V("gm", 128 * h, 128 * h + 128), IND(V("wt"), V("oo", 8 * h, 8 * h + 8)), "a")
-            tr(V("tt", 0, 128), V("gm", 0, 128))
-            scan(V("ss", 0, 128), V("mk", 0, 128), V("tt", 0, 128), OP.min, OP.max)
-            tr(V("tt", 128, 256), V("gm", 128, 256))
-            scan(V("ss", 128, 256), V("mk", 128, 256), V("tt", 128, 256), OP.min, OP.max)
+            cp(V("gm", 0, GA), IND(V("wt"), V("oo", 0, GA // 16)), "a")
+            cp(V("gm", GA, 256), IND(V("wt"), V("oo", GA // 16, 16)), "v")
+            tr(V("tt", GA, 256), V("gm", GA, 256))
+            tr(V("tt", 0, GA), V("gm", 0, GA))
+            scan(V("ss", GA, 256), V("mk", GA, 256), V("tt", GA, 256), OP.min, OP.max)
+            scan(V("ss", 0, GA), V("mk", 0, GA), V("tt", 0, GA), OP.min, OP.max)
             tt(V("q", 0, 16), V("ss", 15, 256, 16), V("cor"), OP.add)
         ts(V("p2"), IND(V("q"), LP2), CF["noff"], OP.add)
         for step in range(3):
@@ -471,7 +503,7 @@ def rank_program(g, core, T, topo):
             ts(V("cor", 0, 4), V("lof", 0, 4), 4096.0, OP.mult, -1920.0, OP.add)
             scan(V("ss", 0, 64), V("mk", 0, 64), V("tt", 0, 64), OP.mult, OP.max)
             tt(V("p2" if step < 2 else "q2", 0, 4), V("ss", 15, 64, 16), V("cor", 0, 4), OP.add)
-        shift_all("q2", 4)
+        shift_now("q2", 4)
         cp(V("rb", 0, 128), IND(V("q2"), V("lst", 28, 36)), "v")
         cp(V("rb", 128, 256), IND(V("q2"), V("lst", 36, 44)), "a")
         tr(V("rf"), V("rb"))
@@ -509,25 +541,25 @@ def rank_program(g, core, T, topo):
         in_range(V("r2f", 80, 96), V("r2f", 96, 112), V("r2f", 32, 48), set_c, 0)
         ts(V("r2f", 48, 64), V("r2f", 32, 48), float(-M * rank), OP.add)
         tt(V("r2f", 112, 128), V("r2f", 48, 64), V("mym"), OP.not_equal)
-        tt(V("s1"), V(hl, 0, 64), V(hl, 64, 128), OP.add)
-        tt(V("s1", 0, 32), V("s1", 0, 32), V("s1", 32, 64), OP.add)
-        tt(V("sz"), V("s1", 0, 16), V("s1", 16, 32), OP.add)
+        cp(V("s1"), IND(V(hl), LZ))
+        scan(V("sz"), V("rs8"), V("s1"), OP.mult, OP.add)
+        size = V("sz", 7, 128, 8)
         cp(V("yb", 0, 256), IND(V("sz"), V("lst", 44, 60)), "a")
         cp(V("yb", 256, 512), IND(V("sz"), V("lst", 60, 76)), "v")
         tr(V("yt"), V("yb"))
         sign(V("jy", 0, CA), V("yt", 0, CA), CF["ba"], V("cc", 0, 1))
         ts(V("jy", CA, 512), V("yt", CA, 512), CF["bd"], OP.is_ge, 2.0, OP.mult)
         red(V("cc", 1, 2), V("jy", CA, 512), OP.add)
-        shift_all("cc", 2)
+        shift_now("cc", 2)
         red(V("cs", 0, 1), V("cc", 0, 9), OP.add)
         ts(V("bb", 0, 32), V("c128"), V("cs", 0, 1), OP.is_le, 2.0, OP.mult)
         ts(V("bb", 32, 64), V("c128"), V("cs", 0, 1), OP.is_gt, V("cs", 0, 1), OP.mult)
         tr(V("bt"), V("bb"))
         red(V("cs", 1, 2), V("bt", 0, 32), OP.add)
         red(V("cs", 2, 3), V("bt", 32, 64), OP.max)
-        ts(V("fl", 0, 16), V("sz"), -2.0, OP.add, V("cs", 1, 2), OP.is_gt)
-        ts(V("fl", 16, 32), V("sz"), -2.0, OP.add, V("cs", 1, 2), OP.is_equal)
-        ts(V("fl", 32, 48), V("sz"), -2.0, OP.add, V("cs", 1, 2), OP.is_lt)
+        ts(V("fl", 0, 16), size, -2.0, OP.add, V("cs", 1, 2), OP.is_gt)
+        ts(V("fl", 16, 32), size, -2.0, OP.add, V("cs", 1, 2), OP.is_equal)
+        ts(V("fl", 32, 48), size, -2.0, OP.add, V("cs", 1, 2), OP.is_lt)
         scan(V("sc"), V("rst", 0, 32), V("fl", 0, 32), OP.mult, OP.add)
         ts(V("pf", 9, 10), V("cs", 2, 3), 0.5, OP.mult)
         ts(V("bb", 0, 32), V("ones"), V("sc", 15, 16), OP.mult)
@@ -549,54 +581,56 @@ def rank_program(g, core, T, topo):
         ts(V("bs", 32, 48), V("bs", 32, 48), 15.0, OP.add)
         red(V("rr", 2, 3), V("pf", 0, 10, 2), OP.add)
         red(V("rr", 3, 4), V("pf", 1, 10, 2), OP.add)
-        tt(V("bs", 48, 64), V("bs", 48, 64), V("bs", 32, 48), OP.add)
-        ts(V("bs", 64, 80), V("fl", 0, 16), V("rr", 2, 3), OP.mult)
-        ts(V("bs", 80, 96), V("fl", 16, 32), V("rr", 3, 4), OP.mult)
-        tt(V("bs", 64, 80), V("bs", 64, 80), V("bs", 48, 64), OP.add)
-        tt(V("vv"), V("bs", 64, 80), V("bs", 80, 96), OP.add)
-        cp(V("vo"), V("vv"))
+        tt(V("v3", 0, 48, 3), V("bs", 48, 64), V("bs", 32, 48), OP.add)
+        ts(V("v3", 1, 48, 3), V("fl", 0, 16), V("rr", 2, 3), OP.mult)
+        ts(V("v3", 2, 48, 3), V("fl", 16, 32), V("rr", 3, 4), OP.mult)
+        scan(V("v3s"), V("rs3"), V("v3"), OP.mult, OP.add)
+        cp(V("vo"), V("v3s", 2, 48, 3))
         emit("v", lambda: g.vector.tensor_copy(ap(IND(V("lw"), V("vo"))), ap(V("sv"))), [V("lw")], [V("sv"), V("vo")])
         tr(V("lt", 0, 64), V("lw", 16, 80))
         tr(V("lt", 64, 160), V("lw", 0, 96))
-        tt(V("zz", 0, 5), V("lt", 0, 160, 32), V("lt", 16, 160, 32), OP.add)
-        shift_all("zz", 8)
-        tt(V("zs"), V("zz", 0, 16), V("zz", 16, 32), OP.add)
-        tt(V("zs", 0, 8), V("zs", 0, 8), V("zs", 8, 16), OP.add)
-        ts(V("pl", 0, 16), IND(V("zs", 0, 8), LCH), float(-1 - M * rank), OP.add, float(M - 1), OP.min)
+        cp(V("zz", 0, 40, 4), V("lt", 0, 160, 16))
+        shift_at_once(lambda m, a, b: V("zz", m, 40, 4, a, b), lambda a, b: V("lt", 0, 160, 16, a, b))
+        scan(V("zs"), V("rs8", 0, 40), V("zz"), OP.mult, OP.add)
+        ts(V("pl", 0, 16), IND(V("zs"), LCH), float(-1 - M * rank), OP.add, float(M - 1), OP.min)
         ca, pa, cb, pb, cc_, pc_ = ["%s%s%d" % (x, s_, t) for s_ in "abc" for x in "cp"]
         pick(V(ca, 0, K), V(pa, 0, K), V(ct, 0, M), V(pt, 0, M), V("pl", 0, 4))
         swap(peer_a, ca, pa, "aa%d" % t)
-        cp(V("ch"), IND(V("zs", 0, 8), LCH))
-        ts(V("q", 0, 16), V("vv"), CF["o4096"], OP.add)
+        cp(V("ch"), IND(V("zs"), LCH))
+        ts(V("q", 0, 16), V("v3s", 2, 48, 3), CF["o4096"], OP.add)
         in_range(V("cht", 0, 4), V("cht", 4, 8), V("ch", 0, 4), set_a, 1)
         in_range(V("cht", 8, 12), V("cht", 12, 16), V("ch", 0, 4), set_b, 1)
         tt(V("cht", 0, 4), V("cht", 0, 4), V("dum", 0, 4), OP.add)
         tt(V("cht", 8, 12), V("cht", 8, 12), V("dum", 0, 4), OP.add)
         ts(V("pl", 16, 20), V("cht", 0, 4), float(-DUMMY), OP.add)
         ts(V("pl", 20, 24), V("cht", 8, 12), float(-DUMMY), OP.add)
-        shift_all("q", 16)
-        cross("q")
-        cp(V("wt"), IND(V("q"), LW), "a")
+        shift_now("q", 16)
         pick(V(cb, 0, K), V(pb, 0, K), V(ca), V(pa), V("pl", 16, 20))
         swap(peer_b, cb, pb, "ab%d" % t)
-        cp(V("gm", 0, 256), IND(V("wt"), V("o3")), "a")
+        cross("q")
+        cp(V("wt"), IND(V("q"), LW), "a")
+        cp(V("gm", 0, 128), IND(V("wt"), V("o3", 0, 8)), "a")
+        cp(V("gm", 128, 256), IND(V("wt"), V("o3", 8, 16)), "v")
         tr(V("tt", 0, 256), V("gm", 0, 256))
         scan(V("ss", 0, 256), V("mk3"), V("tt", 0, 256), OP.mult, OP.max)
+        pick(V(cc_, 0, K), V(pc_, 0, K), V(cb), V(pb), V("pl", 20, 24))
+        swap(peer_c, cc_, pc_, "ac%d" % t)
         tt(V("cht", 16, 32), V("ss", 15, 256, 16), V("r2f", 64, 80), OP.add)
         ts(V("cht", 32, 48), V("cht", 16, 32), -16.0, OP.add, float(K - 1), OP.min)
         ts(V("cht", 48, 64), V("cht", 16, 32), 79.5, OP.is_lt, float(M), OP.mult)
         tt(V("cht", 32, 48), V("cht", 32, 48), V("r2f", 80, 96), OP.add)
         tt(V("cht", 48, 64), V("cht", 48, 64), V("r2f", 112, 128), OP.mult)
         cp(V("pl", 32, 48), IND(V("cht", 32, 48), LA))
+        if t + 1 < R:
+            ts(V("ff"), IND(V("cht", 48, 64), LH), 1.0 / M, OP.mult)
+            products(t, 0)
+            ts(V("nf", 0, 2), V("ff", 0, 2), -1.0, OP.mult, 1.0, OP.add)
+            tt(V("ho", 0, 2), V("psh", t + 1, 1024, 512), V("nf", 0, 2), OP.mult)
         tt(V("cht", 48, 64), V("cht", 48, 64), V("mym"), OP.add)
         cp(V("pl", 48, 64), IND(V("cht", 48, 64), LA))
-        pick(V(cc_, 0, K), V(pc_, 0, K), V(cb), V(pb), V("pl", 20, 24))
-        swap(peer_c, cc_, pc_, "ac%d" % t)
-        if t == 0:
-            unpackers()
-        if t == 1:
-            quant(V("qw"), V("sw"), V("ws"))
         for b in range(4):
+            if t == 0 and b == 0:
+                unpackers()
             mm(V("psd", 512 * b, 512 * b + M), V("qe", 128 * b, 128 * b + 128), V("se", 128 * b, 128 * b + 128), V(ct, 0, M), V(pt, 0, M), True, False)
         cr, pr = "cr%d" % t, "pr%d" % t
         pick(V(cr), V(pr), V(cc_), V(pc_), V("pl", 32, 48))
@@ -609,9 +643,11 @@ def rank_program(g, core, T, topo):
             else:
                 emit("a", lambda: g.scalar.activation(ap(o), ap(i_), ACT.Copy, scale=0.5), [o], [i_])
         quant(V(ct, M, 2 * M), V(pt, M, 2 * M), V("ht"))
-        pick(V("ct%d" % (t + 1), 0, M), V("pt%d" % (t + 1), 0, M), V(ct), V(pt), V("pl", 48, 64))
         if t + 1 < R:
             heights(t + 1)
+        pick(V("ct%d" % (t + 1), 0, M), V("pt%d" % (t + 1), 0, M), V(ct), V(pt), V("pl", 48, 64))
+        if t == 0:
+            quant(V("qw"), V("sw"), V("ws"))
 
     ct, pt = "ct%d" % R, "pt%d" % R
     mm(V("psy", 0, M), V("qw"), V("sw"), V(ct, 0, M), V(pt, 0, M), True, True)

@@ -6,7 +6,7 @@ F32, I32, U16, BF, CODE, PLANE = "float32", "int32", "uint16", "bfloat16", "floa
 NA = 8
 ND = 16 - NA
 CA = 384
-GA = 160
+GA = 128
 DUMMY = 2200
 
 SCRATCH = {}
@@ -23,8 +23,8 @@ for _n, _w, _d in [
     ("ci", 32, I32), ("cf", 32, F32), ("jr", 48, I32), ("tmpi", 128, I32), ("lst", 160, U16),
     ("iot16", 256, F32), ("iot32", 64, F32), ("rst", 256, F32), ("rs8", 128, F32), ("sv", 256, F32), ("tri", 64, F32), ("kk", 64, F32),
     ("nbi", 48, I32), ("nhi", 48, I32), ("nlo", 48, I32), ("qn", 160, F32), ("on", 48, U16), ("mt", 768, F32), ("mf", 768, F32),
-    ("hs", 12, F32), ("q", 160, F32), ("xx", 96, F32), ("wt", 128, F32), ("oo", 16, U16), ("d1", 256, BF),
-    ("gm", 768, F32), ("tt", 768, F32), ("ss", 768, F32), ("mk", 256, BF), ("hi", 16, I32), ("lof", 16, F32),
+    ("hs", 12, F32), ("q", 160, F32), ("xx", 96, F32), ("wt", 128, F32), ("oo", 16, U16), ("d1", 544, BF), ("qq", 160, F32), ("gp", 288, F32),
+    ("gm", 768, F32), ("tt", 768, F32), ("ss", 768, F32), ("mk", 544, BF), ("hi", 40, I32), ("lof", 40, F32),
     ("sm", 160, F32), ("p2", 16, F32), ("q2", 16, F32), ("rb", 256, F32), ("rf", 256, F32),
     ("ja", 256 * (NA + 1), BF), ("acc", 24, F32),
     ("rti", 256, I32), ("rta", 256, F32), ("rtb", 256, F32), ("rto", 768, F32),
@@ -37,8 +37,8 @@ for _n, _w, _d in [
     _sb(_n, _w, _d)
 ALIAS = {}
 for _b, _d, _names in (("kc", F32, [("thx", 16), ("th", 16), ("c128", 32), ("ones", 32), ("mym", 16), ("dum", 16), ("rs3", 48)]),
-                       ("wk", F32, [("cor", 16), ("cs", 8), ("rr", 8), ("ch", 16), ("v3", 48), ("v3s", 48), ("ff", 16), ("nf", 4), ("ho", 4), ("zs", 40)]),
-                       ("wb", BF, [("zb", 256), ("ob", 256), ("rsb", 256), ("jd", 256 * ND), ("js", 256 * ND)])):
+                       ("wk", F32, [("cor", 40), ("cs", 8), ("rr", 8), ("ch", 16), ("v3", 48), ("v3s", 48), ("ff", 16), ("nf", 4), ("ho", 4), ("zs", 40)]),
+                       ("wb", BF, [("zb", 256), ("ob", 256), ("rsb", 768), ("jd", 256 * ND), ("js", 256 * ND)])):
     _o = 0
     for _n, _w in _names:
         ALIAS[_n] = (_b, _o, _w)
@@ -240,15 +240,6 @@ def rank_program(g, core, T, topo):
     for s_ in (set_a, set_b, set_c):
         assert s_ == list(range(s_[0], s_[0] + len(s_)))
 
-    def shift_one(buf, w):
-        for a in range(4):
-            b = (a + 1) % 4
-            cp(V(buf, w, 2 * w, 1, 32 * b, 32 * b + 32), V(buf, 0, w, 1, 32 * a, 32 * a + 32), "a" if a % 2 else "v")
-
-    def shift_two(buf, w):
-        cp(V(buf, 2 * w, 4 * w, 1, 64, 128), V(buf, 0, 2 * w, 1, 0, 64), "v")
-        cp(V(buf, 2 * w, 4 * w, 1, 0, 64), V(buf, 0, 2 * w, 1, 64, 128), "a")
-
     def shift_at_once(dst_, src):
         cp(dst_(2, 64, 128), src(0, 64), "v")
         cp(dst_(2, 0, 64), src(64, 128), "a")
@@ -257,8 +248,8 @@ def rank_program(g, core, T, topo):
                 b = (a + m) % 4
                 cp(dst_(m, 32 * b, 32 * b + 32), src(32 * a, 32 * a + 32), "a" if a % 2 else "v")
 
-    def shift_now(buf, w):
-        shift_at_once(lambda m, a, b: V(buf, m * w, m * w + w, 1, a, b), lambda a, b: V(buf, 0, w, 1, a, b))
+    def shift_now(buf, w, n=None):
+        shift_at_once(lambda m, a, b: V(buf, m * w, m * w + (n or w), 1, a, b), lambda a, b: V(buf, 0, n or w, 1, a, b))
 
     def cross(buf):
         tr(V("xx", 16, 80), V(buf, 0, 64))
@@ -271,13 +262,14 @@ def rank_program(g, core, T, topo):
     dma("s", T.ws[:], T.w[:], "dw", [V("ws")])
 
     CI = {n: V("ci", k, k + 1) for k, n in enumerate(
-        ["p", "i", "g", "hs", "as", "i0", "i1", "i12", "i3", "i123", "q", "ne", "hoff", "nh", "d", "t0", "t1", "t2", "t3", "t4", "t5", "t6"])}
+        ["p", "i", "g", "hs", "as", "i0", "i1", "i12", "i3", "i123", "q", "ne", "hoff", "nh", "d", "t0", "t1", "t2", "t3", "t4", "t5", "t6",
+         "r0", "r1", "r2", "r3", "r4", "r5"])}
     CF = {n: V("cf", k, k + 1) for k, n in enumerate(
-        ["p", "i", "g", "hs", "as", "q", "m128i", "noff", "top", "o4096", "sW", "sO", "p4", "ba", "bd", "g256", "k0", "sZ"])}
+        ["p", "i", "g", "hs", "as", "q", "m128i", "noff", "top", "o4096", "sW", "sO", "p4", "ba", "bd", "g256", "k0", "sZ", "sW2"])}
     LNB, LW, LO, LP2, LO2, LR2, LA, LCH = V("lst", 0, 1), V("lst", 2, 10), V("lst", 10, 13), V("lst", 14, 15), V("lst", 16, 17), V("lst", 18, 19), V("lst", 20, 21), V("lst", 22, 23)
-    LO1 = V("lst", 10, 11)
     LI, LF, LB2 = V("lst", 24, 27), V("lst", 28, 44), V("lst", 44, 76)
     LH, LZ = V("lst", 128, 129), V("lst", 130, 138)
+    LW2, LQ, LS = V("lst", 138, 146), V("lst", 146, 147), V("lst", 148, 151)
 
     def LB(a, b):
         return V("lst", 80 + a, 80 + b)
@@ -291,15 +283,43 @@ def rank_program(g, core, T, topo):
     P = CI["p"]
     ts(CI["i"], P, 15, AND)
     ts(CI["g"], P, 4, SHR)
+    ts(CI["hs"], P, 4, SHR, 1, AND)
+    ts(CI["as"], P, 5, SHR)
+    ts(CI["i0"], P, 1, AND)
     ts(CI["t0"], CI["i"], 5.0, OP.min, 8.0, OP.mult)
+    ts(CI["i1"], P, 1, SHR, 1, AND)
+    ts(CI["i12"], P, 1, SHR, 3, AND)
+    ts(CI["i3"], P, 3, SHR, 1, AND)
+    ts(CI["i123"], P, 1, SHR, 7, AND)
     tt(CI["t1"], CI["t0"], CI["g"], OP.add)
+    ts(CI["q"], P, 31, AND)
+    cp(V("cf", 0, 5), V("ci", 0, 5))
+    tt(CI["ne"], CI["i0"], CI["hs"], OP.not_equal)
+    ts(CI["hoff"], CI["hs"], -32.0, OP.mult, 96.0, OP.add)
     cp(LNB, CI["t1"])
+    tt(CI["t2"], CI["as"], CI["i12"], OP.subtract)
+    fill(V("xx"), 0.0)
+    fill(V("qn", 48, 64), 0.0)
+    ts(CI["t3"], CI["i123"], 2.0, OP.mult, CF["hs"], OP.add)
+    tt(CI["nh"], CI["ne"], CI["hoff"], OP.mult)
+    ts(CI["d"], CI["t2"], 3, AND)
+    cp(LB(0, 48), V("jr"))
     cp(V("nbs", p0=32, p1=64), V("nbs", p1=32))
-    cp(V("nbs", p0=64), V("nbs", p1=64))
+    cp(V("nbs", p0=64, p1=96), V("nbs", p1=32))
+    cp(V("nbs", p0=96), V("nbs", p1=32))
+    tt(CF["sO"], CI["t3"], CI["nh"], OP.add)
+    tt(CI["t4"], CI["i3"], CI["nh"], OP.add)
+    ts(CI["t5"], CI["d"], 16.0, OP.mult)
     cp(V("nbo"), IND(V("nbs"), LNB))
     allgather(V("nbo", 0, 6), "nbl", 6, "an")
     quant(V("ct0", 0, M), V("pt0", 0, M), V("xs"))
     quant(V("qu"), V("su"), V("us"))
+    ts(LO, V("jr", 0, 3), 16.0, OP.mult, CF["sO"], OP.add)
+    tt(CF["sW"], CI["t4"], CI["t5"], OP.add)
+    ts(LI, V("jr", 0, 3), 0.0, OP.mult, CF["i"], OP.add)
+    cp(CF["q"], CI["q"])
+    ts(CF["m128i"], CF["i"], -128.0, OP.mult)
+    ts(CF["noff"], CF["i"], 128.0, OP.mult, -1920.0, OP.add)
 
     def products(t, c0):
         for u in range(2):
@@ -324,107 +344,114 @@ def rank_program(g, core, T, topo):
     iota(V("rs3"), [[0, 16], [1, 3]], 0, 0)
     iota(V("io512"), [[1, 512]], 0, 0)
 
-    ts(CI["hs"], P, 4, SHR, 1, AND)
-    ts(CI["as"], P, 5, SHR)
-    ts(CI["i0"], P, 1, AND)
-    ts(CI["i1"], P, 1, SHR, 1, AND)
-    ts(CI["i12"], P, 1, SHR, 3, AND)
-    ts(CI["i3"], P, 3, SHR, 1, AND)
-    ts(CI["i123"], P, 1, SHR, 7, AND)
-    ts(CI["q"], P, 31, AND)
-    fill(V("xx"), 0.0)
-    fill(V("qn", 48, 64), 0.0)
-    cp(V("cf", 0, 5), V("ci", 0, 5))
-    cp(CF["q"], CI["q"])
-    tt(CI["ne"], CI["i0"], CI["hs"], OP.not_equal)
-    ts(CI["hoff"], CI["hs"], -32.0, OP.mult, 96.0, OP.add)
-    tt(CI["t2"], CI["as"], CI["i12"], OP.subtract)
-    ts(CI["t3"], CI["i123"], 2.0, OP.mult, CF["hs"], OP.add)
-    tt(CI["nh"], CI["ne"], CI["hoff"], OP.mult)
-    ts(CI["d"], CI["t2"], 3, AND)
-    cp(LB(0, 48), V("jr"))
-    tt(CF["sO"], CI["t3"], CI["nh"], OP.add)
-    tt(CI["t4"], CI["i3"], CI["nh"], OP.add)
-    ts(CI["t5"], CI["d"], 16.0, OP.mult)
-    ts(LO, V("jr", 0, 3), 16.0, OP.mult, CF["sO"], OP.add)
-    tt(CF["sW"], CI["t4"], CI["t5"], OP.add)
-    ts(LI, V("jr", 0, 3), 0.0, OP.mult, CF["i"], OP.add)
     ts(LW, V("jr", 0, 8), 2.0, OP.mult, CF["sW"], OP.add)
-    ts(CF["m128i"], CF["i"], -128.0, OP.mult)
-    ts(CF["noff"], CF["i"], 128.0, OP.mult, -1920.0, OP.add)
     ts(CF["top"], CF["i"], -128.0, OP.mult, 2176.0, OP.add)
     ts(CF["k0"], CF["i"], -1.0 / 32, OP.mult, 256.0, OP.add)
     ts(V("rst"), V("iot16"), 0.0, OP.not_equal)
-    ts(V("iot32"), V("iot16", 0, 64), 1.0 / 32, OP.mult)
-    fill(V("d1"), 2048.0)
-    cp(V("rsb"), V("rst"))
     ts(V("tmpi", 0, 16), V("jr", 0, 16), -8.0, OP.mult, CF["g"], OP.subtract)
+    ts(CI["r0"], CI["hs"], -2.0, OP.mult, 18.0, OP.add)
+    tt(CI["r1"], CI["i3"], CI["hs"], OP.not_equal)
+    tt(CI["r2"], CI["i1"], CI["hs"], OP.not_equal)
+    ts(CI["r3"], CI["d"], 40.0, OP.mult)
+    ts(CI["r5"], CI["t3"], -1.0, OP.add, 0.0, OP.max)
+    for k in range(3):
+        cp(V("rsb", 256 * k, 256 * k + 256), V("rst"), "a")
     ts(V("kk", 48, 64), V("tmpi", 0, 16), CF["k0"], OP.add)
+    tt(CI["r4"], CI["ne"], CI["r0"], OP.mult)
+    tt(CI["r1"], CI["r1"], CI["r0"], OP.mult)
+    tt(CI["r2"], CI["r2"], CI["r0"], OP.mult)
+    tt(CI["r3"], CI["r3"], CI["i0"], OP.add)
+    tt(CI["r5"], CI["r5"], CI["nh"], OP.add)
+    fill(V("d1"), 2048.0)
+    tt(CI["r4"], CI["r4"], CI["t3"], OP.add)
+    tt(CF["sW2"], CI["r3"], CI["r1"], OP.add)
+    cp(V("lst", 148, 149), CF["sO"])
+    ts(V("lst", 150, 151), CI["nh"], 15.0, OP.add)
+    cp(V("lst", 149, 150), CI["r5"])
+    fill(V("gp"), 0.0)
+    fill(V("q"), 0.0)
+    fill(V("qq"), 0.0)
+    cp(LQ, CI["r4"])
+    ts(LW2, V("jr", 0, 8), 2.0, OP.mult, CF["sW2"], OP.add)
 
-    def late_constants():
-        ts(CI["t0"], CI["i1"], float(2 * rank), OP.add)
+    def constants():
+        tt(CI["r2"], CI["r2"], CI["i0"], OP.add)
         ts(LO2, CI["i1"], 2.0, OP.mult, CF["hs"], OP.add)
         ts(CI["t2"], CI["d"], 4.0, OP.mult)
+        yield
         ts(CI["t3"], CI["i3"], 2.0, OP.mult)
         ts(CI["t4"], CI["i123"], 2.0, OP.mult)
         ts(CI["t5"], CI["hs"], -1.0, OP.mult, 3.0, OP.add)
-        tt(CI["t1"], CI["t0"], CI["nh"], OP.add)
+        yield
+        ts(V("tmpi", 16, 32), V("jr", 0, 16), 1, SHR, 3, AND)
         tt(CI["t6"], CI["t2"], CI["t3"], OP.add)
         tt(CI["t4"], CI["t4"], CI["ne"], OP.add)
+        yield
         tt(CI["t5"], CI["t5"], CI["ne"], OP.mult)
-        cp(LP2, CI["t1"])
+        ts(V("tmpi", 32, 48), V("jr", 0, 16), 3, SHR)
+        ts(V("tmpi", 48, 64), V("tmpi", 16, 32), -1.0, OP.mult, CF["as"], OP.add)
+        yield
         tt(CI["t6"], CI["t6"], CI["ne"], OP.add)
         cp(LA, CI["t4"])
         tt(CI["t5"], CI["t5"], CI["i1"], OP.add)
-        cp(LR2, CI["t6"])
-        ts(V("tmpi", 16, 32), V("jr", 0, 16), 1, SHR, 3, AND)
-        ts(LCH, CI["t5"], 8.0, OP.mult, 7.0, OP.add)
-        ts(V("tmpi", 32, 48), V("jr", 0, 16), 3, SHR)
-        ts(V("tmpi", 48, 64), V("tmpi", 16, 32), -1.0, OP.mult, CF["as"], OP.add)
+        yield
         ts(V("tmpi", 32, 48), V("tmpi", 32, 48), 2.0, OP.mult, CF["hs"], OP.add)
         ts(V("tmpi", 48, 64), V("tmpi", 48, 64), 3, AND)
+        cp(LR2, CI["t6"])
+        yield
         ts(V("tmpi", 64, 96), V("jr", 0, 32), 1, SHR)
+        ts(LCH, CI["t5"], 8.0, OP.mult, 7.0, OP.add)
         ts(V("tmpi", 48, 64), V("tmpi", 48, 64), 4.0, OP.mult)
+        yield
+        ts(V("th"), V("thx"), -1.0, OP.add, -1.0 / 64, OP.mult)
         ts(LB2, V("tmpi", 64, 96), 8.0, OP.mult, 7.0, OP.add)
         tt(V("tmpi", 48, 64), V("tmpi", 48, 64), V("tmpi", 32, 48), OP.add)
-        ts(V("th"), V("thx"), -1.0, OP.add, -1.0 / 64, OP.mult)
-        cp(LF, V("tmpi", 48, 64))
+        yield
         fill(V("ob"), 1.0)
-
-    def later_constants():
+        cp(LF, V("tmpi", 48, 64))
+        ts(LP2, CI["r2"], float(2 * rank), OP.add)
+        yield
+        ts(V("iot32"), V("iot16", 0, 64), 1.0 / 32, OP.mult)
+        ts(CF["p4"], P, 4.0, OP.mult)
         ts(CF["o4096"], CF["i"], -4096.0, OP.mult, 61440.0, OP.add)
+        yield
         ts(CF["ba"], CF["q"], -2.0, OP.mult, -3.0, OP.add)
         ts(CF["bd"], CF["q"], 2.0, OP.mult, 4.0, OP.add)
         ts(CF["g256"], CF["g"], 256.0, OP.mult)
-        ts(CF["p4"], P, 4.0, OP.mult)
+        yield
         ts(V("tri"), V("tri"), CF["q"], OP.is_lt)
         fill(V("c128"), 128.0)
         fill(V("ones"), 1.0)
+        yield
         fill(V("cc", 8, 9), float(4 * CA))
         fill(V("pf"), 0.0)
         ts(V("rs8"), V("rs8"), 0.0, OP.not_equal)
+        yield
         ts(V("rs3"), V("rs3"), 0.0, OP.not_equal)
         ts(CI["t0"], P, 7, AND)
         ts(CI["t1"], CI["i0"], 4.0, OP.mult, CF["as"], OP.add)
-        ts(V("sv"), V("sv"), CF["g256"], OP.add)
+        yield
         ts(CI["t0"], CI["t0"], 16.0, OP.mult)
         ts(LH, CI["t1"], 2.0, OP.mult)
         ts(V("tmpi", 96, 112), V("jr", 0, 16), 1, AND)
+        yield
         tt(CF["sZ"], CI["t0"], CI["i3"], OP.add)
         ts(V("dum"), V("jr", 0, 16), 16.0, OP.mult, CF["i"], OP.add)
         tt(V("tmpi", 112, 128), V("jr", 0, 16), V("tmpi", 96, 112), OP.subtract)
+        yield
         ts(LZ, V("jr", 0, 8), 2.0, OP.mult, CF["sZ"], OP.add)
         ts(V("tmpi", 96, 112), V("tmpi", 96, 112), CF["hs"], OP.not_equal)
         ts(V("dum"), V("dum"), float(DUMMY), OP.add)
+        yield
         tt(V("tmpi", 96, 112), V("tmpi", 96, 112), V("tmpi", 112, 128), OP.add)
+        ts(V("sv"), V("sv"), CF["g256"], OP.add)
+        yield
         ts(V("mym"), V("tmpi", 96, 112), 16.0, OP.mult, CF["i"], OP.add)
 
-    def unpackers():
-        for b in range(4):
-            ts(V("et", 512 * b, 512 * b + 512), V("io512"), CF["p4"], OP.subtract, float(b), OP.is_equal)
-        quant(V("qe"), V("se"), V("et"))
+    rest = constants()
 
-    late_constants()
+    def unpacker(b):
+        ts(V("et", 512 * b, 512 * b + 512), V("io512"), CF["p4"], OP.subtract, float(b), OP.is_equal)
 
     cp(V("nbl", 6 * rank, 6 * rank + 6), V("nbo", 0, 6))
     for j in range(J):
@@ -433,14 +460,15 @@ def rank_program(g, core, T, topo):
     ts(V("nhi"), V("nbi"), 4, SHR)
     ts(V("nlo"), V("nbi"), 15, AND)
     cp(V("qn", 0, 48), V("nhi"))
-    ts(V("sm", 0, 48), V("nlo"), -1.0 / 32, OP.mult, 256.0, OP.add)
-    cross("qn")
-    tt(V("kk", 0, 48), V("sm", 0, 48), V("nhi"), OP.subtract)
-    cp(V("on"), IND(V("qn"), LO))
     tt(V("mt", 0, 256), IND(V("nlo"), LB(0, 16)), V("iot16"), OP.is_equal)
+    tr(V("xx", 16, 80), V("qn", 0, 64))
     tt(V("mt", 256, 512), IND(V("nlo"), LB(16, 32)), V("iot16"), OP.is_equal)
+    tr(V("qn", 64, 160), V("xx"))
     tt(V("mt", 512, 768), IND(V("nlo"), LB(32, 48)), V("iot16"), OP.is_equal)
+    ts(V("sm", 0, 48), V("nlo"), -1.0 / 32, OP.mult, 256.0, OP.add)
+    cp(V("on"), IND(V("qn"), LO))
     tr(V("mf"), V("mt"))
+    tt(V("kk", 0, 48), V("sm", 0, 48), V("nhi"), OP.subtract)
 
     def in_range(out, tmp, x, ranks, base):
         ts(out, x, float(M * ranks[0] + base), OP.is_ge, float(K), OP.mult)
@@ -466,44 +494,49 @@ def rank_program(g, core, T, topo):
         tt(V("sm", 112, 128), V("sm", 32, 48), V(qh, 0, 16), OP.is_equal)
         tt(V("sm", 64, 128), V("sm", 64, 128), V("kk"), OP.mult)
         tt(V("sm", 128, 160), V("sm", 64, 96), V("sm", 96, 128), OP.max)
-        tt(V("sm", 0, 16), V("sm", 128, 144), V("sm", 144, 160), OP.max)
-        ts(V("q", 0, 16), V("sm", 0, 16), -1.0, OP.mult, CF["top"], OP.add)
+        tt(V("q", 0, 16), V("sm", 128, 144), V("sm", 144, 160), OP.max)
+        tr(V("xx", 16, 48), V("q", 0, 32))
+        tr(V("q", 64, 128), V("xx", 0, 64))
+        ts(V("qq", 0, 48), IND(V("q"), LS), -1.0, OP.mult, CF["top"], OP.add)
         for step in range(10):
-            shift_one("q", 16)
+            next(rest, None)
             if step < 9:
-                cp(V("hi"), V("q", 0, 16))
-            shift_two("q", 16)
-            if step < 9:
-                tt(V("lof"), V("q", 0, 16), V("hi"), OP.subtract)
-            tr(V("xx", 16, 80), V("q", 0, 64))
-            if step < 9:
-                ts(V("d1", 0, 256, 16), V("lof"), -65536.0, OP.mult)
-            tr(V("q", 64, 160), V("xx"))
-            cp(V("wt"), IND(V("q"), LW), "a")
+                cp(V("hi", 0, 34), V("qq", 0, 34))
+            shift_now("qq", 40, 34)
+            cp(V("wt"), IND(V("qq"), LW2), "a")
             if step == 9:
                 break
-            ts(V("oo"), IND(V("q"), LO1), CF["noff"], OP.add)
-            scan(V("mk"), V("rsb"), V("d1"), OP.mult, OP.add)
-            ts(V("cor"), V("lof"), 4096.0, OP.mult, CF["m128i"], OP.add)
-            cp(V("gm", 0, GA), IND(V("wt"), V("oo", 0, GA // 16)), "a")
-            cp(V("gm", GA, 256), IND(V("wt"), V("oo", GA // 16, 16)), "v")
-            tr(V("tt", GA, 256), V("gm", GA, 256))
-            tr(V("tt", 0, GA), V("gm", 0, GA))
-            scan(V("ss", GA, 256), V("mk", GA, 256), V("tt", GA, 256), OP.min, OP.max)
-            scan(V("ss", 0, GA), V("mk", 0, GA), V("tt", 0, GA), OP.min, OP.max)
-            tt(V("q", 0, 16), V("ss", 15, 256, 16), V("cor"), OP.add)
-        ts(V("p2"), IND(V("q"), LP2), CF["noff"], OP.add)
+            tt(V("lof", 0, 34), V("qq", 0, 34), V("hi", 0, 34), OP.subtract)
+            ts(V("oo"), IND(V("qq", 0, 40), LQ), CF["noff"], OP.add)
+            ts(V("d1", 0, 544, 16), V("lof", 0, 34), -65536.0, OP.mult)
+            ts(V("cor", 0, 34), V("lof", 0, 34), 4096.0, OP.mult, CF["m128i"], OP.add)
+            cp(V("gp", 16, 16 + GA), IND(V("wt"), V("oo", 0, GA // 16)), "a")
+            cp(V("gp", 16 + GA, 272), IND(V("wt"), V("oo", GA // 16, 16)), "v")
+            scan(V("mk"), V("rsb", 0, 544), V("d1"), OP.mult, OP.add)
+            tr(V("tt", 0, 256), V("gp", 16, 272))
+            tr(V("tt", 256, 544), V("gp"))
+            scan(V("ss", 0, 256), V("mk", 0, 256), V("tt", 0, 256), OP.min, OP.max)
+            scan(V("ss", 256, 544), V("mk", 256, 544), V("tt", 256, 544), OP.min, OP.max)
+            next(rest, None)
+            tt(V("qq", 0, 34), V("ss", 15, 544, 16), V("cor", 0, 34), OP.add)
+        for _ in rest:
+            pass
+        ts(V("p2"), IND(V("qq", 0, 40), LP2), CF["noff"], OP.add)
         for step in range(3):
             cp(V("oo"), IND(V("p2"), LO2))
             cp(V("hi", 0, 4), V("p2", 0, 4))
             cp(V("gm", 0, 64), IND(V("wt"), V("oo", 0, 4)), "a")
             tt(V("lof", 0, 4), V("p2", 0, 4), V("hi", 0, 4), OP.subtract)
-            tt(V("mk", 0, 64), IND(V("lof"), LB(0, 4)), V("iot32"), OP.not_equal)
+            tt(V("mk", 0, 64), IND(V("lof", 0, 16), LB(0, 4)), V("iot32"), OP.not_equal)
             tr(V("tt", 0, 64), V("gm", 0, 64))
             ts(V("cor", 0, 4), V("lof", 0, 4), 4096.0, OP.mult, -1920.0, OP.add)
             scan(V("ss", 0, 64), V("mk", 0, 64), V("tt", 0, 64), OP.mult, OP.max)
+            if t == 0:
+                unpacker(step)
             tt(V("p2" if step < 2 else "q2", 0, 4), V("ss", 15, 64, 16), V("cor", 0, 4), OP.add)
         shift_now("q2", 4)
+        if t == 0:
+            unpacker(3)
         cp(V("rb", 0, 128), IND(V("q2"), V("lst", 28, 36)), "v")
         cp(V("rb", 128, 256), IND(V("q2"), V("lst", 36, 44)), "a")
         tr(V("rf"), V("rb"))
@@ -517,41 +550,35 @@ def rank_program(g, core, T, topo):
         cp(V(hl, 16 * rank + NA, 16 * rank + 16), V("js", 255, 256 * ND, 256))
         tt(V(hl, 16 * rank, 16 * rank + NA), V("acc", 0, NA), V("acc", 1, NA + 1), OP.subtract)
         allgather(V(hl, 16 * rank, 16 * rank + 16), hl, 16, "az%d" % t)
-        if t == 0:
-            later_constants()
         fill(V("lw", 0, 96), 0.0)
         cp(V("r2"), IND(V("q2"), LR2))
         cp(V("rti", p1=1), V("rf", p1=1))
-        cp(V("r2i", 0, 16), V("r2"))
         ts(V("rta", p1=1), V("rf", p1=1), 32.0, OP.mult)
+        cp(V("r2i", 0, 16), V("r2"))
+        ts(V("rtb", p1=1), V("rti", p1=1), 16.0, OP.mult)
+        cp(V("s1"), IND(V(hl), LZ))
+        tt(V("rto", M * t, M * t + M, p1=1), V("rta", p1=1), V("rtb", p1=1), OP.subtract)
+        dma("s", T.rt[0:1, M * t:M * t + M], ap(V("rto", M * t, M * t + M, p1=1)), "dout", ins=[V("rto", M * t, M * t + M, p1=1)])
+        scan(V("sz"), V("rs8"), V("s1"), OP.mult, OP.add)
         tt(V("r2f", 0, 16), V("r2"), V("r2i", 0, 16), OP.subtract)
         ts(V("r2i", 16, 32), V("r2i", 0, 16), 15, AND)
         ts(V("r2i", 32, 48), V("r2i", 0, 16), 4, SHR)
-        ts(V("rtb", p1=1), V("rti", p1=1), 16.0, OP.mult)
-        ts(V("r2f", 16, 32), V("r2f", 0, 16), 256.0, OP.mult)
-        ts(V("r2f", 32, 48), V("r2"), 32.0, OP.mult)
-        ts(V("r2f", 48, 64), V("r2i", 0, 16), 16.0, OP.mult)
-        tt(V("rto", M * t, M * t + M, p1=1), V("rta", p1=1), V("rtb", p1=1), OP.subtract)
-        tt(V("r2f", 16, 32), V("r2f", 16, 32), V("r2i", 32, 48), OP.add)
-        tt(V("r2f", 32, 48), V("r2f", 32, 48), V("r2f", 48, 64), OP.subtract)
-        dma("s", T.rt[0:1, M * t:M * t + M], ap(V("rto", M * t, M * t + M, p1=1)), "dout", ins=[V("rto", M * t, M * t + M, p1=1)])
-        cp(V("o3"), V("r2f", 16, 32))
-        tt(V("mk3"), IND(V("r2i", 16, 32), LB(0, 16)), V("iot16"), OP.not_equal)
-        ts(V("r2f", 64, 80), V("r2i", 16, 32), 4096.0, OP.mult, -61440.0, OP.add)
-        in_range(V("r2f", 80, 96), V("r2f", 96, 112), V("r2f", 32, 48), set_c, 0)
-        ts(V("r2f", 48, 64), V("r2f", 32, 48), float(-M * rank), OP.add)
-        tt(V("r2f", 112, 128), V("r2f", 48, 64), V("mym"), OP.not_equal)
-        cp(V("s1"), IND(V(hl), LZ))
-        scan(V("sz"), V("rs8"), V("s1"), OP.mult, OP.add)
         size = V("sz", 7, 128, 8)
         cp(V("yb", 0, 256), IND(V("sz"), V("lst", 44, 60)), "a")
         cp(V("yb", 256, 512), IND(V("sz"), V("lst", 60, 76)), "v")
+        ts(V("r2f", 16, 32), V("r2f", 0, 16), 256.0, OP.mult)
+        ts(V("r2f", 32, 48), V("r2"), 32.0, OP.mult)
+        ts(V("r2f", 48, 64), V("r2i", 0, 16), 16.0, OP.mult)
         tr(V("yt"), V("yb"))
         sign(V("jy", 0, CA), V("yt", 0, CA), CF["ba"], V("cc", 0, 1))
         ts(V("jy", CA, 512), V("yt", CA, 512), CF["bd"], OP.is_ge, 2.0, OP.mult)
+        tt(V("r2f", 16, 32), V("r2f", 16, 32), V("r2i", 32, 48), OP.add)
+        tt(V("r2f", 32, 48), V("r2f", 32, 48), V("r2f", 48, 64), OP.subtract)
         red(V("cc", 1, 2), V("jy", CA, 512), OP.add)
         shift_now("cc", 2)
         red(V("cs", 0, 1), V("cc", 0, 9), OP.add)
+        ts(V("r2f", 64, 80), V("r2i", 16, 32), 4096.0, OP.mult, -61440.0, OP.add)
+        cp(V("o3"), V("r2f", 16, 32))
         ts(V("bb", 0, 32), V("c128"), V("cs", 0, 1), OP.is_le, 2.0, OP.mult)
         ts(V("bb", 32, 64), V("c128"), V("cs", 0, 1), OP.is_gt, V("cs", 0, 1), OP.mult)
         tr(V("bt"), V("bb"))
@@ -562,14 +589,17 @@ def rank_program(g, core, T, topo):
         ts(V("fl", 32, 48), size, -2.0, OP.add, V("cs", 1, 2), OP.is_lt)
         scan(V("sc"), V("rst", 0, 32), V("fl", 0, 32), OP.mult, OP.add)
         ts(V("pf", 9, 10), V("cs", 2, 3), 0.5, OP.mult)
+        tt(V("bs", 32, 48), V("fl", 32, 48), V("dum"), OP.mult)
         ts(V("bb", 0, 32), V("ones"), V("sc", 15, 16), OP.mult)
         ts(V("bb", 32, 64), V("ones"), V("sc", 31, 32), OP.mult)
-        tt(V("bs", 32, 48), V("fl", 32, 48), V("dum"), OP.mult)
-        tr(V("bt"), V("bb"))
         tt(V("bs", 0, 32), V("sc"), V("fl", 0, 32), OP.mult)
+        ts(V("bs", 32, 48), V("bs", 32, 48), 15.0, OP.add)
+        tr(V("bt"), V("bb"))
+        tt(V("bs", 48, 64), V("bs", 0, 16), V("bs", 16, 32), OP.add)
         red(V("rr", 0, 1), V("bt", 0, 32), OP.add)
         red(V("rr", 1, 2), V("bt", 32, 64), OP.add)
         tt(V("tm"), V("bt"), V("tri"), OP.mult)
+        tt(V("v3", 0, 48, 3), V("bs", 48, 64), V("bs", 32, 48), OP.add)
         cp(V("pf", 2, 4, 1, 32, 64), V("rr", 0, 2, 1, 0, 32), "a")
         cp(V("pf", 2, 4, 1, 64, 96), V("rr", 0, 2, 1, 32, 64), "a")
         cp(V("pf", 2, 4, 1, 96, 128), V("rr", 0, 2, 1, 64, 96), "a")
@@ -577,16 +607,16 @@ def rank_program(g, core, T, topo):
         cp(V("pf", 6, 8, 1, 96, 128), V("rr", 0, 2, 1, 0, 32), "v")
         red(V("pf", 0, 1), V("tm", 0, 32), OP.add)
         red(V("pf", 1, 2), V("tm", 32, 64), OP.add)
-        tt(V("bs", 48, 64), V("bs", 0, 16), V("bs", 16, 32), OP.add)
-        ts(V("bs", 32, 48), V("bs", 32, 48), 15.0, OP.add)
         red(V("rr", 2, 3), V("pf", 0, 10, 2), OP.add)
         red(V("rr", 3, 4), V("pf", 1, 10, 2), OP.add)
-        tt(V("v3", 0, 48, 3), V("bs", 48, 64), V("bs", 32, 48), OP.add)
         ts(V("v3", 1, 48, 3), V("fl", 0, 16), V("rr", 2, 3), OP.mult)
         ts(V("v3", 2, 48, 3), V("fl", 16, 32), V("rr", 3, 4), OP.mult)
         scan(V("v3s"), V("rs3"), V("v3"), OP.mult, OP.add)
         cp(V("vo"), V("v3s", 2, 48, 3))
+        ts(V("q", 0, 16), V("v3s", 2, 48, 3), CF["o4096"], OP.add)
         emit("v", lambda: g.vector.tensor_copy(ap(IND(V("lw"), V("vo"))), ap(V("sv"))), [V("lw")], [V("sv"), V("vo")])
+        if t == 0:
+            quant(V("qe"), V("se"), V("et"))
         tr(V("lt", 0, 64), V("lw", 16, 80))
         tr(V("lt", 64, 160), V("lw", 0, 96))
         cp(V("zz", 0, 40, 4), V("lt", 0, 160, 16))
@@ -594,48 +624,57 @@ def rank_program(g, core, T, topo):
         scan(V("zs"), V("rs8", 0, 40), V("zz"), OP.mult, OP.add)
         ts(V("pl", 0, 16), IND(V("zs"), LCH), float(-1 - M * rank), OP.add, float(M - 1), OP.min)
         ca, pa, cb, pb, cc_, pc_ = ["%s%s%d" % (x, s_, t) for s_ in "abc" for x in "cp"]
+        cp(V("ch"), IND(V("zs"), LCH))
         pick(V(ca, 0, K), V(pa, 0, K), V(ct, 0, M), V(pt, 0, M), V("pl", 0, 4))
         swap(peer_a, ca, pa, "aa%d" % t)
-        cp(V("ch"), IND(V("zs"), LCH))
-        ts(V("q", 0, 16), V("v3s", 2, 48, 3), CF["o4096"], OP.add)
-        in_range(V("cht", 0, 4), V("cht", 4, 8), V("ch", 0, 4), set_a, 1)
-        in_range(V("cht", 8, 12), V("cht", 12, 16), V("ch", 0, 4), set_b, 1)
+        for b in range(4):
+            mm(V("psd", 512 * b, 512 * b + M), V("qe", 128 * b, 128 * b + 128), V("se", 128 * b, 128 * b + 128), V(ct, 0, M), V(pt, 0, M), True, False)
+        ts(V("cht", 0, 4), V("ch", 0, 4), float(M * set_a[0] + 1), OP.is_ge, float(K), OP.mult)
+        ts(V("cht", 4, 8), V("ch", 0, 4), float(M * (set_a[-1] + 1) + 1), OP.is_lt)
+        ts(V("cht", 8, 12), V("ch", 0, 4), float(M * set_b[0] + 1), OP.is_ge, float(K), OP.mult)
+        ts(V("cht", 12, 16), V("ch", 0, 4), float(M * (set_b[-1] + 1) + 1), OP.is_lt)
+        shift_now("q", 16)
+        tt(V("cht", 0, 4), V("cht", 0, 4), V("cht", 4, 8), OP.mult)
+        tt(V("cht", 8, 12), V("cht", 8, 12), V("cht", 12, 16), OP.mult)
+        tt(V("mk3"), IND(V("r2i", 16, 32), LB(0, 16)), V("iot16"), OP.not_equal)
         tt(V("cht", 0, 4), V("cht", 0, 4), V("dum", 0, 4), OP.add)
         tt(V("cht", 8, 12), V("cht", 8, 12), V("dum", 0, 4), OP.add)
+        tr(V("xx", 16, 80), V("q", 0, 64))
+        ts(V("r2f", 48, 64), V("r2f", 32, 48), float(-M * rank), OP.add)
         ts(V("pl", 16, 20), V("cht", 0, 4), float(-DUMMY), OP.add)
         ts(V("pl", 20, 24), V("cht", 8, 12), float(-DUMMY), OP.add)
-        shift_now("q", 16)
+        tr(V("q", 64, 160), V("xx"))
         pick(V(cb, 0, K), V(pb, 0, K), V(ca), V(pa), V("pl", 16, 20))
         swap(peer_b, cb, pb, "ab%d" % t)
-        cross("q")
         cp(V("wt"), IND(V("q"), LW), "a")
+        tt(V("r2f", 112, 128), V("r2f", 48, 64), V("mym"), OP.not_equal)
+        in_range(V("r2f", 80, 96), V("r2f", 96, 112), V("r2f", 32, 48), set_c, 0)
         cp(V("gm", 0, 128), IND(V("wt"), V("o3", 0, 8)), "a")
         cp(V("gm", 128, 256), IND(V("wt"), V("o3", 8, 16)), "v")
         tr(V("tt", 0, 256), V("gm", 0, 256))
-        scan(V("ss", 0, 256), V("mk3"), V("tt", 0, 256), OP.mult, OP.max)
         pick(V(cc_, 0, K), V(pc_, 0, K), V(cb), V(pb), V("pl", 20, 24))
         swap(peer_c, cc_, pc_, "ac%d" % t)
+        scan(V("ss", 0, 256), V("mk3"), V("tt", 0, 256), OP.mult, OP.max)
+        if t + 1 < R:
+            products(t, 0)
         tt(V("cht", 16, 32), V("ss", 15, 256, 16), V("r2f", 64, 80), OP.add)
         ts(V("cht", 32, 48), V("cht", 16, 32), -16.0, OP.add, float(K - 1), OP.min)
         ts(V("cht", 48, 64), V("cht", 16, 32), 79.5, OP.is_lt, float(M), OP.mult)
         tt(V("cht", 32, 48), V("cht", 32, 48), V("r2f", 80, 96), OP.add)
         tt(V("cht", 48, 64), V("cht", 48, 64), V("r2f", 112, 128), OP.mult)
         cp(V("pl", 32, 48), IND(V("cht", 32, 48), LA))
-        if t + 1 < R:
-            ts(V("ff"), IND(V("cht", 48, 64), LH), 1.0 / M, OP.mult)
-            products(t, 0)
-            ts(V("nf", 0, 2), V("ff", 0, 2), -1.0, OP.mult, 1.0, OP.add)
-            tt(V("ho", 0, 2), V("psh", t + 1, 1024, 512), V("nf", 0, 2), OP.mult)
-        tt(V("cht", 48, 64), V("cht", 48, 64), V("mym"), OP.add)
-        cp(V("pl", 48, 64), IND(V("cht", 48, 64), LA))
-        for b in range(4):
-            if t == 0 and b == 0:
-                unpackers()
-            mm(V("psd", 512 * b, 512 * b + M), V("qe", 128 * b, 128 * b + 128), V("se", 128 * b, 128 * b + 128), V(ct, 0, M), V(pt, 0, M), True, False)
         cr, pr = "cr%d" % t, "pr%d" % t
         pick(V(cr), V(pr), V(cc_), V(pc_), V("pl", 32, 48))
         for b in range(4):
             mm(V("psd", 512 * b, 512 * b + M), V("qe", 128 * b, 128 * b + 128), V("se", 128 * b, 128 * b + 128), V(cr), V(pr), False, True)
+        if t + 1 < R:
+            ts(V("ff"), IND(V("cht", 48, 64), LH), 1.0 / M, OP.mult)
+        tt(V("cht", 0, 16), V("cht", 48, 64), V("mym"), OP.add)
+        if t + 1 < R:
+            ts(V("nf", 0, 2), V("ff", 0, 2), -1.0, OP.mult, 1.0, OP.add)
+        cp(V("pl", 48, 64), IND(V("cht", 0, 16), LA))
+        if t + 1 < R:
+            tt(V("ho", 0, 2), V("psh", t + 1, 1024, 512), V("nf", 0, 2), OP.mult)
         for b in range(4):
             o, i_ = V("ht", b, 1024, 4), V("psd", 512 * b, 512 * b + M)
             if b % 2:

@@ -3,11 +3,17 @@ from concourse.mybir import dt, AluOpType, AxisListType, ActivationFunctionType
 
 N, M, K, J, R = 8, 256, 64, 3, 3
 F32, I32, U16, BF, CODE, PLANE = "float32", "int32", "uint16", "bfloat16", "float8_e4m3fn_x4", "uint8"
-NA = 8
+NA = 7
 ND = 16 - NA
-CA = 384
-GA = 128
+NS = 7
+NC = 3
 DUMMY = 2200
+BIG = 2.0 ** 90
+ROUND32 = 1.5 * 2.0 ** 28
+MKW = 4128
+HOP, FAR, LOCAL, CYCLE = 0.235, 1.4, 1.3, 0.00083
+PIECES_R = ((0, 128, "v"), (128, 256, "a"))
+PIECES_W = ((0, 128, "v"), (128, 256, "v"))
 
 SCRATCH = {}
 
@@ -19,33 +25,36 @@ def _sb(name, n, d):
 for _n, _w, _d in [
     ("xs", 1024, BF), ("us", 512, BF), ("ws", 512, BF), ("nbs", 48, I32), ("nbo", 16, U16), ("nbl", 48, U16),
     ("qu", 128, CODE), ("su", 128, PLANE), ("qw", 128, CODE), ("sw", 128, PLANE),
-    ("et", 2048, BF), ("qe", 512, CODE), ("se", 512, PLANE), ("io512", 512, F32),
-    ("ci", 32, I32), ("cf", 32, F32), ("jr", 48, I32), ("tmpi", 128, I32), ("lst", 160, U16),
-    ("iot16", 256, F32), ("iot32", 64, F32), ("rst", 256, F32), ("rs8", 128, F32), ("sv", 256, F32), ("tri", 64, F32), ("kk", 64, F32),
-    ("nbi", 48, I32), ("nhi", 48, I32), ("nlo", 48, I32), ("qn", 160, F32), ("on", 48, U16), ("mt", 768, F32), ("mf", 768, F32),
-    ("hs", 12, F32), ("q", 160, F32), ("xx", 96, F32), ("wt", 128, F32), ("oo", 16, U16), ("d1", 544, BF), ("qq", 160, F32), ("gp", 288, F32),
-    ("gm", 768, F32), ("tt", 768, F32), ("ss", 768, F32), ("mk", 544, BF), ("hi", 40, I32), ("lof", 40, F32),
-    ("sm", 160, F32), ("p2", 16, F32), ("q2", 16, F32), ("rb", 256, F32), ("rf", 256, F32),
-    ("ja", 256 * (NA + 1), BF), ("acc", 24, F32),
-    ("rti", 256, I32), ("rta", 256, F32), ("rtb", 256, F32), ("rto", 768, F32),
-    ("r2", 16, F32), ("r2i", 48, I32), ("r2f", 128, F32), ("o3", 16, U16), ("mk3", 256, F32),
-    ("s1", 128, F32), ("sz", 128, F32), ("yb", 512, BF), ("yt", 512, BF), ("jy", 512, BF), ("cc", 16, F32),
-    ("bb", 64, F32), ("bt", 64, F32), ("fl", 48, F32), ("sc", 32, F32), ("tm", 64, F32), ("pf", 16, F32),
-    ("bs", 64, F32), ("vo", 16, U16), ("lw", 2480, F32), ("lt", 160, F32), ("zz", 40, F32),
-    ("cht", 64, F32), ("pl", 80, U16), ("ht", 1024, BF), ("yo", 256, F32),
+    ("et", 2048, BF), ("qe", 512, CODE), ("se", 512, PLANE), ("io128", 128, F32),
+    ("ci", 32, I32), ("cf", 32, F32), ("jr", 48, I32), ("tmpi", 160, I32), ("lst", 32, U16),
+    ("mk", MKW, BF), ("eqm", 16, BF), ("mt3", 768, BF), ("rs48", 192, BF), ("rst", 512, BF), ("sv", 256, F32),
+    ("qn", 224, F32), ("xx", 128, F32), ("on", 48, U16), ("ok", 48, U16),
+    ("hs", 12, F32), ("tbh", 224, F32), ("tbp", 224, F32), ("tbs", 224, F32), ("gn", 768, F32), ("tn", 768, F32), ("sn", 768, F32),
+    ("gm", 512, F32), ("tt", 512, F32), ("sp", 544, F32), ("mg", 512, BF), ("mt", 512, BF), ("oo", 32, U16), ("o2", 32, U16),
+    ("o3", 16, U16), ("o4", 16, U16), ("ow", 16, U16), ("yb", 64, F32), ("rf", 256, F32), ("rt2", 256, F32), ("mgs", 256, BF),
+    ("gs", 256, F32), ("tts", 256, F32), ("sps", 256, F32),
+    ("ja", 256 * (NA + 1), BF), ("acc", 24, F32), ("qi", 64, I32), ("nn", 32, F32), ("nt", 32 * R, F32),
+    ("s1", 128, F32), ("sz", 128, F32), ("th0", 512, BF), ("th1", 512, BF), ("ctb", 224, BF), ("pf2", 224, F32),
+    ("vo", 16, U16), ("lw", 2480, F32), ("lt", 160, F32),
+    ("zo", 16, F32), ("zz", 40, F32), ("zs", 48, F32), ("pl", 80, U16), ("ht", 1024, BF), ("yo", 256, F32),
 ]:
     _sb(_n, _w, _d)
 ALIAS = {}
-for _b, _d, _names in (("kc", F32, [("thx", 16), ("th", 16), ("c128", 32), ("ones", 32), ("mym", 16), ("dum", 16), ("rs3", 48)]),
-                       ("wk", F32, [("cor", 40), ("cs", 8), ("rr", 8), ("ch", 16), ("v3", 48), ("v3s", 48), ("ff", 16), ("nf", 4), ("ho", 4), ("zs", 40)]),
-                       ("wb", BF, [("zb", 256), ("ob", 256), ("rsb", 768), ("jd", 256 * ND), ("js", 256 * ND)])):
+for _b, _d, _names in (
+        ("kc", F32, [("th", 16), ("c128", 32), ("cn", 32), ("mym", 16), ("dum", 16), ("rs8", 128), ("odd", 32), ("nodd", 32), ("zero", 16),
+                     ("my8", 16), ("sv3", 48), ("sn3", 48), ("bm", 48), ("h1", 112)]),
+        ("wk", F32, [("so", 48), ("so2", 48), ("cs", 16), ("ch", 16), ("ff", 16), ("nf", 16), ("ho", 16),
+                     ("dd", 32), ("ds", 32), ("hm", 48), ("mx", 16), ("h0", 112), ("hz", 128), ("w1", 32), ("w2", 32), ("cv", 16),
+                     ("gw", 64), ("tw", 64), ("szh", 16), ("bb", 64), ("bt", 80), ("pfb", 48), ("df", 48), ("se0", 48), ("se1", 32),
+                     ("fl", 32), ("k0", 64), ("k1", 64), ("k2", 64), ("tv", 64), ("qf", 96), ("cht", 64)]),
+        ("wb", BF, [("zb", 256), ("ob", 256), ("mw", 64), ("nw", 64), ("jd", 256 * ND), ("js", 256 * ND)])):
     _o = 0
     for _n, _w in _names:
         ALIAS[_n] = (_b, _o, _w)
         _o += _w
     _sb(_b, _o, _d)
 for _t in range(R):
-    _sb("qh%d" % _t, 160, F32)
+    _sb("qh%d" % _t, 32, F32)
     _sb("hl%d" % _t, 128, BF)
     for _s in "abc":
         _sb("c%s%d" % (_s, _t), 128, CODE)
@@ -76,12 +85,16 @@ def rank_program(g, core, T, topo):
     count = {s: 0 for s in SEMAPHORES}
     known = {q: {} for q in queues}
     hist = {}
+    ops = []
 
     def V(name, c0=0, c1=None, s=1, p0=0, p1=128):
         if name in ALIAS:
             b, o, w = ALIAS[name]
             return (b, o + c0, o + (w if c1 is None else c1), s, p0, p1)
         return (name, c0, SCRATCH[name][1][1] if c1 is None else c1, s, p0, p1)
+
+    def on(x, p0, p1):
+        return x[:4] + (p0, p1)
 
     def IND(win, off):
         return ("*", win, off)
@@ -106,86 +119,161 @@ def rank_program(g, core, T, topo):
             return False
         return not (a[3] > 1 and a[3] == b[3] and (a[1] - b[1]) % a[3] != 0)
 
+    def covers(a, b):
+        return a[1] <= b[1] and b[2] <= a[2] and a[4] <= b[4] and b[5] <= a[5] and (a[3] == 1 or (a[3] == b[3] and (a[1] - b[1]) % a[3] == 0))
+
+    def size(x):
+        return 16 * size(x[2]) if x[0] == "*" else (x[2] - x[1] + x[3] - 1) // x[3]
+
+    def narrow(*xs):
+        return all(SCRATCH[x[0]][2] in (BF, U16) for x in xs)
+
+    def add(q, call, outs, ins, cost, lat=HOP, sem=None, chain=False):
+        outs, ins = flat(outs), flat(ins)
+        pre = set()
+        for regs, wr in ((ins, False), (outs, True)):
+            for x in regs:
+                for (y, yw, k) in hist.get(x[0], ()):
+                    if (wr or yw) and meet(x, y):
+                        pre.add(k)
+        k = len(ops)
+        for x in outs:
+            hist[x[0]] = [e for e in hist.get(x[0], ()) if not covers(x, e[0])]
+        for regs, wr in ((ins, False), (outs, True)):
+            for x in regs:
+                hist.setdefault(x[0], []).append((x, wr, k))
+        ops.append({"q": q, "call": call, "pre": sorted(pre), "cost": cost, "lat": lat, "sem": sem, "chain": chain})
+
+    def vcost(out, x, *more, k=1):
+        if x[0] == "*":
+            return 0.05 + 1.56 * CYCLE * size(x)
+        return CYCLE * max(64, k * size(x) * (0.5 if k == 1 and narrow(out, x, *more) else 1))
+
+    def acost(x):
+        return 0.065 + 1.56 * CYCLE * size(x) if x[0] == "*" else 0.03 + CYCLE * size(x)
+
     def wait(q, sem, val):
         if known[q].get(sem, 0) < val:
             queues[q].wait_ge(T.sem[sem], val)
             known[q][sem] = val
 
-    def order(q, outs, ins, skip=None):
-        need = {}
-        for regs, wr in ((ins, False), (outs, True)):
-            for x in regs:
-                for (y, yw, sem), val in hist.get(x[0], {}).items():
-                    if (wr or yw) and sem != skip and meet(x, y):
-                        need[sem] = max(need.get(sem, 0), val)
-        for sem, val in need.items():
-            wait(q, sem, val)
+    def issue():
+        n = len(ops)
+        post = [[] for _ in range(n)]
+        for k, o in enumerate(ops):
+            for j in o["pre"]:
+                post[j].append(k)
 
-    def note(outs, ins, sem, val):
-        for regs, wr in ((ins, False), (outs, True)):
-            for x in regs:
-                hist.setdefault(x[0], {})[(x, wr, sem)] = val
-
-    def emit(q, call, outs, ins, skip=None):
-        outs, ins = flat(outs), flat(ins)
-        order(q, outs, ins, skip)
-        sem = own_sem[q]
-        call().then_inc(T.sem[sem], 1)
-        count[sem] += 1
-        note(outs, ins, sem, count[sem])
+        def gap(j, k):
+            return 0.0 if ops[k]["chain"] and ops[j]["q"] == "t" else ops[j]["lat"]
+        left = [0.0] * n
+        for k in range(n - 1, -1, -1):
+            left[k] = ops[k]["cost"] + max([gap(k, j) + left[j] for j in post[k]] + [ops[k]["lat"]])
+        need = [len(o["pre"]) for o in ops]
+        ready = [0.0] * n
+        cand = {q: [] for q in queues}
+        free = {q: 0.0 for q in queues}
+        for k in range(n):
+            if not need[k]:
+                cand[ops[k]["q"]].append(k)
+        done = []
+        while len(done) < n:
+            best = None
+            for q, cs_ in cand.items():
+                if not cs_:
+                    continue
+                top = max(cs_, key=lambda k: (left[k], -k))
+                at = max(free[q], ready[top])
+                fit = [k for k in cs_ if max(free[q], ready[k]) + ops[k]["cost"] <= at + 0.01]
+                k = min(fit, key=lambda k: (max(free[q], ready[k]), -left[k], k)) if fit else top
+                at = max(free[q], ready[k])
+                if best is None or at < best[0]:
+                    best = (at, k)
+            at, k = best
+            o = ops[k]
+            cand[o["q"]].remove(k)
+            free[o["q"]] = at + o["cost"]
+            done.append(k)
+            for j in post[k]:
+                ready[j] = max(ready[j], at + o["cost"] + gap(k, j))
+                need[j] -= 1
+                if not need[j]:
+                    cand[ops[j]["q"]].append(j)
+        sig = {}
+        for k in done:
+            o = ops[k]
+            want = {}
+            for j in o["pre"]:
+                if not (o["chain"] and ops[j]["q"] == "t"):
+                    s_, v_ = sig[j]
+                    want[s_] = max(want.get(s_, 0), v_)
+            for s_, v_ in want.items():
+                wait(o["q"], s_, v_)
+            if o["sem"] is None:
+                s_ = own_sem[o["q"]]
+                o["call"]().then_inc(T.sem[s_], 1)
+                count[s_] += 1
+                sig[k] = (s_, count[s_])
+            else:
+                sig[k] = o["call"]()
 
     def cp(out, in_, q="v"):
         if q == "v":
-            emit("v", lambda: g.vector.tensor_copy(ap(out), ap(in_)), [out], [in_])
+            add("v", lambda: g.vector.tensor_copy(ap(out), ap(in_)), [out], [in_], vcost(out, in_))
         else:
-            emit("a", lambda: g.scalar.activation(ap(out), ap(in_), ACT.Copy), [out], [in_])
+            add("a", lambda: g.scalar.activation(ap(out), ap(in_), ACT.Copy), [out], [in_], acost(in_))
+
+    def scale(out, in_, s):
+        add("a", lambda: g.scalar.activation(ap(out), ap(in_), ACT.Copy, scale=ap(s)), [out], [in_, s], acost(in_))
 
     def tt(out, a, b, op):
-        emit("v", lambda: g.vector.tensor_tensor(ap(out), ap(a), ap(b), op), [out], [a, b])
+        add("v", lambda: g.vector.tensor_tensor(ap(out), ap(a), ap(b), op), [out], [a, b], vcost(out, a, k=2))
 
     def ts(out, a, s1, op0, s2=None, op1=None):
         if op1 is None:
-            emit("v", lambda: g.vector.tensor_scalar(ap(out), ap(a), ap(s1), None, op0), [out], [a, s1])
+            add("v", lambda: g.vector.tensor_scalar(ap(out), ap(a), ap(s1), None, op0), [out], [a, s1], vcost(out, a))
         else:
-            emit("v", lambda: g.vector.tensor_scalar(ap(out), ap(a), ap(s1), ap(s2), op0, op1), [out], [a, s1, s2])
+            add("v", lambda: g.vector.tensor_scalar(ap(out), ap(a), ap(s1), ap(s2), op0, op1), [out], [a, s1, s2], vcost(out, a))
 
     def red(out, a, op):
-        emit("v", lambda: g.vector.tensor_reduce(ap(out), ap(a), AxisListType.X, op), [out], [a])
+        add("v", lambda: g.vector.tensor_reduce(ap(out), ap(a), AxisListType.X, op), [out], [a], vcost(out, a))
 
-    def scan(out, d0, d1, op0, op1):
-        emit("v", lambda: g.vector.tensor_tensor_scan(ap(out), ap(d0), ap(d1), 0.0, op0, op1), [out], [d0, d1])
+    def scan(out, d0, d1, op0, op1, first=0.0):
+        add("v", lambda: g.vector.tensor_tensor_scan(ap(out), ap(d0), ap(d1), ap(first), op0, op1), [out], [d0, d1, first], vcost(out, d0, d1))
 
     def tr(out, a):
-        emit("v", lambda: g.vector.transpose(ap(out), ap(a)), [out], [a])
+        add("v", lambda: g.vector.transpose(ap(out), ap(a)), [out], [a], vcost(out, a))
 
     def fill(out, c):
-        emit("v", lambda: g.vector.memset(ap(out), c), [out], [])
+        add("v", lambda: g.vector.memset(ap(out), c), [out], [], vcost(out, out))
 
-    def sign(out, a, bias, accum):
-        emit("a", lambda: g.scalar.activation(ap(out), ap(a), ACT.Sign, bias=ap(bias), accum_out=ap(accum)), [out, accum], [a, bias])
+    def sign(out, a, bias, accum=None):
+        add("a", lambda: g.scalar.activation(ap(out), ap(a), ACT.Sign, bias=ap(bias), accum_out=ap(accum)), [out, accum], [a, bias], acost(a) + 0.02)
 
     def iota(out, pattern, base, mult):
         if SCRATCH[out[0]][2] == I32:
-            emit("g", lambda: g.iota(ap(out), pattern, base, mult), [out], [])
+            add("g", lambda: g.iota(ap(out), pattern, base, mult), [out], [], 0.13 + 2 * CYCLE * size(out))
         else:
-            emit("g", lambda: g.iota(ap(out), pattern, base, mult, allow_small_or_imprecise_dtypes=True), [out], [])
+            add("g", lambda: g.iota(ap(out), pattern, base, mult, allow_small_or_imprecise_dtypes=True), [out], [], 0.13 + 2 * CYCLE * size(out))
 
     def quant(c, s, a):
-        emit("v", lambda: g.vector.quantize_mx(ap(c), ap(s), ap(a)), [c, s], [a])
+        add("v", lambda: g.vector.quantize_mx(ap(c), ap(s), ap(a)), [c, s], [a], 0.012 + 0.00022 * size(a))
 
     def mm(out, lc, ls_, rc, rs, start, stop):
-        emit("t", lambda: g.tensor.matmul_mx(ap(out), ap(lc), ap(ls_), ap(rc), ap(rs), start, stop), [out], [lc, ls_, rc, rs],
-             skip=None if start else "kt")
+        add("t", lambda: g.tensor.matmul_mx(ap(out), ap(lc), ap(ls_), ap(rc), ap(rs), start, stop), [out], [lc, ls_, rc, rs],
+            0.0006 * (size(rc) + 16), chain=not start)
 
     def pick(oc_, op_, wc, wp, off):
-        emit("v", lambda: g.vector.tensor_copy(ap(oc_).bitcast(dt.uint32), ap(wc).bitcast(dt.uint32).indirect(ap(off))), [oc_], [wc, off])
+        add("v", lambda: g.vector.tensor_copy(ap(oc_).bitcast(dt.uint32), ap(wc).bitcast(dt.uint32).indirect(ap(off))), [oc_], [wc, off],
+            vcost(oc_, IND(wc, off)))
         cp(op_, IND(wp, off), "a")
 
-    def dma(q, out, in_, sem, outs=(), ins=(), total=None):
-        order(q, [], list(ins))
-        queues[q].dma_start(out, in_).then_inc(T.sem[sem], 16)
-        count[sem] += 16
-        note(list(outs), [], sem, total or count[sem])
+    def dma(q, out, in_, sem, outs=(), ins=(), total=None, lat=LOCAL):
+        def call():
+            queues[q].dma_start(out, in_).then_inc(T.sem[sem], 16)
+            count[sem] += 16
+            return sem, total or count[sem]
+        add(q, call, list(outs), list(ins), 0.05, lat, sem)
 
     def bits(m):
         return bin(m).count("1")
@@ -205,30 +293,32 @@ def rank_program(g, core, T, topo):
         mn = topo.mask(src, near[0]) & ~mf_
         return near, far, mn, mf_
 
-    def allgather(src, buf, w, sem):
-        near, far, mn, mf_ = split(core)
-        land = ap(V(buf, w * rank, w * rank + w))
-        order("g", [], [src])
-        g.remote_dma_fused([RemoteDMATransfer(dst_ids=[dst(c) for c in cs_], dma_engine_mask=m, remote_sem=T.sem[sem],
-                                              srcs=[ap(src)], dsts=[land for _ in cs_]) for cs_, m in ((far, mf_), (near, mn))],
-                           local_sem=T.sem.ls)
-        count["ls"] += bits(mf_) + bits(mn)
-        for c in cores:
-            if c != core:
-                n2, f2, mn2, mf2 = split(c)
-                count[sem] += bits(mn2) if core in n2 else bits(mf2)
-        note([V(buf, 0, w * N)], [], sem, count[sem])
+    def allgather(src, buf, w, sem, lat=FAR):
+        def call():
+            near, far, mn, mf_ = split(core)
+            land = ap(V(buf, w * rank, w * rank + w))
+            g.remote_dma_fused([RemoteDMATransfer(dst_ids=[dst(c) for c in cs_], dma_engine_mask=m, remote_sem=T.sem[sem],
+                                                  srcs=[ap(src)], dsts=[land for _ in cs_]) for cs_, m in ((far, mf_), (near, mn))],
+                               local_sem=T.sem.ls)
+            count["ls"] += bits(mf_) + bits(mn)
+            for c in cores:
+                if c != core:
+                    n2, f2, mn2, mf2 = split(c)
+                    count[sem] += bits(mn2) if core in n2 else bits(mf2)
+            return sem, count[sem]
+        others = [V(buf, a, b) for a, b in ((0, w * rank), (w * rank + w, w * N)) if a < b]
+        add("g", call, others, [src], 0.1, lat, sem)
 
     def swap(peer, cb, pb, sem):
-        rid, pid, _ = topo.addr(peer)
-        m = topo.mask(core, peer)
-        order("g", [], [V(cb, 0, K)])
-        g.remote_dma(ap(V(cb, K, 2 * K)).bitcast(dt.uint8), ap(V(cb, 0, K)).bitcast(dt.uint8), T.sem[sem], T.sem.ls, pid, rid, m)
-        order("g", [], [V(pb, 0, K)])
-        g.remote_dma(ap(V(pb, K, 2 * K)), ap(V(pb, 0, K)), T.sem[sem], T.sem.ls, pid, rid, m)
-        count["ls"] += 2 * bits(m)
-        count[sem] += 2 * bits(topo.mask(peer, core))
-        note([V(cb, K, 2 * K), V(pb, K, 2 * K)], [], sem, count[sem])
+        def call():
+            rid, pid, _ = topo.addr(peer)
+            m = topo.mask(core, peer)
+            g.remote_dma(ap(V(cb, K, 2 * K)).bitcast(dt.uint8), ap(V(cb, 0, K)).bitcast(dt.uint8), T.sem[sem], T.sem.ls, pid, rid, m)
+            g.remote_dma(ap(V(pb, K, 2 * K)), ap(V(pb, 0, K)), T.sem[sem], T.sem.ls, pid, rid, m)
+            count["ls"] += 2 * bits(m)
+            count[sem] += 2 * bits(topo.mask(peer, core))
+            return sem, count[sem]
+        add("g", call, [V(cb, K, 2 * K), V(pb, K, 2 * K)], [V(cb, 0, K), V(pb, 0, K)], 0.2, FAR, sem)
 
     me = topo.chip(core)
     peer_a = [c for c in cores if c != core and topo.chip(c) == me][0]
@@ -248,78 +338,159 @@ def rank_program(g, core, T, topo):
                 b = (a + m) % 4
                 cp(dst_(m, 32 * b, 32 * b + 32), src(32 * a, 32 * a + 32), "a" if a % 2 else "v")
 
-    def shift_now(buf, w, n=None):
-        shift_at_once(lambda m, a, b: V(buf, m * w, m * w + (n or w), 1, a, b), lambda a, b: V(buf, 0, n or w, 1, a, b))
+    def turn(place, src, nc):
+        tr(place(0, 0), src)
+        pairs = [(a, b) for a in range(4) for b in range(4) if (a - b) % 2]
+        for a, b in pairs[:nc]:
+            cp(on(place(a, b), 32 * b, 32 * b + 32), on(place(0, 0), 32 * a, 32 * a + 32), "a")
+        tr(on(place(0, 2), 64, 128), on(src, 0, 64))
+        tr(on(place(2, 0), 0, 64), on(src, 64, 128))
+        for a, b in pairs[nc:]:
+            tr(on(place(a, b), 32 * b, 32 * b + 32), on(src, 32 * a, 32 * a + 32))
 
-    def cross(buf):
-        tr(V("xx", 16, 80), V(buf, 0, 64))
-        tr(V(buf, 64, 160), V("xx"))
+    def table(tb, src):
+        turn(lambda a, b: V(tb, 96 + 32 * (a - b), 128 + 32 * (a - b)), src, NC)
 
     dma("a", T.nbs[0:16, :], T.nb[:], "dn", [V("nbs", p1=16)], total=32)
     dma("a", T.nbs[16:32, :], T.nb[:], "dn", [V("nbs", p0=16, p1=32)], total=32)
-    dma("s", T.xs[:], T.x[:], "dx", [V("xs")])
-    dma("s", T.us[:], T.u[:], "du", [V("us")])
-    dma("s", T.ws[:], T.w[:], "dw", [V("ws")])
+    dma("s", T.xs[:], T.x[:], "dx", [V("xs")], lat=2.0)
+    dma("s", T.us[:], T.u[:], "du", [V("us")], lat=1.9)
 
     CI = {n: V("ci", k, k + 1) for k, n in enumerate(
-        ["p", "i", "g", "hs", "as", "i0", "i1", "i12", "i3", "i123", "q", "ne", "hoff", "nh", "d", "t0", "t1", "t2", "t3", "t4", "t5", "t6",
-         "r0", "r1", "r2", "r3", "r4", "r5"])}
+        ["p", "i", "g", "h", "lo", "hi", "r", "e", "i1", "i2", "i3", "ne", "u3", "t0", "t1", "t2", "t3", "t5", "t7", "t8", "t9",
+         "s0", "s1", "s2", "s3", "s4", "s5"])}
     CF = {n: V("cf", k, k + 1) for k, n in enumerate(
-        ["p", "i", "g", "hs", "as", "q", "m128i", "noff", "top", "o4096", "sW", "sO", "p4", "ba", "bd", "g256", "k0", "sZ", "sW2"])}
-    LNB, LW, LO, LP2, LO2, LR2, LA, LCH = V("lst", 0, 1), V("lst", 2, 10), V("lst", 10, 13), V("lst", 14, 15), V("lst", 16, 17), V("lst", 18, 19), V("lst", 20, 21), V("lst", 22, 23)
-    LI, LF, LB2 = V("lst", 24, 27), V("lst", 28, 44), V("lst", 44, 76)
-    LH, LZ = V("lst", 128, 129), V("lst", 130, 138)
-    LW2, LQ, LS = V("lst", 138, 146), V("lst", 146, 147), V("lst", 148, 151)
-
-    def LB(a, b):
-        return V("lst", 80 + a, 80 + b)
-
+        ["p", "i", "g", "h", "lo", "hi", "r", "coff", "base", "sO", "g256", "sZ", "cC", "t0", "t1"])}
+    LNB, LO, LK, L3, LZ, LQ, LCH, LF, LH = [V("lst", a, b) for a, b in (
+        (0, 1), (2, 5), (6, 9), (10, 13), (14, 22), (22, 23), (24, 25), (26, 27), (28, 29))]
     AND, SHR = OP.bitwise_and, OP.logical_shift_right
+    io32 = V("io128", 0, 32)
     iota(CI["p"], [[0, 1]], 0, 1)
     iota(V("jr"), [[1, 48]], 0, 0)
-    iota(V("iot16"), [[0, 16], [1, 16]], 0, 0)
-    iota(V("thx"), [[2, 16]], 0, 64)
-    iota(V("tri"), [[0, 2], [1, 32]], 0, 0)
+    iota(V("io128"), [[1, 128]], 0, 0)
+    iota(V("sv3"), [[1, 16], [0, 3]], 0, 0)
+    iota(V("sv", 0, 128), [[1, 8], [16, 16]], 1, 0)
     P = CI["p"]
     ts(CI["i"], P, 15, AND)
     ts(CI["g"], P, 4, SHR)
-    ts(CI["hs"], P, 4, SHR, 1, AND)
-    ts(CI["as"], P, 5, SHR)
-    ts(CI["i0"], P, 1, AND)
-    ts(CI["t0"], CI["i"], 5.0, OP.min, 8.0, OP.mult)
+    ts(CI["h"], P, 4, SHR, 1, AND)
+    ts(CI["lo"], P, 5, SHR, 1, AND)
+    ts(CI["hi"], P, 6, SHR)
+    ts(CI["r"], P, 31, AND)
+    ts(CI["t0"], CI["i"], 5.0, OP.min, 16.0, OP.mult)
+    ts(CI["u3"], CI["i"], 3.0, OP.is_ge, -40.0, OP.mult)
+    cp(V("cf", 0, 7), V("ci", 0, 7))
+    ts(CI["e"], P, 1, AND)
+    tt(CI["t1"], CI["t0"], CI["u3"], OP.add)
+    ts(V("mk", 0, 31), V("io128", 0, 31), CF["i"], OP.is_lt)
+    ts(V("eqm"), V("io128", 0, 16), CF["i"], OP.not_equal, -BIG, OP.mult)
+    ts(LNB, CI["t1"], CF["g"], OP.add)
+    fill(V("mk", 31, 32), 1.0)
+    for b_ in ("xx", "tbh", "tbp", "tbs", "ctb", "h0", "hz", "tv", "nn", "zo", "zero", "k0"):
+        fill(V(b_), 0.0)
+    for c_ in (271, 543):
+        fill(V("sp", c_, c_ + 1), 0.0)
+    w_ = 32
+    while w_ < MKW:
+        n_ = min(w_, MKW - w_, 256)
+        cp(V("mk", w_, w_ + n_), V("mk", 0, n_), "a")
+        w_ += n_
+    ts(CF["t0"], CI["hi"], -64.0, OP.mult, 96.0, OP.add)
+    tt(CI["ne"], CI["e"], CI["h"], OP.not_equal)
+    ts(CI["t2"], CI["h"], -32.0, OP.mult, 128.0, OP.add)
+    tt(CI["t3"], CI["i"], CI["e"], OP.subtract)
+    ts(CF["coff"], CI["lo"], -32.0, OP.mult, CF["t0"], OP.add)
+    tt(CI["t2"], CI["t2"], CI["ne"], OP.mult)
+    tt(CI["t3"], CI["t3"], CI["h"], OP.add)
+    tt(CF["sO"], CI["t2"], CI["t3"], OP.add)
+    ts(LO, V("jr", 0, 3), 16.0, OP.mult, CF["sO"], OP.add)
+    ts(LK, LO, 48.0, OP.add)
+    ts(V("tmpi", 96, 99), V("jr", 0, 3), 16.0, OP.mult, CF["i"], OP.add)
+    ts(L3, V("tmpi", 96, 99), -1.0, OP.add, 1.0 / 3, OP.mult)
+    ts(CF["t1"], P, 32.0, OP.mult)
+    ts(V("sn3"), V("sv3"), 128.0, OP.mult, CF["p"], OP.add)
+    ts(V("sv3"), V("sv3"), CF["t1"], OP.add)
+    cp(V("h1", 6, 112, 7), V("sv3", 0, 48, 3))
+    for b_, n_, hi_, lo_ in (("rs48", 48, 2 * BIG, -2 * BIG), ("rst", 16, 1.0, 0.0), ("rs8", 8, 1.0, 0.0)):
+        fill(V(b_), hi_)
+        fill(V(b_, 0, None, n_), lo_)
+    ts(CI["t5"], P, 7, AND)
+    ts(CI["i2"], P, 2, SHR, 1, AND)
+    ts(CI["t5"], CI["t5"], 16.0, OP.mult)
+    fill(V("cn"), -4095.0 / 32)
+    fill(V("ob"), 1.0)
+    ts(CF["base"], P, 16.0, OP.mult)
+    ts(V("th"), V("io128", 0, 16), CF["base"], OP.add, -1.0, OP.mult)
+    ts(V("th"), V("th"), 0.5, OP.add)
     ts(CI["i1"], P, 1, SHR, 1, AND)
-    ts(CI["i12"], P, 1, SHR, 3, AND)
     ts(CI["i3"], P, 3, SHR, 1, AND)
-    ts(CI["i123"], P, 1, SHR, 7, AND)
-    tt(CI["t1"], CI["t0"], CI["g"], OP.add)
-    ts(CI["q"], P, 31, AND)
-    cp(V("cf", 0, 5), V("ci", 0, 5))
-    tt(CI["ne"], CI["i0"], CI["hs"], OP.not_equal)
-    ts(CI["hoff"], CI["hs"], -32.0, OP.mult, 96.0, OP.add)
-    cp(LNB, CI["t1"])
-    tt(CI["t2"], CI["as"], CI["i12"], OP.subtract)
-    fill(V("xx"), 0.0)
-    fill(V("qn", 48, 64), 0.0)
-    ts(CI["t3"], CI["i123"], 2.0, OP.mult, CF["hs"], OP.add)
-    tt(CI["nh"], CI["ne"], CI["hoff"], OP.mult)
-    ts(CI["d"], CI["t2"], 3, AND)
-    cp(LB(0, 48), V("jr"))
+    ts(CI["s0"], CI["h"], -1.0, OP.mult, 3.0, OP.add)
+    ts(V("tmpi", 104, 112), V("jr", 0, 8), 1, SHR, 1, AND)
+    ts(V("tmpi", 112, 120), V("jr", 0, 8), 2, SHR)
+    ts(V("tmpi", 120, 128), V("jr", 0, 8), 1, AND)
+    tt(CF["sZ"], CI["t5"], CI["i3"], OP.add)
+    tt(CI["s0"], CI["s0"], CI["ne"], OP.mult)
+    tt(CI["s1"], CI["i1"], CI["lo"], OP.not_equal)
+    tt(CI["s2"], CI["i2"], CI["hi"], OP.not_equal)
+    ts(CI["s3"], CI["i3"], 32.0, OP.mult, 15.0, OP.add)
+    ts(CI["s4"], CI["e"], 16.0, OP.mult)
+    ts(V("tmpi", 104, 112), V("tmpi", 104, 112), CF["lo"], OP.not_equal, 32.0, OP.mult)
+    ts(V("tmpi", 112, 120), V("tmpi", 112, 120), CF["hi"], OP.not_equal, 64.0, OP.mult)
+    ts(V("tmpi", 120, 128), V("tmpi", 120, 128), 128.0, OP.mult, CF["r"], OP.add)
+    ts(LZ, V("jr", 0, 8), 2.0, OP.mult, CF["sZ"], OP.add)
+    tt(CI["s0"], CI["s0"], CI["i1"], OP.add)
+    ts(CI["s1"], CI["s1"], 64.0, OP.mult)
+    ts(CI["s2"], CI["s2"], 128.0, OP.mult)
+    tt(CI["s3"], CI["s3"], CI["s4"], OP.add)
+    ts(CI["s5"], CI["h"], 16.0, OP.mult, 15.0, OP.add)
+    ts(CI["t7"], CI["e"], 32.0, OP.mult)
+    tt(V("tmpi", 104, 112), V("tmpi", 104, 112), V("tmpi", 112, 120), OP.add)
+    ts(V("tmpi", 120, 128), V("tmpi", 120, 128), float(M * rank), OP.add)
+    cp(LQ, CI["s0"])
+    ts(LCH, CI["s0"], 8.0, OP.mult, 7.0, OP.add)
+    tt(CI["s1"], CI["s1"], CI["s2"], OP.add)
+    tt(CI["s5"], CI["s5"], CI["t7"], OP.add)
+    tt(V("my8", 0, 8), V("tmpi", 104, 112), V("tmpi", 120, 128), OP.add)
+    tt(CI["s1"], CI["s1"], CI["s3"], OP.add)
+    cp(LH, CI["s5"])
+    ts(CF["g256"], CF["g"], 256.0, OP.mult)
+    cp(LF, CI["s1"])
+    ts(V("mym"), V("jr", 0, 16), 16.0, OP.mult, CF["i"], OP.add)
+    ts(CI["t8"], CI["g"], float(set_c[0]), OP.is_ge, float(K), OP.mult)
+    ts(CI["t9"], CI["g"], float(set_c[-1]), OP.is_le)
+    ts(V("sv", 128, 256), V("sv", 0, 128), 8.0, OP.add, CF["g256"], OP.add)
+    ts(V("sv", 0, 128), V("sv", 0, 128), CF["g256"], OP.add)
+    ts(V("dum"), V("mym"), float(DUMMY), OP.add)
+    tt(CF["cC"], CI["t8"], CI["t9"], OP.mult)
+    fill(V("c128"), 128.0)
+    ts(V("odd"), io32, 2.0, OP.mult, 1.0, OP.add)
+    ts(V("nodd"), io32, -2.0, OP.mult, -1.0, OP.add)
+    fill(V("bt", 0, 1), 0.0)
+    fill(V("k0", 3, 64, 4), 1.0)
+    ts(V("pfb", 0, 1), P, float(32 - NS), OP.mult, 128.0 * NS, OP.add)
+    ts(V("pfb", 33, 34), P, float(-NS), OP.mult, 128.0 * NS, OP.add)
+    for b in range(4):
+        fill(V("et", 512 * b, 512 * b + 512), 0.0)
+        ts(V("et", 512 * b + b, 512 * b + 512, 4), V("io128"), CF["p"], OP.is_equal)
+        quant(V("qe", 128 * b, 128 * b + 128), V("se", 128 * b, 128 * b + 128), V("et", 512 * b, 512 * b + 512))
+
     cp(V("nbs", p0=32, p1=64), V("nbs", p1=32))
     cp(V("nbs", p0=64, p1=96), V("nbs", p1=32))
     cp(V("nbs", p0=96), V("nbs", p1=32))
-    tt(CF["sO"], CI["t3"], CI["nh"], OP.add)
-    tt(CI["t4"], CI["i3"], CI["nh"], OP.add)
-    ts(CI["t5"], CI["d"], 16.0, OP.mult)
-    cp(V("nbo"), IND(V("nbs"), LNB))
-    allgather(V("nbo", 0, 6), "nbl", 6, "an")
-    quant(V("ct0", 0, M), V("pt0", 0, M), V("xs"))
+    cp(V("so", 0, 16), IND(V("nbs"), LNB))
+    tt(V("so", 16, 18), V("so", 0, 6, 3), V("so", 1, 6, 3), OP.min)
+    tt(V("so", 18, 20), V("so", 0, 6, 3), V("so", 1, 6, 3), OP.max)
+    tt(V("so", 20, 22), V("so", 18, 20), V("so", 2, 6, 3), OP.min)
+    ts(V("nbo", 0, 1), V("so", 16, 17), V("so", 2, 3), OP.min)
+    ts(V("nbo", 3, 4), V("so", 17, 18), V("so", 5, 6), OP.min)
+    ts(V("nbo", 2, 3), V("so", 18, 19), V("so", 2, 3), OP.max)
+    ts(V("nbo", 5, 6), V("so", 19, 20), V("so", 5, 6), OP.max)
+    ts(V("nbo", 1, 2), V("so", 16, 17), V("so", 20, 21), OP.max)
+    ts(V("nbo", 4, 5), V("so", 17, 18), V("so", 21, 22), OP.max)
+    allgather(V("nbo", 0, 6), "nbl", 6, "an", FAR + 1.0)
+    quant(V("ct0", 0, 128), V("pt0", 0, 128), V("xs", 0, 512))
+    quant(V("ct0", 128, M), V("pt0", 128, M), V("xs", 512, 1024))
     quant(V("qu"), V("su"), V("us"))
-    ts(LO, V("jr", 0, 3), 16.0, OP.mult, CF["sO"], OP.add)
-    tt(CF["sW"], CI["t4"], CI["t5"], OP.add)
-    ts(LI, V("jr", 0, 3), 0.0, OP.mult, CF["i"], OP.add)
-    cp(CF["q"], CI["q"])
-    ts(CF["m128i"], CF["i"], -128.0, OP.mult)
-    ts(CF["noff"], CF["i"], 128.0, OP.mult, -1920.0, OP.add)
 
     def products(t, c0):
         for u in range(2):
@@ -339,354 +510,217 @@ def rank_program(g, core, T, topo):
         dma("s", ap(own), ap(mine), "dh", [own], [mine])
 
     heights(0)
-    iota(V("sv"), [[1, 16], [16, 16]], 1, 0)
-    iota(V("rs8"), [[0, 16], [1, 8]], 0, 0)
-    iota(V("rs3"), [[0, 16], [1, 3]], 0, 0)
-    iota(V("io512"), [[1, 512]], 0, 0)
+    dma("s", T.ws[:], T.w[:], "dw", [V("ws")], [V("hs", 0, 2)], lat=2.0)
+    quant(V("qw"), V("sw"), V("ws"))
 
-    ts(LW, V("jr", 0, 8), 2.0, OP.mult, CF["sW"], OP.add)
-    ts(CF["top"], CF["i"], -128.0, OP.mult, 2176.0, OP.add)
-    ts(CF["k0"], CF["i"], -1.0 / 32, OP.mult, 256.0, OP.add)
-    ts(V("rst"), V("iot16"), 0.0, OP.not_equal)
-    ts(V("tmpi", 0, 16), V("jr", 0, 16), -8.0, OP.mult, CF["g"], OP.subtract)
-    ts(CI["r0"], CI["hs"], -2.0, OP.mult, 18.0, OP.add)
-    tt(CI["r1"], CI["i3"], CI["hs"], OP.not_equal)
-    tt(CI["r2"], CI["i1"], CI["hs"], OP.not_equal)
-    ts(CI["r3"], CI["d"], 40.0, OP.mult)
-    ts(CI["r5"], CI["t3"], -1.0, OP.add, 0.0, OP.max)
-    for k in range(3):
-        cp(V("rsb", 256 * k, 256 * k + 256), V("rst"), "a")
-    ts(V("kk", 48, 64), V("tmpi", 0, 16), CF["k0"], OP.add)
-    tt(CI["r4"], CI["ne"], CI["r0"], OP.mult)
-    tt(CI["r1"], CI["r1"], CI["r0"], OP.mult)
-    tt(CI["r2"], CI["r2"], CI["r0"], OP.mult)
-    tt(CI["r3"], CI["r3"], CI["i0"], OP.add)
-    tt(CI["r5"], CI["r5"], CI["nh"], OP.add)
-    fill(V("d1"), 2048.0)
-    tt(CI["r4"], CI["r4"], CI["t3"], OP.add)
-    tt(CF["sW2"], CI["r3"], CI["r1"], OP.add)
-    cp(V("lst", 148, 149), CF["sO"])
-    ts(V("lst", 150, 151), CI["nh"], 15.0, OP.add)
-    cp(V("lst", 149, 150), CI["r5"])
-    fill(V("gp"), 0.0)
-    fill(V("q"), 0.0)
-    fill(V("qq"), 0.0)
-    cp(LQ, CI["r4"])
-    ts(LW2, V("jr", 0, 8), 2.0, OP.mult, CF["sW2"], OP.add)
-
-    def constants():
-        tt(CI["r2"], CI["r2"], CI["i0"], OP.add)
-        ts(LO2, CI["i1"], 2.0, OP.mult, CF["hs"], OP.add)
-        ts(CI["t2"], CI["d"], 4.0, OP.mult)
-        yield
-        ts(CI["t3"], CI["i3"], 2.0, OP.mult)
-        ts(CI["t4"], CI["i123"], 2.0, OP.mult)
-        ts(CI["t5"], CI["hs"], -1.0, OP.mult, 3.0, OP.add)
-        yield
-        ts(V("tmpi", 16, 32), V("jr", 0, 16), 1, SHR, 3, AND)
-        tt(CI["t6"], CI["t2"], CI["t3"], OP.add)
-        tt(CI["t4"], CI["t4"], CI["ne"], OP.add)
-        yield
-        tt(CI["t5"], CI["t5"], CI["ne"], OP.mult)
-        ts(V("tmpi", 32, 48), V("jr", 0, 16), 3, SHR)
-        ts(V("tmpi", 48, 64), V("tmpi", 16, 32), -1.0, OP.mult, CF["as"], OP.add)
-        yield
-        tt(CI["t6"], CI["t6"], CI["ne"], OP.add)
-        cp(LA, CI["t4"])
-        tt(CI["t5"], CI["t5"], CI["i1"], OP.add)
-        yield
-        ts(V("tmpi", 32, 48), V("tmpi", 32, 48), 2.0, OP.mult, CF["hs"], OP.add)
-        ts(V("tmpi", 48, 64), V("tmpi", 48, 64), 3, AND)
-        cp(LR2, CI["t6"])
-        yield
-        ts(V("tmpi", 64, 96), V("jr", 0, 32), 1, SHR)
-        ts(LCH, CI["t5"], 8.0, OP.mult, 7.0, OP.add)
-        ts(V("tmpi", 48, 64), V("tmpi", 48, 64), 4.0, OP.mult)
-        yield
-        ts(V("th"), V("thx"), -1.0, OP.add, -1.0 / 64, OP.mult)
-        ts(LB2, V("tmpi", 64, 96), 8.0, OP.mult, 7.0, OP.add)
-        tt(V("tmpi", 48, 64), V("tmpi", 48, 64), V("tmpi", 32, 48), OP.add)
-        yield
-        fill(V("ob"), 1.0)
-        cp(LF, V("tmpi", 48, 64))
-        ts(LP2, CI["r2"], float(2 * rank), OP.add)
-        yield
-        ts(V("iot32"), V("iot16", 0, 64), 1.0 / 32, OP.mult)
-        ts(CF["p4"], P, 4.0, OP.mult)
-        ts(CF["o4096"], CF["i"], -4096.0, OP.mult, 61440.0, OP.add)
-        yield
-        ts(CF["ba"], CF["q"], -2.0, OP.mult, -3.0, OP.add)
-        ts(CF["bd"], CF["q"], 2.0, OP.mult, 4.0, OP.add)
-        ts(CF["g256"], CF["g"], 256.0, OP.mult)
-        yield
-        ts(V("tri"), V("tri"), CF["q"], OP.is_lt)
-        fill(V("c128"), 128.0)
-        fill(V("ones"), 1.0)
-        yield
-        fill(V("cc", 8, 9), float(4 * CA))
-        fill(V("pf"), 0.0)
-        ts(V("rs8"), V("rs8"), 0.0, OP.not_equal)
-        yield
-        ts(V("rs3"), V("rs3"), 0.0, OP.not_equal)
-        ts(CI["t0"], P, 7, AND)
-        ts(CI["t1"], CI["i0"], 4.0, OP.mult, CF["as"], OP.add)
-        yield
-        ts(CI["t0"], CI["t0"], 16.0, OP.mult)
-        ts(LH, CI["t1"], 2.0, OP.mult)
-        ts(V("tmpi", 96, 112), V("jr", 0, 16), 1, AND)
-        yield
-        tt(CF["sZ"], CI["t0"], CI["i3"], OP.add)
-        ts(V("dum"), V("jr", 0, 16), 16.0, OP.mult, CF["i"], OP.add)
-        tt(V("tmpi", 112, 128), V("jr", 0, 16), V("tmpi", 96, 112), OP.subtract)
-        yield
-        ts(LZ, V("jr", 0, 8), 2.0, OP.mult, CF["sZ"], OP.add)
-        ts(V("tmpi", 96, 112), V("tmpi", 96, 112), CF["hs"], OP.not_equal)
-        ts(V("dum"), V("dum"), float(DUMMY), OP.add)
-        yield
-        tt(V("tmpi", 96, 112), V("tmpi", 96, 112), V("tmpi", 112, 128), OP.add)
-        ts(V("sv"), V("sv"), CF["g256"], OP.add)
-        yield
-        ts(V("mym"), V("tmpi", 96, 112), 16.0, OP.mult, CF["i"], OP.add)
-
-    rest = constants()
-
-    def unpacker(b):
-        ts(V("et", 512 * b, 512 * b + 512), V("io512"), CF["p4"], OP.subtract, float(b), OP.is_equal)
-
-    cp(V("nbl", 6 * rank, 6 * rank + 6), V("nbo", 0, 6))
+    for a, b in ((0, 6 * rank), (6 * rank + 6, 48)):
+        if a < b:
+            cp(V("tmpi", a, b), V("nbl", a, b))
+    cp(V("tmpi", 6 * rank, 6 * rank + 6), V("nbo", 0, 6))
+    ts(V("tmpi", 48, 96), V("tmpi", 0, 48), 127, AND)
+    ts(V("qi", 0, 48), V("tmpi", 0, 48), 7, SHR)
+    cp(V("qn", 48, 96), V("qi", 0, 48))
+    cp(V("qn", 0, 48), V("tmpi", 48, 96))
+    tt(V("bm"), V("tmpi", 0, 48), V("sn3"), OP.is_lt)
+    tr(V("xx", 16, 112), V("qn", 0, 96))
+    ts(V("so2"), V("qn", 0, 48), 32.0, OP.mult)
+    tr(V("qn", 96, 224), V("xx"))
+    tt(V("so2"), V("so2"), V("qn", 48, 96), OP.add)
+    cp(V("ok"), IND(V("qn"), LK))
+    ts(V("on"), IND(V("qn"), LO), CF["coff"], OP.add)
+    for k in range(4):
+        cp(V("mt3", 192 * k, 192 * k + 192), IND(V("eqm"), V("ok", 12 * k, 12 * k + 12)), "a")
+    tt(V("so2"), V("so2"), V("sv3"), OP.subtract)
+    ts(V("bm"), V("bm"), -BIG, OP.mult)
     for j in range(J):
-        for u in range(2):
-            cp(V("nbi", 16 * j + u, 16 * j + 16, 2), V("nbl", 2 * j + u, 48, 6))
-    ts(V("nhi"), V("nbi"), 4, SHR)
-    ts(V("nlo"), V("nbi"), 15, AND)
-    cp(V("qn", 0, 48), V("nhi"))
-    tt(V("mt", 0, 256), IND(V("nlo"), LB(0, 16)), V("iot16"), OP.is_equal)
-    tr(V("xx", 16, 80), V("qn", 0, 64))
-    tt(V("mt", 256, 512), IND(V("nlo"), LB(16, 32)), V("iot16"), OP.is_equal)
-    tr(V("qn", 64, 160), V("xx"))
-    tt(V("mt", 512, 768), IND(V("nlo"), LB(32, 48)), V("iot16"), OP.is_equal)
-    ts(V("sm", 0, 48), V("nlo"), -1.0 / 32, OP.mult, 256.0, OP.add)
-    cp(V("on"), IND(V("qn"), LO))
-    tr(V("mf"), V("mt"))
-    tt(V("kk", 0, 48), V("sm", 0, 48), V("nhi"), OP.subtract)
+        cp(V("h1", 5 - 2 * j, 112, 7), V("so2", j, 48, 3))
+        ts(V("h1", 4 - 2 * j, 112, 7), V("so2", j, 48, 3), -1.0, OP.mult)
 
-    def in_range(out, tmp, x, ranks, base):
-        ts(out, x, float(M * ranks[0] + base), OP.is_ge, float(K), OP.mult)
-        ts(tmp, x, float(M * (ranks[-1] + 1) + base), OP.is_lt)
-        tt(out, out, tmp, OP.mult)
+    def lookup(src, c0, s, d, pieces):
+        for a, b, q in pieces:
+            x = V(src, c0 + s * (a // 16), c0 + s * (b // 16 - 1) + 1, s)
+            o2, oo = V("o2", 16 * d + a // 16, 16 * d + b // 16), V("oo", 16 * d + a // 16, 16 * d + b // 16)
+            mg, mt, gm, tt_ = [V(n_, 256 * d + a, 256 * d + b) for n_ in ("mg", "mt", "gm", "tt")]
+            cp(o2, x)
+            ts(oo, x, 1.0 / 32, OP.mult, CF["coff"], OP.add)
+            cp(mg, IND(V("mk"), o2), "a")
+            cp(gm, IND(V("tbp"), oo), q)
+            tr(mt, mg)
+            tr(tt_, gm)
+            scan(V("sp", 272 * d + a, 272 * d + b), mt, tt_, OP.mult, OP.add)
+
+    def pointers(src, c0, s):
+        for k in range(2):
+            tt(V("dd", 16 * k, 16 * k + 16), V(src, c0, c0 + 15 * s + 1, s), V(src, c0 + s, c0 + 16 * s + 1, s), OP.subtract)
+        table("tbp", V("dd"))
+
+    def walk(out, x, d):
+        o2, oo = V("ow", 4 * d, 4 * d + 2), V("ow", 4 * d + 2, 4 * d + 4)
+        mg, mt, gm, tt_ = [V(n_, 32 * d, 32 * d + 32) for n_ in ("mw", "nw", "gw", "tw")]
+        cp(o2, x)
+        ts(oo, x, 1.0 / 32, OP.mult, CF["coff"], OP.add)
+        cp(mg, IND(V("mk"), o2), "a")
+        cp(gm, IND(V("tbp"), oo))
+        tr(mt, mg)
+        tr(tt_, gm)
+        scan(out, mt, tt_, OP.mult, OP.add)
 
     for t in range(R):
         ct, pt, qh, hl = "ct%d" % t, "pt%d" % t, "qh%d" % t, "hl%d" % t
-        shift_now(qh, 16)
-        cross(qh)
-        cp(V("wt", 0, 64), IND(V(qh), V("lst", 2, 6)), "a")
-        cp(V("wt", 64, 128), IND(V(qh), V("lst", 6, 10)), "v")
+        cp(V(qh, 16, 32), V(qh, 0, 16))
+        tt(V("hm"), IND(V(qh, 0, 16), L3), V("bm"), OP.add)
+        table("tbh", V(qh))
+        for k in range(4):
+            gn, tn, sn, mt3 = [V(n_, 192 * k, 192 * k + 192) for n_ in ("gn", "tn", "sn", "mt3")]
+            tt(gn, IND(V("tbh"), V("on", 12 * k, 12 * k + 12)), mt3, OP.add)
+            tr(tn, gn)
+            scan(sn, V("rs48"), tn, OP.min, OP.max)
+        tt(V("mx"), V("sn", 47, 768, 48), V(qh, 0, 16), OP.max)
         for j in range(J):
-            tt(V("gm", 256 * j, 256 * j + 256), IND(V("wt"), V("on", 16 * j, 16 * j + 16)), V("mf", 256 * j, 256 * j + 256), OP.mult)
+            tt(V("h0", 6 - 2 * j, 112, 7), V("hm", j, 48, 3), V("mx"), OP.is_lt)
         for j in range(J):
-            tr(V("tt", 256 * j, 256 * j + 256), V("gm", 256 * j, 256 * j + 256))
-        for j in range(J):
-            scan(V("ss", 256 * j, 256 * j + 256), V("rst"), V("tt", 256 * j, 256 * j + 256), OP.mult, OP.add)
-        tt(V("sm", 0, 16), V("ss", 15, 256, 16), V("ss", 271, 512, 16), OP.max)
-        tt(V("sm", 16, 32), V("ss", 527, 768, 16), V(qh, 0, 16), OP.max)
-        tt(V("sm", 32, 48), V("sm", 0, 16), V("sm", 16, 32), OP.max)
-        tt(V("sm", 64, 112), IND(V("sm", 32, 48), LI), V("ss", 15, 768, 16), OP.is_equal)
-        tt(V("sm", 112, 128), V("sm", 32, 48), V(qh, 0, 16), OP.is_equal)
-        tt(V("sm", 64, 128), V("sm", 64, 128), V("kk"), OP.mult)
-        tt(V("sm", 128, 160), V("sm", 64, 96), V("sm", 96, 128), OP.max)
-        tt(V("q", 0, 16), V("sm", 128, 144), V("sm", 144, 160), OP.max)
-        tr(V("xx", 16, 48), V("q", 0, 32))
-        tr(V("q", 64, 128), V("xx", 0, 64))
-        ts(V("qq", 0, 48), IND(V("q"), LS), -1.0, OP.mult, CF["top"], OP.add)
-        for step in range(10):
-            next(rest, None)
-            if step < 9:
-                cp(V("hi", 0, 34), V("qq", 0, 34))
-            shift_now("qq", 40, 34)
-            cp(V("wt"), IND(V("qq"), LW2), "a")
-            if step == 9:
-                break
-            tt(V("lof", 0, 34), V("qq", 0, 34), V("hi", 0, 34), OP.subtract)
-            ts(V("oo"), IND(V("qq", 0, 40), LQ), CF["noff"], OP.add)
-            ts(V("d1", 0, 544, 16), V("lof", 0, 34), -65536.0, OP.mult)
-            ts(V("cor", 0, 34), V("lof", 0, 34), 4096.0, OP.mult, CF["m128i"], OP.add)
-            cp(V("gp", 16, 16 + GA), IND(V("wt"), V("oo", 0, GA // 16)), "a")
-            cp(V("gp", 16 + GA, 272), IND(V("wt"), V("oo", GA // 16, 16)), "v")
-            scan(V("mk"), V("rsb", 0, 544), V("d1"), OP.mult, OP.add)
-            tr(V("tt", 0, 256), V("gp", 16, 272))
-            tr(V("tt", 256, 544), V("gp"))
-            scan(V("ss", 0, 256), V("mk", 0, 256), V("tt", 0, 256), OP.min, OP.max)
-            scan(V("ss", 256, 544), V("mk", 256, 544), V("tt", 256, 544), OP.min, OP.max)
-            next(rest, None)
-            tt(V("qq", 0, 34), V("ss", 15, 544, 16), V("cor", 0, 34), OP.add)
-        for _ in rest:
-            pass
-        ts(V("p2"), IND(V("qq", 0, 40), LP2), CF["noff"], OP.add)
-        for step in range(3):
-            cp(V("oo"), IND(V("p2"), LO2))
-            cp(V("hi", 0, 4), V("p2", 0, 4))
-            cp(V("gm", 0, 64), IND(V("wt"), V("oo", 0, 4)), "a")
-            tt(V("lof", 0, 4), V("p2", 0, 4), V("hi", 0, 4), OP.subtract)
-            tt(V("mk", 0, 64), IND(V("lof", 0, 16), LB(0, 4)), V("iot32"), OP.not_equal)
-            tr(V("tt", 0, 64), V("gm", 0, 64))
-            ts(V("cor", 0, 4), V("lof", 0, 4), 4096.0, OP.mult, -1920.0, OP.add)
-            scan(V("ss", 0, 64), V("mk", 0, 64), V("tt", 0, 64), OP.mult, OP.max)
-            if t == 0:
-                unpacker(step)
-            tt(V("p2" if step < 2 else "q2", 0, 4), V("ss", 15, 64, 16), V("cor", 0, 4), OP.add)
-        shift_now("q2", 4)
-        if t == 0:
-            unpacker(3)
-        cp(V("rb", 0, 128), IND(V("q2"), V("lst", 28, 36)), "v")
-        cp(V("rb", 128, 256), IND(V("q2"), V("lst", 36, 44)), "a")
-        tr(V("rf"), V("rb"))
-        ts(V("zb"), V("rf"), CF["p"], OP.subtract)
+            tt(V("h0", 5 - 2 * j, 112, 7), V("sn", 16 * j + 15, 768, 48), V("mx"), OP.is_lt)
+        scan(V("hz", 0, 112), V("h0"), V("h1"), OP.mult, OP.add)
+        for step in range(6):
+            src = ("hz", 6, 7) if step == 0 else ("sp", 272 + 15, 16)
+            pointers(*src)
+            lookup(*src, 0, PIECES_R)
+            lookup("sp", 15, 16, 1, PIECES_W)
+        pointers("sp", 272 + 15, 16)
+        walk(V("w1"), V("sp", 272 + 32 * rank + 15, 272 + 32 * rank + 32, 16), 0)
+        walk(V("w2"), V("w1", 15, 32, 16), 1)
+        ts(V("cv", 0, 2), V("w2", 15, 32, 16), ROUND32, OP.add, ROUND32, OP.subtract)
+        ts(V("cv", 2, 4), V("w2", 15, 32, 16), 128.0, OP.mult)
+        for u in range(2):
+            ts(V("yb", 32 * u, 32 * u + 32), V("cn"), V("cv", u, u + 1), OP.mult, V("cv", 2 + u, 3 + u), OP.add)
+        turn(lambda a, b: V("rf", 64 * (a ^ b), 64 * (a ^ b) + 64), V("yb"), NC)
+        ts(V("zb"), V("rf"), CF["base"], OP.subtract)
         for k in range(NA + 1):
             sign(V("ja", 256 * k, 256 * k + 256), V("rf"), V("th", k, k + 1), V("acc", k, k + 1))
         for k in range(ND):
-            ts(V("jd", 256 * k, 256 * k + 256), V("zb"), (NA + k) / 32.0, OP.is_equal, 2.0, OP.mult)
+            ts(V("jd", 256 * k, 256 * k + 256), V("zb"), float(NA + k), OP.is_equal, 2.0, OP.mult)
         for k in range(ND):
             scan(V("js", 256 * k, 256 * k + 256), V("ob"), V("jd", 256 * k, 256 * k + 256), OP.mult, OP.add)
         cp(V(hl, 16 * rank + NA, 16 * rank + 16), V("js", 255, 256 * ND, 256))
         tt(V(hl, 16 * rank, 16 * rank + NA), V("acc", 0, NA), V("acc", 1, NA + 1), OP.subtract)
         allgather(V(hl, 16 * rank, 16 * rank + 16), hl, 16, "az%d" % t)
-        fill(V("lw", 0, 96), 0.0)
-        cp(V("r2"), IND(V("q2"), LR2))
-        cp(V("rti", p1=1), V("rf", p1=1))
-        ts(V("rta", p1=1), V("rf", p1=1), 32.0, OP.mult)
-        cp(V("r2i", 0, 16), V("r2"))
-        ts(V("rtb", p1=1), V("rti", p1=1), 16.0, OP.mult)
-        cp(V("s1"), IND(V(hl), LZ))
-        tt(V("rto", M * t, M * t + M, p1=1), V("rta", p1=1), V("rtb", p1=1), OP.subtract)
-        dma("s", T.rt[0:1, M * t:M * t + M], ap(V("rto", M * t, M * t + M, p1=1)), "dout", ins=[V("rto", M * t, M * t + M, p1=1)])
-        scan(V("sz"), V("rs8"), V("s1"), OP.mult, OP.add)
-        tt(V("r2f", 0, 16), V("r2"), V("r2i", 0, 16), OP.subtract)
-        ts(V("r2i", 16, 32), V("r2i", 0, 16), 15, AND)
-        ts(V("r2i", 32, 48), V("r2i", 0, 16), 4, SHR)
-        size = V("sz", 7, 128, 8)
-        cp(V("yb", 0, 256), IND(V("sz"), V("lst", 44, 60)), "a")
-        cp(V("yb", 256, 512), IND(V("sz"), V("lst", 60, 76)), "v")
-        ts(V("r2f", 16, 32), V("r2f", 0, 16), 256.0, OP.mult)
-        ts(V("r2f", 32, 48), V("r2"), 32.0, OP.mult)
-        ts(V("r2f", 48, 64), V("r2i", 0, 16), 16.0, OP.mult)
-        tr(V("yt"), V("yb"))
-        sign(V("jy", 0, CA), V("yt", 0, CA), CF["ba"], V("cc", 0, 1))
-        ts(V("jy", CA, 512), V("yt", CA, 512), CF["bd"], OP.is_ge, 2.0, OP.mult)
-        tt(V("r2f", 16, 32), V("r2f", 16, 32), V("r2i", 32, 48), OP.add)
-        tt(V("r2f", 32, 48), V("r2f", 32, 48), V("r2f", 48, 64), OP.subtract)
-        red(V("cc", 1, 2), V("jy", CA, 512), OP.add)
-        shift_now("cc", 2)
-        red(V("cs", 0, 1), V("cc", 0, 9), OP.add)
-        ts(V("r2f", 64, 80), V("r2i", 16, 32), 4096.0, OP.mult, -61440.0, OP.add)
-        cp(V("o3"), V("r2f", 16, 32))
-        ts(V("bb", 0, 32), V("c128"), V("cs", 0, 1), OP.is_le, 2.0, OP.mult)
-        ts(V("bb", 32, 64), V("c128"), V("cs", 0, 1), OP.is_gt, V("cs", 0, 1), OP.mult)
-        tr(V("bt"), V("bb"))
-        red(V("cs", 1, 2), V("bt", 0, 32), OP.add)
-        red(V("cs", 2, 3), V("bt", 32, 64), OP.max)
-        ts(V("fl", 0, 16), size, -2.0, OP.add, V("cs", 1, 2), OP.is_gt)
-        ts(V("fl", 16, 32), size, -2.0, OP.add, V("cs", 1, 2), OP.is_equal)
-        ts(V("fl", 32, 48), size, -2.0, OP.add, V("cs", 1, 2), OP.is_lt)
-        scan(V("sc"), V("rst", 0, 32), V("fl", 0, 32), OP.mult, OP.add)
-        ts(V("pf", 9, 10), V("cs", 2, 3), 0.5, OP.mult)
-        tt(V("bs", 32, 48), V("fl", 32, 48), V("dum"), OP.mult)
-        ts(V("bb", 0, 32), V("ones"), V("sc", 15, 16), OP.mult)
-        ts(V("bb", 32, 64), V("ones"), V("sc", 31, 32), OP.mult)
-        tt(V("bs", 0, 32), V("sc"), V("fl", 0, 32), OP.mult)
-        ts(V("bs", 32, 48), V("bs", 32, 48), 15.0, OP.add)
-        tr(V("bt"), V("bb"))
-        tt(V("bs", 48, 64), V("bs", 0, 16), V("bs", 16, 32), OP.add)
-        red(V("rr", 0, 1), V("bt", 0, 32), OP.add)
-        red(V("rr", 1, 2), V("bt", 32, 64), OP.add)
-        tt(V("tm"), V("bt"), V("tri"), OP.mult)
-        tt(V("v3", 0, 48, 3), V("bs", 48, 64), V("bs", 32, 48), OP.add)
-        cp(V("pf", 2, 4, 1, 32, 64), V("rr", 0, 2, 1, 0, 32), "a")
-        cp(V("pf", 2, 4, 1, 64, 96), V("rr", 0, 2, 1, 32, 64), "a")
-        cp(V("pf", 2, 4, 1, 96, 128), V("rr", 0, 2, 1, 64, 96), "a")
-        cp(V("pf", 4, 6, 1, 64, 128), V("rr", 0, 2, 1, 0, 64), "v")
-        cp(V("pf", 6, 8, 1, 96, 128), V("rr", 0, 2, 1, 0, 32), "v")
-        red(V("pf", 0, 1), V("tm", 0, 32), OP.add)
-        red(V("pf", 1, 2), V("tm", 32, 64), OP.add)
-        red(V("rr", 2, 3), V("pf", 0, 10, 2), OP.add)
-        red(V("rr", 3, 4), V("pf", 1, 10, 2), OP.add)
-        ts(V("v3", 1, 48, 3), V("fl", 0, 16), V("rr", 2, 3), OP.mult)
-        ts(V("v3", 2, 48, 3), V("fl", 16, 32), V("rr", 3, 4), OP.mult)
-        scan(V("v3s"), V("rs3"), V("v3"), OP.mult, OP.add)
-        cp(V("vo"), V("v3s", 2, 48, 3))
-        ts(V("q", 0, 16), V("v3s", 2, 48, 3), CF["o4096"], OP.add)
-        emit("v", lambda: g.vector.tensor_copy(ap(IND(V("lw"), V("vo"))), ap(V("sv"))), [V("lw")], [V("sv"), V("vo")])
-        if t == 0:
-            quant(V("qe"), V("se"), V("et"))
+        tr(V("rt2"), V("rf"))
+        fill(V("lw", 0, 112), 0.0)
+        cp(V("qi", 0, 8), V("rt2", 0, 256, 32))
+        ts(V("qi", 8, 16), V("qi", 0, 8), 4, SHR)
+        ts(V("qi", 24, 32), V("qi", 0, 8), 15, AND)
+        ts(V("qf", 48, 56), V("qi", 24, 32), 15.0, OP.add)
+        for e in range(2):
+            ts(V("o3", e, 16, 2), V("qi", 8, 16), CF["coff"], OP.add)
+        for u in range(2):
+            cp(V("nn", 4 * u, 4 * u + 4), V("rt2", 32 * u, 256, 64))
+        tt(V("qf", 56, 64), V("rt2", 0, 256, 32), V("my8", 0, 8), OP.not_equal)
+        tr(V("nt", 32 * t, 32 * t + 32, 1, 0, 32), V("nn", p1=32))
+        tt(V("qf", 48, 56), V("qf", 48, 56), V("qf", 56, 64), OP.mult)
+        dma("s", T.rt[0:1, M * t:M * t + M], ap(V("nt", 32 * t, 32 * t + 32, 1, 0, 8)), "dout", ins=[V("nt", 32 * t, 32 * t + 32, 1, 0, 32)])
+        for e in range(2):
+            ts(V("o4", e, 16, 2), V("qf", 48, 56), 16.0, OP.add)
+        for k in range(2):
+            cp(V("mgs", 128 * k, 128 * k + 128), IND(V("mk", 0, 64), V("o4", 8 * k, 8 * k + 8)), "a")
+        cp(V("s1", 64, 128), IND(V(hl), V("lst", 18, 22)), "a")
+        cp(V("s1", 0, 64), IND(V(hl), V("lst", 14, 18)))
+        for k in range(2):
+            scan(V("sz", 64 * k, 64 * k + 64), V("rs8", 0, 64), V("s1", 64 * k, 64 * k + 64), OP.mult, OP.add)
+        ts(V("szh"), V("sz", 7, 128, 8), 0.5, OP.mult)
+        for k in range(16):
+            if k < 16 - NS:
+                ts(V("th0", k, 512, 16), V("odd"), V("sz", 8 * k + 7, 8 * k + 8), OP.is_lt, 2.0, OP.mult)
+            else:
+                sign(V("th0", k, 512, 16), V("nodd"), V("sz", 8 * k + 7, 8 * k + 8))
+        scan(V("th1"), V("rst"), V("th0"), OP.mult, OP.add)
+        table("ctb", V("th1", 15, 512, 16))
+        scan(V("pf2"), V("ob", 0, 224), V("ctb"), OP.mult, OP.add, 128.0 * NS)
+        total = V("pf2", 223, 224)
+        ts(V("bb", 0, 32), V("c128"), total, OP.is_ge)
+        ts(V("bb", 32, 64), V("c128"), total, OP.is_ge, total, OP.mult)
+        tr(V("pfb", 1, 33), V("pf2", 95, 127))
+        tr(V("bt", 1, 65), V("bb"))
+        tt(V("df", 0, 33), V("pfb", 0, 33), V("pfb", 1, 34), OP.subtract)
+        red(V("cs", 0, 1), V("bt", 1, 33), OP.add)
+        scan(V("se0", 0, 33), V("bt", 0, 33), V("df", 0, 33), OP.mult, OP.add)
+        scan(V("se1"), V("bt", 0, 32), V("df", 1, 33), OP.mult, OP.add)
+        red(V("cs", 1, 2), V("bt", 33, 65), OP.max)
+        GT, EQ = V("k0", 1, 64, 4), V("fl", 0, 16)
+        ts(GT, V("szh"), V("cs", 0, 1), OP.add, 32.0, OP.is_gt)
+        ts(EQ, V("szh"), V("cs", 0, 1), OP.add, 32.0, OP.is_equal)
+        ts(V("cs", 2, 3), V("se0", 32, 33), -0.5, OP.mult, V("se1", 31, 32), OP.add)
+        ts(V("cs", 3, 4), V("se0", 32, 33), V("se1", 31, 32), OP.subtract, 0.5, OP.mult)
+        ts(V("fl", 16, 32), V("szh"), V("cs", 0, 1), OP.add, 32.0, OP.is_lt)
+        ts(V("k0", 2, 64, 4), V("szh"), V("cs", 0, 1), OP.add, 32.0, OP.is_ge)
+        scan(V("k1", 0, 64, 4), GT, EQ, OP.add, OP.subtract, V("cs", 2, 3))
+        scan(V("k1", 1, 64, 4), EQ, V("zero"), OP.add, OP.add, V("cs", 3, 4))
+        tt(V("k1", 2, 64, 4), V("fl", 16, 32), V("dum"), OP.mult)
+        ts(V("k1", 3, 64, 4), EQ, V("cs", 1, 2), OP.mult, 0.5, OP.mult)
+        scan(V("k2"), V("k0"), V("k1"), OP.mult, OP.add)
+        val = V("k2", 3, 64, 4)
+        ts(V("vo"), val, 15.0, OP.add)
+        add("v", lambda: g.vector.tensor_copy(ap(IND(V("lw"), V("vo"))), ap(V("sv"))), [V("lw")], [V("sv"), V("vo")], 0.05 + 3.8 * CYCLE * 256)
+        a0, h0 = 32 * (rank // 2), 16 * (rank % 2)
         tr(V("lt", 0, 64), V("lw", 16, 80))
         tr(V("lt", 64, 160), V("lw", 0, 96))
-        cp(V("zz", 0, 40, 4), V("lt", 0, 160, 16))
-        shift_at_once(lambda m, a, b: V("zz", m, 40, 4, a, b), lambda a, b: V("lt", 0, 160, 16, a, b))
-        scan(V("zs"), V("rs8", 0, 40), V("zz"), OP.mult, OP.add)
-        ts(V("pl", 0, 16), IND(V("zs"), LCH), float(-1 - M * rank), OP.add, float(M - 1), OP.min)
+        for a in range(4):
+            cp(V("zo", 0, 5, 1, 32 * a, 32 * a + 32), V("lt", h0, 160, 32, a0, a0 + 32), "a" if a % 2 else "v")
+        ts(V("pl", 0, 16), IND(V("zo"), LQ), float(-1 - M * rank), OP.add)
         ca, pa, cb, pb, cc_, pc_ = ["%s%s%d" % (x, s_, t) for s_ in "abc" for x in "cp"]
-        cp(V("ch"), IND(V("zs"), LCH))
         pick(V(ca, 0, K), V(pa, 0, K), V(ct, 0, M), V(pt, 0, M), V("pl", 0, 4))
         swap(peer_a, ca, pa, "aa%d" % t)
         for b in range(4):
             mm(V("psd", 512 * b, 512 * b + M), V("qe", 128 * b, 128 * b + 128), V("se", 128 * b, 128 * b + 128), V(ct, 0, M), V(pt, 0, M), True, False)
-        ts(V("cht", 0, 4), V("ch", 0, 4), float(M * set_a[0] + 1), OP.is_ge, float(K), OP.mult)
-        ts(V("cht", 4, 8), V("ch", 0, 4), float(M * (set_a[-1] + 1) + 1), OP.is_lt)
-        ts(V("cht", 8, 12), V("ch", 0, 4), float(M * set_b[0] + 1), OP.is_ge, float(K), OP.mult)
-        ts(V("cht", 12, 16), V("ch", 0, 4), float(M * (set_b[-1] + 1) + 1), OP.is_lt)
-        shift_now("q", 16)
-        tt(V("cht", 0, 4), V("cht", 0, 4), V("cht", 4, 8), OP.mult)
-        tt(V("cht", 8, 12), V("cht", 8, 12), V("cht", 12, 16), OP.mult)
-        tt(V("mk3"), IND(V("r2i", 16, 32), LB(0, 16)), V("iot16"), OP.not_equal)
-        tt(V("cht", 0, 4), V("cht", 0, 4), V("dum", 0, 4), OP.add)
-        tt(V("cht", 8, 12), V("cht", 8, 12), V("dum", 0, 4), OP.add)
-        tr(V("xx", 16, 80), V("q", 0, 64))
-        ts(V("r2f", 48, 64), V("r2f", 32, 48), float(-M * rank), OP.add)
-        ts(V("pl", 16, 20), V("cht", 0, 4), float(-DUMMY), OP.add)
-        ts(V("pl", 20, 24), V("cht", 8, 12), float(-DUMMY), OP.add)
-        tr(V("q", 64, 160), V("xx"))
+        cp(V("zz", 0, 40, 4), V("lt", 0, 160, 16))
+        shift_at_once(lambda m, a, b: V("zz", m, 40, 4, a, b), lambda a, b: V("lt", 0, 160, 16, a, b))
+        scan(V("zs", 0, 40), V("rs8", 0, 40), V("zz"), OP.mult, OP.add)
+        cp(V("ch"), IND(V("zs", 0, 40), LCH))
+        for k, s_ in enumerate((set_a, set_b)):
+            ts(V("cht", 8 * k, 8 * k + 4), V("ch", 0, 4), float(M * s_[0] + 1), OP.is_ge, float(K), OP.mult)
+            ts(V("cht", 8 * k + 4, 8 * k + 8), V("ch", 0, 4), float(M * (s_[-1] + 1) + 1), OP.is_ge, float(-K), OP.mult)
+            tt(V("cht", 8 * k, 8 * k + 4), V("cht", 8 * k, 8 * k + 4), V("mym", 0, 4), OP.add)
+            tt(V("cht", 8 * k, 8 * k + 4), V("cht", 8 * k, 8 * k + 4), V("cht", 8 * k + 4, 8 * k + 8), OP.add)
+            cp(V("pl", 16 + 4 * k, 20 + 4 * k), V("cht", 8 * k, 8 * k + 4))
         pick(V(cb, 0, K), V(pb, 0, K), V(ca), V(pa), V("pl", 16, 20))
         swap(peer_b, cb, pb, "ab%d" % t)
-        cp(V("wt"), IND(V("q"), LW), "a")
-        tt(V("r2f", 112, 128), V("r2f", 48, 64), V("mym"), OP.not_equal)
-        in_range(V("r2f", 80, 96), V("r2f", 96, 112), V("r2f", 32, 48), set_c, 0)
-        cp(V("gm", 0, 128), IND(V("wt"), V("o3", 0, 8)), "a")
-        cp(V("gm", 128, 256), IND(V("wt"), V("o3", 8, 16)), "v")
-        tr(V("tt", 0, 256), V("gm", 0, 256))
         pick(V(cc_, 0, K), V(pc_, 0, K), V(cb), V(pb), V("pl", 20, 24))
         swap(peer_c, cc_, pc_, "ac%d" % t)
-        scan(V("ss", 0, 256), V("mk3"), V("tt", 0, 256), OP.mult, OP.max)
+        ts(V("tv", 48, 64), val, 64.5, OP.is_lt)
+        ts(V("tv", 32, 48), val, CF["cC"], OP.add)
+        tt(V("tv", 0, 16), V("tv", 32, 48), V("tv", 48, 64), OP.mult)
+        for k in range(2):
+            tt(V("ds", 16 * k, 16 * k + 16), V("tv", 0, 16), V("tv", 1, 17), OP.subtract)
+        table("tbs", V("ds"))
+        for k in range(2):
+            gs, tts, sps, mgs = [V(n_, 128 * k, 128 * k + 128) for n_ in ("gs", "tts", "sps", "mgs")]
+            tt(gs, IND(V("tbs"), V("o3", 8 * k, 8 * k + 8)), mgs, OP.mult)
+            tr(tts, gs)
+            scan(sps, V("rst", 0, 128), tts, OP.mult, OP.add)
+        ts(V("pl", 32, 48), IND(V("sps"), LF), -1.0, OP.add)
+        ts(V("cht", 48, 64), IND(V("sps"), LF), 0.5, OP.is_gt, float(M), OP.mult)
+        tt(V("cht", 16, 32), V("cht", 48, 64), V("mym"), OP.add)
+        cp(V("pl", 48, 64), V("cht", 16, 32))
         if t + 1 < R:
             products(t, 0)
-        tt(V("cht", 16, 32), V("ss", 15, 256, 16), V("r2f", 64, 80), OP.add)
-        ts(V("cht", 32, 48), V("cht", 16, 32), -16.0, OP.add, float(K - 1), OP.min)
-        ts(V("cht", 48, 64), V("cht", 16, 32), 79.5, OP.is_lt, float(M), OP.mult)
-        tt(V("cht", 32, 48), V("cht", 32, 48), V("r2f", 80, 96), OP.add)
-        tt(V("cht", 48, 64), V("cht", 48, 64), V("r2f", 112, 128), OP.mult)
-        cp(V("pl", 32, 48), IND(V("cht", 32, 48), LA))
+            ts(V("ff"), IND(V("sps"), LH), 0.5, OP.is_gt)
+            ts(V("nf"), IND(V("sps"), LH), 0.5, OP.is_lt)
+            tt(V("ho", 0, 2), V("psh", t + 1, 1024, 512), V("nf", 0, 2), OP.mult)
         cr, pr = "cr%d" % t, "pr%d" % t
         pick(V(cr), V(pr), V(cc_), V(pc_), V("pl", 32, 48))
         for b in range(4):
             mm(V("psd", 512 * b, 512 * b + M), V("qe", 128 * b, 128 * b + 128), V("se", 128 * b, 128 * b + 128), V(cr), V(pr), False, True)
-        if t + 1 < R:
-            ts(V("ff"), IND(V("cht", 48, 64), LH), 1.0 / M, OP.mult)
-        tt(V("cht", 0, 16), V("cht", 48, 64), V("mym"), OP.add)
-        if t + 1 < R:
-            ts(V("nf", 0, 2), V("ff", 0, 2), -1.0, OP.mult, 1.0, OP.add)
-        cp(V("pl", 48, 64), IND(V("cht", 0, 16), LA))
-        if t + 1 < R:
-            tt(V("ho", 0, 2), V("psh", t + 1, 1024, 512), V("nf", 0, 2), OP.mult)
         for b in range(4):
             o, i_ = V("ht", b, 1024, 4), V("psd", 512 * b, 512 * b + M)
             if b % 2:
                 ts(o, i_, 0.5, OP.mult)
             else:
-                emit("a", lambda: g.scalar.activation(ap(o), ap(i_), ACT.Copy, scale=0.5), [o], [i_])
-        quant(V(ct, M, 2 * M), V(pt, M, 2 * M), V("ht"))
+                scale(o, i_, 0.5)
+        for u in range(2):
+            quant(V(ct, M + 128 * u, M + 128 * u + 128), V(pt, M + 128 * u, M + 128 * u + 128), V("ht", 512 * u, 512 * u + 512))
         if t + 1 < R:
             heights(t + 1)
-        pick(V("ct%d" % (t + 1), 0, M), V("pt%d" % (t + 1), 0, M), V(ct), V(pt), V("pl", 48, 64))
-        if t == 0:
-            quant(V("qw"), V("sw"), V("ws"))
+        for u in range(2):
+            pick(V("ct%d" % (t + 1), 128 * u, 128 * u + 128), V("pt%d" % (t + 1), 128 * u, 128 * u + 128), V(ct), V(pt), V("pl", 48 + 8 * u, 56 + 8 * u))
 
     ct, pt = "ct%d" % R, "pt%d" % R
     mm(V("psy", 0, M), V("qw"), V("sw"), V(ct, 0, M), V(pt, 0, M), True, True)
@@ -695,6 +729,7 @@ def rank_program(g, core, T, topo):
         dma("a", T.osc[4 * k:4 * k + 4, :], T[pt][32 * k:32 * k + 4, 0:M], "dout", ins=[V(pt, 0, M)])
     cp(V("yo"), V("psy", 0, M))
     dma("s", T.y[:], T.yo[:], "dout", ins=[V("yo")])
+    issue()
     for s_ in SEMAPHORES:
         if count[s_]:
             wait("g", s_, count[s_])

@@ -2,11 +2,12 @@ from concourse.bass import DstId, RemoteDMATransfer
 from concourse.mybir import dt, AluOpType, AxisListType, ActivationFunctionType
 
 N, M, K, J, R = 8, 256, 64, 3, 3
+H = K // 2
 F32, I32, U16, BF, CODE, PLANE = "float32", "int32", "uint16", "bfloat16", "float8_e4m3fn_x4", "uint8"
 NA = 7
 ND = 16 - NA
-NS = 7
-NC = 3
+NS = 6
+NC = 2
 DUMMY = 2200
 BIG = 2.0 ** 90
 ROUND32 = 1.5 * 2.0 ** 28
@@ -26,25 +27,24 @@ for _n, _w, _d in [
     ("xs", 1024, BF), ("us", 512, BF), ("ws", 512, BF), ("nbs", 48, I32), ("nbo", 16, U16), ("nbl", 48, U16),
     ("qu", 128, CODE), ("su", 128, PLANE), ("qw", 128, CODE), ("sw", 128, PLANE),
     ("et", 2048, BF), ("qe", 512, CODE), ("se", 512, PLANE), ("io128", 128, F32),
-    ("ci", 32, I32), ("cf", 32, F32), ("jr", 48, I32), ("tmpi", 160, I32), ("lst", 32, U16),
-    ("mk", MKW, BF), ("eqm", 16, BF), ("mt3", 768, BF), ("rs48", 192, BF), ("rst", 512, BF), ("sv", 256, F32),
-    ("qn", 224, F32), ("xx", 128, F32), ("on", 48, U16), ("ok", 48, U16),
-    ("hs", 12, F32), ("tbh", 224, F32), ("tbp", 224, F32), ("tbs", 224, F32), ("gn", 768, F32), ("tn", 768, F32), ("sn", 768, F32),
+    ("ci", 48, I32), ("cf", 32, F32), ("jr", 48, I32), ("tmpi", 160, I32), ("lst", 48, U16),
+    ("mk", MKW, BF), ("eqn", 2048, BF), ("z128", 128, BF), ("qd", 64, F32), ("mt3", 768, BF), ("rs24", 192, BF), ("rst", 512, BF), ("sv", 256, F32),
+    ("qn", 160, F32), ("xx", 96, F32), ("on", 48, U16), ("ni", 192, I32),
+    ("hs", 12, F32), ("tbh", 448, F32), ("tbp", 224, F32), ("tbs", 224, F32), ("gn", 768, F32), ("tn", 768, F32), ("sn", 384, F32),
     ("gm", 512, F32), ("tt", 512, F32), ("sp", 544, F32), ("mg", 512, BF), ("mt", 512, BF), ("oo", 32, U16), ("o2", 32, U16),
     ("o3", 16, U16), ("o4", 16, U16), ("ow", 16, U16), ("yb", 64, F32), ("rf", 256, F32), ("rt2", 256, F32), ("mgs", 256, BF),
     ("gs", 256, F32), ("tts", 256, F32), ("sps", 256, F32),
     ("ja", 256 * (NA + 1), BF), ("acc", 24, F32), ("qi", 64, I32), ("nn", 32, F32), ("nt", 32 * R, F32),
-    ("s1", 128, F32), ("sz", 128, F32), ("th0", 512, BF), ("th1", 512, BF), ("ctb", 224, BF), ("pf2", 224, F32),
-    ("vo", 16, U16), ("lw", 2480, F32), ("lt", 160, F32),
-    ("zo", 16, F32), ("zz", 40, F32), ("zs", 48, F32), ("pl", 80, U16), ("ht", 1024, BF), ("yo", 256, F32),
+    ("s1", 128, F32), ("sz", 16, F32), ("th0", 512, BF), ("th1", 512, BF), ("ctb", 224, BF), ("pf2", 224, F32),
+    ("vo", 16, U16), ("lw", 2480, F32), ("lt", 160, F32), ("zo", 32, F32), ("pl", 80, U16), ("ht", 1024, BF), ("yo", 256, F32),
 ]:
     _sb(_n, _w, _d)
 ALIAS = {}
 for _b, _d, _names in (
-        ("kc", F32, [("th", 16), ("c128", 32), ("cn", 32), ("mym", 16), ("dum", 16), ("rs8", 128), ("odd", 32), ("nodd", 32), ("zero", 16),
+        ("kc", F32, [("th", 16), ("c128", 32), ("cn", 32), ("mym", 16), ("dum", 16), ("odd", 32), ("nodd", 32), ("zero", 16), ("eq8", 16),
                      ("my8", 16), ("sv3", 48), ("sn3", 48), ("bm", 48), ("h1", 112)]),
-        ("wk", F32, [("so", 48), ("so2", 48), ("cs", 16), ("ch", 16), ("ff", 16), ("nf", 16), ("ho", 16),
-                     ("dd", 32), ("ds", 32), ("hm", 48), ("mx", 16), ("h0", 112), ("hz", 128), ("w1", 32), ("w2", 32), ("cv", 16),
+        ("wk", F32, [("so", 48), ("so2", 48), ("cs", 16), ("own", 48), ("ff", 16), ("nf", 16), ("ho", 16), ("hp", 16),
+                     ("dd", 32), ("ds", 32), ("hm", 48), ("h0", 112), ("hz", 128), ("w1", 32), ("w2", 32), ("cv", 16),
                      ("gw", 64), ("tw", 64), ("szh", 16), ("bb", 64), ("bt", 80), ("pfb", 48), ("df", 48), ("se0", 48), ("se1", 32),
                      ("fl", 32), ("k0", 64), ("k1", 64), ("k2", 64), ("tv", 64), ("qf", 96), ("cht", 64)]),
         ("wb", BF, [("zb", 256), ("ob", 256), ("mw", 64), ("nw", 64), ("jd", 256 * ND), ("js", 256 * ND)])):
@@ -54,22 +54,18 @@ for _b, _d, _names in (
         _o += _w
     _sb(_b, _o, _d)
 for _t in range(R):
-    _sb("qh%d" % _t, 32, F32)
+    _sb("qh%d" % _t, 16, F32)
     _sb("hl%d" % _t, 128, BF)
-    for _s in "abc":
-        _sb("c%s%d" % (_s, _t), 128, CODE)
-        _sb("p%s%d" % (_s, _t), 128, PLANE)
-    _sb("cr%d" % _t, 256, CODE)
-    _sb("pr%d" % _t, 256, PLANE)
+    for _s, _w in (("a", 160), ("b", 128), ("r", 256)):
+        _sb("c%s%d" % (_s, _t), _w, CODE)
+        _sb("p%s%d" % (_s, _t), _w, PLANE)
 for _t in range(R + 1):
     _sb("ct%d" % _t, 512, CODE)
     _sb("pt%d" % _t, 512, PLANE)
-SCRATCH["psh"] = ("psum", [128, 1024], F32)
-SCRATCH["psd"] = ("psum", [128, 2048], F32)
-SCRATCH["psy"] = ("psum", [128, 512], F32)
+SCRATCH["ps"] = ("psum", [128, 4096], F32)
 
-SEMAPHORES = ["kv", "ka", "kt", "kg", "ls", "dx", "du", "dw", "dn", "dh", "dout", "an"] + \
-    ["%s%d" % (_s, _t) for _s in ("ah", "az", "aa", "ab", "ac") for _t in range(R)]
+SEMAPHORES = ["kv", "ka", "kt", "kg", "ls", "dx", "du", "dw", "dn", "dm", "dh", "dout", "an"] + \
+    ["%s%d" % (_s, _t) for _s in ("ah", "az", "aa", "ab") for _t in range(R)]
 
 OP = AluOpType
 ACT = ActivationFunctionType
@@ -128,7 +124,7 @@ def rank_program(g, core, T, topo):
     def narrow(*xs):
         return all(SCRATCH[x[0]][2] in (BF, U16) for x in xs)
 
-    def add(q, call, outs, ins, cost, lat=HOP, sem=None, chain=False):
+    def add(q, call, outs, ins, cost, lat=HOP, sem=None, chain=False, ahead=0.0):
         outs, ins = flat(outs), flat(ins)
         pre = set()
         for regs, wr in ((ins, False), (outs, True)):
@@ -142,7 +138,7 @@ def rank_program(g, core, T, topo):
         for regs, wr in ((ins, False), (outs, True)):
             for x in regs:
                 hist.setdefault(x[0], []).append((x, wr, k))
-        ops.append({"q": q, "call": call, "pre": sorted(pre), "cost": cost, "lat": lat, "sem": sem, "chain": chain})
+        ops.append({"q": q, "call": call, "pre": sorted(pre), "cost": cost, "lat": lat, "sem": sem, "ahead": ahead, "chain": chain})
 
     def vcost(out, x, *more, k=1):
         if x[0] == "*":
@@ -150,7 +146,7 @@ def rank_program(g, core, T, topo):
         return CYCLE * max(64, k * size(x) * (0.5 if k == 1 and narrow(out, x, *more) else 1))
 
     def acost(x):
-        return 0.065 + 1.56 * CYCLE * size(x) if x[0] == "*" else 0.03 + CYCLE * size(x)
+        return 0.065 + 1.56 * CYCLE * size(x) if x[0] == "*" else 0.055 + CYCLE * size(x)
 
     def wait(q, sem, val):
         if known[q].get(sem, 0) < val:
@@ -168,7 +164,7 @@ def rank_program(g, core, T, topo):
             return 0.0 if ops[k]["chain"] and ops[j]["q"] == "t" else ops[j]["lat"]
         left = [0.0] * n
         for k in range(n - 1, -1, -1):
-            left[k] = ops[k]["cost"] + max([gap(k, j) + left[j] for j in post[k]] + [ops[k]["lat"]])
+            left[k] = ops[k]["ahead"] + ops[k]["cost"] + max([gap(k, j) + left[j] for j in post[k]] + [ops[k]["lat"]])
         need = [len(o["pre"]) for o in ops]
         ready = [0.0] * n
         cand = {q: [] for q in queues}
@@ -250,6 +246,12 @@ def rank_program(g, core, T, topo):
     def sign(out, a, bias, accum=None):
         add("a", lambda: g.scalar.activation(ap(out), ap(a), ACT.Sign, bias=ap(bias), accum_out=ap(accum)), [out, accum], [a, bias], acost(a) + 0.02)
 
+    def total_of(out, a, accum):
+        add("a", lambda: g.scalar.activation(ap(out), ap(a), ACT.Copy, accum_out=ap(accum)), [out, accum], [a], acost(a) + 0.02)
+
+    def shift(out, a, bias):
+        add("a", lambda: g.scalar.activation(ap(out), ap(a), ACT.Identity, bias=ap(bias)), [out], [a, bias], acost(a))
+
     def iota(out, pattern, base, mult):
         if SCRATCH[out[0]][2] == I32:
             add("g", lambda: g.iota(ap(out), pattern, base, mult), [out], [], 0.13 + 2 * CYCLE * size(out))
@@ -259,9 +261,9 @@ def rank_program(g, core, T, topo):
     def quant(c, s, a):
         add("v", lambda: g.vector.quantize_mx(ap(c), ap(s), ap(a)), [c, s], [a], 0.012 + 0.00022 * size(a))
 
-    def mm(out, lc, ls_, rc, rs, start, stop):
+    def mm(out, lc, ls_, rc, rs, start, stop, ahead=0.0):
         add("t", lambda: g.tensor.matmul_mx(ap(out), ap(lc), ap(ls_), ap(rc), ap(rs), start, stop), [out], [lc, ls_, rc, rs],
-            0.0006 * (size(rc) + 16), chain=not start)
+            0.0006 * (size(rc) + 16), chain=not start, ahead=ahead)
 
     def pick(oc_, op_, wc, wp, off):
         add("v", lambda: g.vector.tensor_copy(ap(oc_).bitcast(dt.uint32), ap(wc).bitcast(dt.uint32).indirect(ap(off))), [oc_], [wc, off],
@@ -285,20 +287,20 @@ def rank_program(g, core, T, topo):
     def split(src):
         i0 = cores.index(src)
         others = [cores[(i0 + k) % N] for k in range(1, N)]
-        near = [c for c in others if topo.chip(c) == topo.chip(src)]
+        near_ = [c for c in others if topo.chip(c) == topo.chip(src)]
         far = [c for c in others if topo.chip(c) != topo.chip(src)]
         mf_ = topo.mask(src, far[0])
         for c in far:
             mf_ &= topo.mask(src, c)
-        mn = topo.mask(src, near[0]) & ~mf_
-        return near, far, mn, mf_
+        mn = topo.mask(src, near_[0]) & ~mf_
+        return near_, far, mn, mf_
 
-    def allgather(src, buf, w, sem, lat=FAR):
+    def allgather(src, buf, w, sem, lat=FAR, cost=0.1):
         def call():
-            near, far, mn, mf_ = split(core)
+            near_, far, mn, mf_ = split(core)
             land = ap(V(buf, w * rank, w * rank + w))
             g.remote_dma_fused([RemoteDMATransfer(dst_ids=[dst(c) for c in cs_], dma_engine_mask=m, remote_sem=T.sem[sem],
-                                                  srcs=[ap(src)], dsts=[land for _ in cs_]) for cs_, m in ((far, mf_), (near, mn))],
+                                                  srcs=[ap(src)], dsts=[land for _ in cs_]) for cs_, m in ((far, mf_), (near_, mn))],
                                local_sem=T.sem.ls)
             count["ls"] += bits(mf_) + bits(mn)
             for c in cores:
@@ -307,36 +309,30 @@ def rank_program(g, core, T, topo):
                     count[sem] += bits(mn2) if core in n2 else bits(mf2)
             return sem, count[sem]
         others = [V(buf, a, b) for a, b in ((0, w * rank), (w * rank + w, w * N)) if a < b]
-        add("g", call, others, [src], 0.1, lat, sem)
+        add("g", call, others, [src], cost, lat, sem)
 
-    def swap(peer, cb, pb, sem):
+    def spread(moves, cb, pb, sem, lands, reads):
         def call():
-            rid, pid, _ = topo.addr(peer)
-            m = topo.mask(core, peer)
-            g.remote_dma(ap(V(cb, K, 2 * K)).bitcast(dt.uint8), ap(V(cb, 0, K)).bitcast(dt.uint8), T.sem[sem], T.sem.ls, pid, rid, m)
-            g.remote_dma(ap(V(pb, K, 2 * K)), ap(V(pb, 0, K)), T.sem[sem], T.sem.ls, pid, rid, m)
-            count["ls"] += 2 * bits(m)
-            count[sem] += 2 * bits(topo.mask(peer, core))
+            _, _, mn, mf_ = split(core)
+            en = [e for e in topo.engines(core, moves[1][0]) if mf_ >> e & 1]
+            masks = [mn, sum(1 << e for e in en[:len(en) // 2]), sum(1 << e for e in en[len(en) // 2:])]
+            for b_, view in ((cb, lambda x: ap(x).bitcast(dt.uint8)), (pb, ap)):
+                g.remote_dma_fused([RemoteDMATransfer(dst_ids=[dst(c)], dma_engine_mask=m, remote_sem=T.sem[sem],
+                                                      srcs=[view(V(b_, a, a + H))], dsts=[view(V(b_, b, b + H))])
+                                    for (c, a, b), m in zip(moves, masks)], local_sem=T.sem.ls)
+            count["ls"] += 2 * sum(bits(m) for m in masks)
+            count[sem] += 2 * sum(bits(m) for m in masks)
             return sem, count[sem]
-        add("g", call, [V(cb, K, 2 * K), V(pb, K, 2 * K)], [V(cb, 0, K), V(pb, 0, K)], 0.2, FAR, sem)
+        add("g", call, [V(b_, a, a + H) for b_ in (cb, pb) for a in lands], [V(b_, *reads) for b_ in (cb, pb)], 0.2, FAR + 0.2, sem)
 
     me = topo.chip(core)
-    peer_a = [c for c in cores if c != core and topo.chip(c) == me][0]
-    peer_b = [c for c in cores if topo.mates(topo.chip(c), me) and topo.die(c) == topo.die(core)][0]
-    peer_c = [c for c in cores if topo.same_plane(topo.chip(c), me) and topo.die(c) == topo.die(core)][0]
-    set_a = [cores.index(peer_a)]
-    set_b = [k for k in range(N) if topo.chip(cores[k]) == topo.chip(peer_b)]
-    set_c = [k for k in range(N) if topo.chip(cores[k]) not in (me, topo.chip(peer_b))]
-    for s_ in (set_a, set_b, set_c):
-        assert s_ == list(range(s_[0], s_[0] + len(s_)))
-
-    def shift_at_once(dst_, src):
-        cp(dst_(2, 64, 128), src(0, 64), "v")
-        cp(dst_(2, 0, 64), src(64, 128), "a")
-        for m in (1, 3):
-            for a in range(4):
-                b = (a + m) % 4
-                cp(dst_(m, 32 * b, 32 * b + 32), src(32 * a, 32 * a + 32), "a" if a % 2 else "v")
+    half = rank % 2
+    near = [c for c in cores if c != core and topo.chip(c) == me][0]
+    mate = sorted([c for c in cores if topo.mates(topo.chip(c), me)], key=lambda c: cores.index(c) % 2 != half)
+    plane = sorted([c for c in cores if topo.same_plane(topo.chip(c), me)], key=lambda c: cores.index(c) % 2 != half)
+    set_c = [k for k in range(N) if topo.chip(cores[k]) not in (me, topo.chip(mate[0]))]
+    assert set_c == list(range(set_c[0], set_c[0] + len(set_c))) and cores.index(near) // 2 == rank // 2
+    assert len(mate) == 2 and len(plane) == 2 and cores.index(mate[0]) // 2 == cores.index(mate[1]) // 2
 
     def turn(place, src, nc):
         tr(place(0, 0), src)
@@ -357,12 +353,11 @@ def rank_program(g, core, T, topo):
     dma("s", T.us[:], T.u[:], "du", [V("us")], lat=1.9)
 
     CI = {n: V("ci", k, k + 1) for k, n in enumerate(
-        ["p", "i", "g", "h", "lo", "hi", "r", "e", "i1", "i2", "i3", "ne", "u3", "t0", "t1", "t2", "t3", "t5", "t7", "t8", "t9",
-         "s0", "s1", "s2", "s3", "s4", "s5"])}
+        ["p", "i", "g", "h", "lo", "hi", "r", "e", "i1", "i2", "i3", "ne", "t2", "t3", "t7", "t8", "t9",
+         "s0", "s1", "s2", "s3", "s4", "s5", "n3", "n4", "n5", "n6"])}
     CF = {n: V("cf", k, k + 1) for k, n in enumerate(
-        ["p", "i", "g", "h", "lo", "hi", "r", "coff", "base", "sO", "g256", "sZ", "cC", "t0", "t1"])}
-    LNB, LO, LK, L3, LZ, LQ, LCH, LF, LH = [V("lst", a, b) for a, b in (
-        (0, 1), (2, 5), (6, 9), (10, 13), (14, 22), (22, 23), (24, 25), (26, 27), (28, 29))]
+        ["p", "i", "g", "h", "lo", "hi", "r", "coff", "base", "sO", "cC", "t0", "t1", "coff2", "bin"])}
+    LO, LY, L3, LQ, LF, LH, LD = [V("lst", a, b) for a, b in ((2, 5), (6, 7), (10, 13), (22, 23), (26, 27), (28, 29), (40, 42))]
     AND, SHR = OP.bitwise_and, OP.logical_shift_right
     io32 = V("io128", 0, 32)
     iota(CI["p"], [[0, 1]], 0, 1)
@@ -377,17 +372,21 @@ def rank_program(g, core, T, topo):
     ts(CI["lo"], P, 5, SHR, 1, AND)
     ts(CI["hi"], P, 6, SHR)
     ts(CI["r"], P, 31, AND)
-    ts(CI["t0"], CI["i"], 5.0, OP.min, 16.0, OP.mult)
-    ts(CI["u3"], CI["i"], 3.0, OP.is_ge, -40.0, OP.mult)
     cp(V("cf", 0, 7), V("ci", 0, 7))
     ts(CI["e"], P, 1, AND)
-    tt(CI["t1"], CI["t0"], CI["u3"], OP.add)
     ts(V("mk", 0, 31), V("io128", 0, 31), CF["i"], OP.is_lt)
-    ts(V("eqm"), V("io128", 0, 16), CF["i"], OP.not_equal, -BIG, OP.mult)
-    ts(LNB, CI["t1"], CF["g"], OP.add)
+    ts(V("eq8", 0, 8), V("io128", 0, 16, 2), CF["i"], OP.not_equal, -BIG, OP.mult)
+    fill(V("z128"), 0.0)
+    for k in range(16):
+        if k % 2:
+            shift(V("eqn", 128 * k, 128 * k + 128), V("z128"), V("eq8", k % 8, k % 8 + 1))
+        else:
+            ts(V("eqn", 128 * k, 128 * k + 128), V("z128"), V("eq8", k % 8, k % 8 + 1), OP.add)
     fill(V("mk", 31, 32), 1.0)
-    for b_ in ("xx", "tbh", "tbp", "tbs", "ctb", "h0", "hz", "tv", "nn", "zo", "zero", "k0"):
+    for b_ in ("xx", "tbp", "tbs", "qd", "ctb", "h0", "hz", "tv", "nn", "zo", "zero", "k0"):
         fill(V(b_), 0.0)
+    for c_ in (0, 224):
+        fill(V("tbh", c_, c_ + 224), 0.0)
     for c_ in (271, 543):
         fill(V("sp", c_, c_ + 1), 0.0)
     w_ = 32
@@ -397,29 +396,38 @@ def rank_program(g, core, T, topo):
         w_ += n_
     ts(CF["t0"], CI["hi"], -64.0, OP.mult, 96.0, OP.add)
     tt(CI["ne"], CI["e"], CI["h"], OP.not_equal)
-    ts(CI["t2"], CI["h"], -32.0, OP.mult, 128.0, OP.add)
+    ts(CI["t2"], CI["h"], -32.0, OP.mult, 96.0, OP.add)
     tt(CI["t3"], CI["i"], CI["e"], OP.subtract)
     ts(CF["coff"], CI["lo"], -32.0, OP.mult, CF["t0"], OP.add)
     tt(CI["t2"], CI["t2"], CI["ne"], OP.mult)
     tt(CI["t3"], CI["t3"], CI["h"], OP.add)
     tt(CF["sO"], CI["t2"], CI["t3"], OP.add)
     ts(LO, V("jr", 0, 3), 16.0, OP.mult, CF["sO"], OP.add)
-    ts(LK, LO, 48.0, OP.add)
+    ts(CI["n3"], CI["t3"], 5.0, OP.min)
+    ts(CI["n4"], CI["t3"], 3.0, OP.is_ge, 3.0, OP.mult)
+    ts(CI["n5"], CI["e"], 3.0, OP.mult)
+    tt(CI["n3"], CI["n3"], CI["n4"], OP.add)
+    tt(CI["n3"], CI["n3"], CI["n5"], OP.add)
+    cp(LY, CI["n3"])
+    ts(CI["n6"], P, 7, AND)
+    ts(V("lst", 40, 41), CI["n6"], 0.0, OP.add)
+    ts(V("lst", 41, 42), CI["n6"], 8.0, OP.add)
+    ts(CF["coff2"], CF["coff"], 2.0, OP.mult)
     ts(V("tmpi", 96, 99), V("jr", 0, 3), 16.0, OP.mult, CF["i"], OP.add)
     ts(L3, V("tmpi", 96, 99), -1.0, OP.add, 1.0 / 3, OP.mult)
     ts(CF["t1"], P, 32.0, OP.mult)
     ts(V("sn3"), V("sv3"), 128.0, OP.mult, CF["p"], OP.add)
     ts(V("sv3"), V("sv3"), CF["t1"], OP.add)
     cp(V("h1", 6, 112, 7), V("sv3", 0, 48, 3))
-    for b_, n_, hi_, lo_ in (("rs48", 48, 2 * BIG, -2 * BIG), ("rst", 16, 1.0, 0.0), ("rs8", 8, 1.0, 0.0)):
+    fill(V("h1", 5, 112, 7), 0.0)
+    for b_, n_, hi_, lo_ in (("rs24", 24, 2 * BIG, -2 * BIG), ("rst", 16, 1.0, 0.0)):
         fill(V(b_), hi_)
         fill(V(b_, 0, None, n_), lo_)
-    ts(CI["t5"], P, 7, AND)
     ts(CI["i2"], P, 2, SHR, 1, AND)
-    ts(CI["t5"], CI["t5"], 16.0, OP.mult)
     fill(V("cn"), -4095.0 / 32)
     fill(V("ob"), 1.0)
     ts(CF["base"], P, 16.0, OP.mult)
+    ts(CF["bin"], P, 16.0, OP.mult, float(NA), OP.add)
     ts(V("th"), V("io128", 0, 16), CF["base"], OP.add, -1.0, OP.mult)
     ts(V("th"), V("th"), 0.5, OP.add)
     ts(CI["i1"], P, 1, SHR, 1, AND)
@@ -428,7 +436,6 @@ def rank_program(g, core, T, topo):
     ts(V("tmpi", 104, 112), V("jr", 0, 8), 1, SHR, 1, AND)
     ts(V("tmpi", 112, 120), V("jr", 0, 8), 2, SHR)
     ts(V("tmpi", 120, 128), V("jr", 0, 8), 1, AND)
-    tt(CF["sZ"], CI["t5"], CI["i3"], OP.add)
     tt(CI["s0"], CI["s0"], CI["ne"], OP.mult)
     tt(CI["s1"], CI["i1"], CI["lo"], OP.not_equal)
     tt(CI["s2"], CI["i2"], CI["hi"], OP.not_equal)
@@ -437,7 +444,6 @@ def rank_program(g, core, T, topo):
     ts(V("tmpi", 104, 112), V("tmpi", 104, 112), CF["lo"], OP.not_equal, 32.0, OP.mult)
     ts(V("tmpi", 112, 120), V("tmpi", 112, 120), CF["hi"], OP.not_equal, 64.0, OP.mult)
     ts(V("tmpi", 120, 128), V("tmpi", 120, 128), 128.0, OP.mult, CF["r"], OP.add)
-    ts(LZ, V("jr", 0, 8), 2.0, OP.mult, CF["sZ"], OP.add)
     tt(CI["s0"], CI["s0"], CI["i1"], OP.add)
     ts(CI["s1"], CI["s1"], 64.0, OP.mult)
     ts(CI["s2"], CI["s2"], 128.0, OP.mult)
@@ -446,20 +452,21 @@ def rank_program(g, core, T, topo):
     ts(CI["t7"], CI["e"], 32.0, OP.mult)
     tt(V("tmpi", 104, 112), V("tmpi", 104, 112), V("tmpi", 112, 120), OP.add)
     ts(V("tmpi", 120, 128), V("tmpi", 120, 128), float(M * rank), OP.add)
-    cp(LQ, CI["s0"])
-    ts(LCH, CI["s0"], 8.0, OP.mult, 7.0, OP.add)
+    ts(LQ, CI["s0"], 2.0, OP.mult, float(half), OP.add)
+    for k, o_ in enumerate((1 - half, 16 + half, 17 - half)):
+        ts(V("lst", 30 + 2 * k, 31 + 2 * k), CI["s0"], 2.0, OP.mult, float(o_), OP.add)
     tt(CI["s1"], CI["s1"], CI["s2"], OP.add)
     tt(CI["s5"], CI["s5"], CI["t7"], OP.add)
     tt(V("my8", 0, 8), V("tmpi", 104, 112), V("tmpi", 120, 128), OP.add)
     tt(CI["s1"], CI["s1"], CI["s3"], OP.add)
     cp(LH, CI["s5"])
-    ts(CF["g256"], CF["g"], 256.0, OP.mult)
     cp(LF, CI["s1"])
     ts(V("mym"), V("jr", 0, 16), 16.0, OP.mult, CF["i"], OP.add)
     ts(CI["t8"], CI["g"], float(set_c[0]), OP.is_ge, float(K), OP.mult)
     ts(CI["t9"], CI["g"], float(set_c[-1]), OP.is_le)
-    ts(V("sv", 128, 256), V("sv", 0, 128), 8.0, OP.add, CF["g256"], OP.add)
-    ts(V("sv", 0, 128), V("sv", 0, 128), CF["g256"], OP.add)
+    ts(V("sv", 128, 256), V("sv", 0, 128), 128.0, OP.is_gt, 128.0, OP.mult)
+    tt(V("sv", 0, 128), V("sv", 0, 128), V("sv", 128, 256), OP.add)
+    ts(V("sv", 128, 256), V("sv", 0, 128), 8.0, OP.add)
     ts(V("dum"), V("mym"), float(DUMMY), OP.add)
     tt(CF["cC"], CI["t8"], CI["t9"], OP.mult)
     fill(V("c128"), 128.0)
@@ -467,6 +474,7 @@ def rank_program(g, core, T, topo):
     ts(V("nodd"), io32, -2.0, OP.mult, -1.0, OP.add)
     fill(V("bt", 0, 1), 0.0)
     fill(V("k0", 3, 64, 4), 1.0)
+    fill(V("qn", 48, 64), 0.0)
     ts(V("pfb", 0, 1), P, float(32 - NS), OP.mult, 128.0 * NS, OP.add)
     ts(V("pfb", 33, 34), P, float(-NS), OP.mult, 128.0 * NS, OP.add)
     for b in range(4):
@@ -474,67 +482,75 @@ def rank_program(g, core, T, topo):
         ts(V("et", 512 * b + b, 512 * b + 512, 4), V("io128"), CF["p"], OP.is_equal)
         quant(V("qe", 128 * b, 128 * b + 128), V("se", 128 * b, 128 * b + 128), V("et", 512 * b, 512 * b + 512))
 
-    cp(V("nbs", p0=32, p1=64), V("nbs", p1=32))
-    cp(V("nbs", p0=64, p1=96), V("nbs", p1=32))
-    cp(V("nbs", p0=96), V("nbs", p1=32))
-    cp(V("so", 0, 16), IND(V("nbs"), LNB))
-    tt(V("so", 16, 18), V("so", 0, 6, 3), V("so", 1, 6, 3), OP.min)
-    tt(V("so", 18, 20), V("so", 0, 6, 3), V("so", 1, 6, 3), OP.max)
-    tt(V("so", 20, 22), V("so", 18, 20), V("so", 2, 6, 3), OP.min)
-    ts(V("nbo", 0, 1), V("so", 16, 17), V("so", 2, 3), OP.min)
-    ts(V("nbo", 3, 4), V("so", 17, 18), V("so", 5, 6), OP.min)
-    ts(V("nbo", 2, 3), V("so", 18, 19), V("so", 2, 3), OP.max)
-    ts(V("nbo", 5, 6), V("so", 19, 20), V("so", 5, 6), OP.max)
-    ts(V("nbo", 1, 2), V("so", 16, 17), V("so", 20, 21), OP.max)
-    ts(V("nbo", 4, 5), V("so", 17, 18), V("so", 21, 22), OP.max)
-    allgather(V("nbo", 0, 6), "nbl", 6, "an", FAR + 1.0)
-    quant(V("ct0", 0, 128), V("pt0", 0, 128), V("xs", 0, 512))
-    quant(V("ct0", 128, M), V("pt0", 128, M), V("xs", 512, 1024))
+    for a in range(4):
+        for e in range(2):
+            cp(V("so", e, 12, 2, 32 * a, 32 * a + 32), V("nbs", 2 * a + e, 48, 8, 0, 32))
+    tt(V("so", 16, 20), V("so", 0, 4), V("so", 4, 8), OP.min)
+    tt(V("so", 20, 24), V("so", 0, 4), V("so", 4, 8), OP.max)
+    tt(V("so", 24, 28), V("so", 20, 24), V("so", 8, 12), OP.min)
+    tt(V("so", 32, 44, 3), V("so", 16, 20), V("so", 8, 12), OP.min)
+    tt(V("so", 34, 44, 3), V("so", 20, 24), V("so", 8, 12), OP.max)
+    tt(V("so", 33, 44, 3), V("so", 16, 20), V("so", 24, 28), OP.max)
+    cp(V("nbo"), IND(V("so", 32, 44), LY))
+    allgather(V("nbo", 0, 6), "nbl", 6, "an", FAR, 1.1)
+    dma("s", ap(V("nbl", 6 * rank, 6 * rank + 6)), ap(V("nbo", 0, 6)), "dm", [V("nbl", 6 * rank, 6 * rank + 6)], [V("nbo", 0, 6)])
+    for u in range(2):
+        quant(V("ct0", M * u, M * u + 128), V("pt0", M * u, M * u + 128), V("xs", 512 * u, 512 * u + 512))
     quant(V("qu"), V("su"), V("us"))
 
     def products(t, c0):
         for u in range(2):
-            mm(V("psh", 512 * u, 512 * u + 128), V("ct%d" % t, c0 + 128 * u, c0 + 128 * u + 128), V("pt%d" % t, c0 + 128 * u, c0 + 128 * u + 128),
+            mm(V("ps", 2048 * u, 2048 * u + 128), V("ct%d" % t, c0 + M * u, c0 + M * u + 128), V("pt%d" % t, c0 + M * u, c0 + M * u + 128),
                V("qu"), V("su"), True, True)
+
+    def unpack(c, s, first, w):
+        for u in range(2):
+            for b in range(4):
+                mm(V("ps", 2048 * u + 512 * b, 2048 * u + 512 * b + 128), V("qe", 128 * b, 128 * b + 128), V("se", 128 * b, 128 * b + 128),
+                   V(c, w * u, w * u + 128), V(s, w * u, w * u + 128), first, not first, 0.0 if first else 0.1 * (7 - 4 * u - b))
 
     def heights(t):
         if t == 0:
             products(0, 0)
-            cp(V("hs", 0, 2), V("psh", 0, 1024, 512))
+            cp(V("hs", 0, 2), V("ps", 0, 2049, 2048))
         else:
-            products(t - 1, M)
+            products(t - 1, 128)
             for u in range(2):
-                ts(V("hs", 4 * t + u, 4 * t + u + 1), V("psh", 512 * u + t, 512 * u + t + 1), V("ff", u, u + 1), OP.mult, V("ho", u, u + 1), OP.add)
+                ts(V("hs", 4 * t + u, 4 * t + u + 1), V("ps", 2048 * u + t, 2048 * u + t + 1), V("ff", u, u + 1), OP.mult, V("ho", u, u + 1), OP.add)
         mine, own = V("hs", 4 * t, 4 * t + 2), V("qh%d" % t, 2 * rank, 2 * rank + 2)
-        allgather(mine, "qh%d" % t, 2, "ah%d" % t)
+        allgather(mine, "qh%d" % t, 2, "ah%d" % t, FAR if t else FAR + 0.4)
         dma("s", ap(own), ap(mine), "dh", [own], [mine])
 
     heights(0)
     dma("s", T.ws[:], T.w[:], "dw", [V("ws")], [V("hs", 0, 2)], lat=2.0)
     quant(V("qw"), V("sw"), V("ws"))
 
-    for a, b in ((0, 6 * rank), (6 * rank + 6, 48)):
-        if a < b:
-            cp(V("tmpi", a, b), V("nbl", a, b))
-    cp(V("tmpi", 6 * rank, 6 * rank + 6), V("nbo", 0, 6))
+    for k in range(4):
+        cp(V("mt3", 192 * k, 192 * k + 192), IND(V("eqn"), V("nbl", 12 * k, 12 * k + 12)), "a")
+    cp(V("ni", 0, 48), V("nbl"))
+    ts(V("ni", 48, 96), V("ni", 0, 48), 127, AND)
+    ts(V("ni", 96, 144), V("ni", 0, 48), 96, AND)
+    ts(V("ni", 144, 192), V("ni", 0, 48), 5, SHR, 32, AND)
+    ts(V("qf", 0, 48), V("ni", 48, 96), CF["coff2"], OP.add)
+    tt(V("hm"), V("ni", 96, 144), V("ni", 144, 192), OP.add)
+    tt(V("qf", 0, 48), V("qf", 0, 48), V("hm"), OP.add)
+    cp(V("on"), V("qf", 0, 48))
+    cp(V("qn", 0, 48), V("nbl"))
+    tr(V("xx", 16, 80), V("qn", 0, 64))
+    tr(V("qn", 64, 160), V("xx"))
+    cp(V("tmpi", 0, 48), IND(V("qn"), LO))
+    ops[-1]["ahead"] = 2.0
     ts(V("tmpi", 48, 96), V("tmpi", 0, 48), 127, AND)
     ts(V("qi", 0, 48), V("tmpi", 0, 48), 7, SHR)
-    cp(V("qn", 48, 96), V("qi", 0, 48))
-    cp(V("qn", 0, 48), V("tmpi", 48, 96))
     tt(V("bm"), V("tmpi", 0, 48), V("sn3"), OP.is_lt)
-    tr(V("xx", 16, 112), V("qn", 0, 96))
-    ts(V("so2"), V("qn", 0, 48), 32.0, OP.mult)
-    tr(V("qn", 96, 224), V("xx"))
-    tt(V("so2"), V("so2"), V("qn", 48, 96), OP.add)
-    cp(V("ok"), IND(V("qn"), LK))
-    ts(V("on"), IND(V("qn"), LO), CF["coff"], OP.add)
-    for k in range(4):
-        cp(V("mt3", 192 * k, 192 * k + 192), IND(V("eqm"), V("ok", 12 * k, 12 * k + 12)), "a")
-    tt(V("so2"), V("so2"), V("sv3"), OP.subtract)
-    ts(V("bm"), V("bm"), -BIG, OP.mult)
+    ts(V("so2"), V("tmpi", 48, 96), 32.0, OP.mult)
+    tt(V("so"), V("qi", 0, 48), V("sv3"), OP.subtract)
+    tt(V("so2"), V("so2"), V("so"), OP.add)
+    scale(V("bm"), V("bm"), -BIG)
     for j in range(J):
-        cp(V("h1", 5 - 2 * j, 112, 7), V("so2", j, 48, 3))
-        ts(V("h1", 4 - 2 * j, 112, 7), V("so2", j, 48, 3), -1.0, OP.mult)
+        cp(V("h1", 4 - 2 * j, 112, 7), V("so2", j, 48, 3), "a")
+        if j < J - 1:
+            scale(V("h1", 3 - 2 * j, 112, 7), V("so2", j, 48, 3), -1.0)
 
     def lookup(src, c0, s, d, pieces):
         for a, b, q in pieces:
@@ -567,19 +583,20 @@ def rank_program(g, core, T, topo):
 
     for t in range(R):
         ct, pt, qh, hl = "ct%d" % t, "pt%d" % t, "qh%d" % t, "hl%d" % t
-        cp(V(qh, 16, 32), V(qh, 0, 16))
-        tt(V("hm"), IND(V(qh, 0, 16), L3), V("bm"), OP.add)
-        table("tbh", V(qh))
-        for k in range(4):
-            gn, tn, sn, mt3 = [V(n_, 192 * k, 192 * k + 192) for n_ in ("gn", "tn", "sn", "mt3")]
-            tt(gn, IND(V("tbh"), V("on", 12 * k, 12 * k + 12)), mt3, OP.add)
+        cp(V("qd", 0, 64, 2), IND(V(qh), LD))
+        tt(V("hm"), IND(V(qh), L3), V("bm"), OP.add)
+        turn(lambda a, b: V("tbh", 192 + 64 * (a - b), 256 + 64 * (a - b)), V("qd"), 1)
+        for k in range(2):
+            gn, tn, mt3 = [V(n_, 384 * k, 384 * k + 384) for n_ in ("gn", "tn", "mt3")]
+            tt(gn, IND(V("tbh"), V("on", 24 * k, 24 * k + 24)), mt3, OP.add)
             tr(tn, gn)
-            scan(sn, V("rs48"), tn, OP.min, OP.max)
-        tt(V("mx"), V("sn", 47, 768, 48), V(qh, 0, 16), OP.max)
+            scan(V("sn", 192 * k, 192 * k + 192), V("rs24"), V("tn", 384 * k, 384 * k + 384, 2), OP.min, OP.max)
+        top = V("sn", 23, 384, 24)
+        tt(V("h0", 6, 112, 7), V(qh), top, OP.is_le)
         for j in range(J):
-            tt(V("h0", 6 - 2 * j, 112, 7), V("hm", j, 48, 3), V("mx"), OP.is_lt)
-        for j in range(J):
-            tt(V("h0", 5 - 2 * j, 112, 7), V("sn", 16 * j + 15, 768, 48), V("mx"), OP.is_lt)
+            tt(V("h0", 5 - 2 * j, 112, 7), V("hm", j, 48, 3), top, OP.is_lt)
+        for j in range(J - 1):
+            tt(V("h0", 4 - 2 * j, 112, 7), V("sn", 8 * j + 7, 384, 24), top, OP.is_lt)
         scan(V("hz", 0, 112), V("h0"), V("h1"), OP.mult, OP.add)
         for step in range(6):
             src = ("hz", 6, 7) if step == 0 else ("sp", 272 + 15, 16)
@@ -593,11 +610,12 @@ def rank_program(g, core, T, topo):
         ts(V("cv", 2, 4), V("w2", 15, 32, 16), 128.0, OP.mult)
         for u in range(2):
             ts(V("yb", 32 * u, 32 * u + 32), V("cn"), V("cv", u, u + 1), OP.mult, V("cv", 2 + u, 3 + u), OP.add)
-        turn(lambda a, b: V("rf", 64 * (a ^ b), 64 * (a ^ b) + 64), V("yb"), NC)
+        turn(lambda a, b: V("rf", 64 * (a ^ b), 64 * (a ^ b) + 64), V("yb"), 1)
         ts(V("zb"), V("rf"), CF["base"], OP.subtract)
         for k in range(NA + 1):
             sign(V("ja", 256 * k, 256 * k + 256), V("rf"), V("th", k, k + 1), V("acc", k, k + 1))
-        for k in range(ND):
+        ts(V("jd", 0, 256), V("rf"), CF["bin"], OP.is_equal, 2.0, OP.mult)
+        for k in range(1, ND):
             ts(V("jd", 256 * k, 256 * k + 256), V("zb"), float(NA + k), OP.is_equal, 2.0, OP.mult)
         for k in range(ND):
             scan(V("js", 256 * k, 256 * k + 256), V("ob"), V("jd", 256 * k, 256 * k + 256), OP.mult, OP.add)
@@ -622,16 +640,17 @@ def rank_program(g, core, T, topo):
             ts(V("o4", e, 16, 2), V("qf", 48, 56), 16.0, OP.add)
         for k in range(2):
             cp(V("mgs", 128 * k, 128 * k + 128), IND(V("mk", 0, 64), V("o4", 8 * k, 8 * k + 8)), "a")
-        cp(V("s1", 64, 128), IND(V(hl), V("lst", 18, 22)), "a")
-        cp(V("s1", 0, 64), IND(V(hl), V("lst", 14, 18)))
-        for k in range(2):
-            scan(V("sz", 64 * k, 64 * k + 64), V("rs8", 0, 64), V("s1", 64 * k, 64 * k + 64), OP.mult, OP.add)
-        ts(V("szh"), V("sz", 7, 128, 8), 0.5, OP.mult)
         for k in range(16):
             if k < 16 - NS:
-                ts(V("th0", k, 512, 16), V("odd"), V("sz", 8 * k + 7, 8 * k + 8), OP.is_lt, 2.0, OP.mult)
+                red(V("sz", k, k + 1), V(hl, k, 128, 16), OP.add)
             else:
-                sign(V("th0", k, 512, 16), V("nodd"), V("sz", 8 * k + 7, 8 * k + 8))
+                total_of(V("s1", 8 * k, 8 * k + 8), V(hl, k, 128, 16), V("sz", k, k + 1))
+        ts(V("szh"), V("sz"), 0.5, OP.mult)
+        for k in range(16):
+            if k < 16 - NS:
+                ts(V("th0", k, 512, 16), V("odd"), V("sz", k, k + 1), OP.is_lt, 2.0, OP.mult)
+            else:
+                sign(V("th0", k, 512, 16), V("nodd"), V("sz", k, k + 1))
         scan(V("th1"), V("rst"), V("th0"), OP.mult, OP.add)
         table("ctb", V("th1", 15, 512, 16))
         scan(V("pf2"), V("ob", 0, 224), V("ctb"), OP.mult, OP.add, 128.0 * NS)
@@ -639,7 +658,8 @@ def rank_program(g, core, T, topo):
         ts(V("bb", 0, 32), V("c128"), total, OP.is_ge)
         ts(V("bb", 32, 64), V("c128"), total, OP.is_ge, total, OP.mult)
         tr(V("pfb", 1, 33), V("pf2", 95, 127))
-        tr(V("bt", 1, 65), V("bb"))
+        tr(V("bt", 1, 33), V("bb", 0, 32))
+        tr(V("bt", 33, 65), V("bb", 32, 64))
         tt(V("df", 0, 33), V("pfb", 0, 33), V("pfb", 1, 34), OP.subtract)
         red(V("cs", 0, 1), V("bt", 1, 33), OP.add)
         scan(V("se0", 0, 33), V("bt", 0, 33), V("df", 0, 33), OP.mult, OP.add)
@@ -660,31 +680,30 @@ def rank_program(g, core, T, topo):
         val = V("k2", 3, 64, 4)
         ts(V("vo"), val, 15.0, OP.add)
         add("v", lambda: g.vector.tensor_copy(ap(IND(V("lw"), V("vo"))), ap(V("sv"))), [V("lw")], [V("sv"), V("vo")], 0.05 + 3.8 * CYCLE * 256)
-        a0, h0 = 32 * (rank // 2), 16 * (rank % 2)
         tr(V("lt", 0, 64), V("lw", 16, 80))
         tr(V("lt", 64, 160), V("lw", 0, 96))
-        for a in range(4):
-            cp(V("zo", 0, 5, 1, 32 * a, 32 * a + 32), V("lt", h0, 160, 32, a0, a0 + 32), "a" if a % 2 else "v")
-        ts(V("pl", 0, 16), IND(V("zo"), LQ), float(-1 - M * rank), OP.add)
-        ca, pa, cb, pb, cc_, pc_ = ["%s%s%d" % (x, s_, t) for s_ in "abc" for x in "cp"]
-        pick(V(ca, 0, K), V(pa, 0, K), V(ct, 0, M), V(pt, 0, M), V("pl", 0, 4))
-        swap(peer_a, ca, pa, "aa%d" % t)
-        for b in range(4):
-            mm(V("psd", 512 * b, 512 * b + M), V("qe", 128 * b, 128 * b + 128), V("se", 128 * b, 128 * b + 128), V(ct, 0, M), V(pt, 0, M), True, False)
-        cp(V("zz", 0, 40, 4), V("lt", 0, 160, 16))
-        shift_at_once(lambda m, a, b: V("zz", m, 40, 4, a, b), lambda a, b: V("lt", 0, 160, 16, a, b))
-        scan(V("zs", 0, 40), V("rs8", 0, 40), V("zz"), OP.mult, OP.add)
-        cp(V("ch"), IND(V("zs", 0, 40), LCH))
-        for k, s_ in enumerate((set_a, set_b)):
-            ts(V("cht", 8 * k, 8 * k + 4), V("ch", 0, 4), float(M * s_[0] + 1), OP.is_ge, float(K), OP.mult)
-            ts(V("cht", 8 * k + 4, 8 * k + 8), V("ch", 0, 4), float(M * (s_[-1] + 1) + 1), OP.is_ge, float(-K), OP.mult)
-            tt(V("cht", 8 * k, 8 * k + 4), V("cht", 8 * k, 8 * k + 4), V("mym", 0, 4), OP.add)
-            tt(V("cht", 8 * k, 8 * k + 4), V("cht", 8 * k, 8 * k + 4), V("cht", 8 * k + 4, 8 * k + 8), OP.add)
-            cp(V("pl", 16 + 4 * k, 20 + 4 * k), V("cht", 8 * k, 8 * k + 4))
-        pick(V(cb, 0, K), V(pb, 0, K), V(ca), V(pa), V("pl", 16, 20))
-        swap(peer_b, cb, pb, "ab%d" % t)
-        pick(V(cc_, 0, K), V(pc_, 0, K), V(cb), V(pb), V("pl", 20, 24))
-        swap(peer_c, cc_, pc_, "ac%d" % t)
+        for k, a0 in enumerate((32 * (rank // 2), 32 * (cores.index(mate[0]) // 2))):
+            for a in range(4):
+                cp(V("zo", 16 * k, 16 * k + 10, 1, 32 * a, 32 * a + 32), V("lt", 0, 160, 16, a0, a0 + 32), "a" if a % 2 else "v")
+        ts(V("pl", 0, 16), IND(V("zo", 0, 16), LQ), -1.0, OP.add)
+        ca, pa, cc_, pc_, cr, pr = ["%s%s%d" % (x, s_, t) for s_ in "abr" for x in "cp"]
+        pick(V(ca, 0, K), V(pa, 0, K), V(ct, 0, M + 128), V(pt, 0, M + 128), V("pl", 0, 4))
+        spread([(near, H * (1 - half), 2 * H), (mate[0], H * half, 3 * H), (mate[1], H * (1 - half), 4 * H)], ca, pa, "aa%d" % t, (2 * H, 3 * H, 4 * H), (0, K))
+        if t + 1 < R:
+            if t:
+                products(t, 0)
+            cp(V("hp", 0, 2), V("ps", t + 1, 2048 + t + 2, 2048))
+        unpack(ct, pt, True, M)
+        for k in range(3):
+            ts(V("own", 16 * k, 16 * k + 16), IND(V("zo"), V("lst", 30 + 2 * k, 31 + 2 * k)), 0.5, OP.is_gt, float(H * (2 + k - half)), OP.mult)
+        c0 = 2 * half
+        tt(V("cht", 0, 2), V("own", c0, c0 + 2), V("mym", c0, c0 + 2), OP.add)
+        tt(V("cht", 2, 4), V("own", 16 + c0, 18 + c0), V("own", 32 + c0, 34 + c0), OP.add)
+        tt(V("cht", 4, 6), V("cht", 0, 2), V("cht", 2, 4), OP.add)
+        cp(V("pl", 16, 18), V("cht", 4, 6))
+        o_ = H * half
+        pick(V(cc_, o_, o_ + H), V(pc_, o_, o_ + H), V(ca), V(pa), V("pl", 16, 18))
+        spread([(near, o_, o_), (plane[0], o_, K + o_), (plane[1], o_, K + o_)], cc_, pc_, "ab%d" % t, (H - o_, K, K + H), (o_, o_ + H))
         ts(V("tv", 48, 64), val, 64.5, OP.is_lt)
         ts(V("tv", 32, 48), val, CF["cC"], OP.add)
         tt(V("tv", 0, 16), V("tv", 32, 48), V("tv", 48, 64), OP.mult)
@@ -697,38 +716,40 @@ def rank_program(g, core, T, topo):
             tr(tts, gs)
             scan(sps, V("rst", 0, 128), tts, OP.mult, OP.add)
         ts(V("pl", 32, 48), IND(V("sps"), LF), -1.0, OP.add)
-        ts(V("cht", 48, 64), IND(V("sps"), LF), 0.5, OP.is_gt, float(M), OP.mult)
-        tt(V("cht", 16, 32), V("cht", 48, 64), V("mym"), OP.add)
+        ts(V("cht", 48, 64), IND(V("sps"), LF), 0.5, OP.is_gt, 128.0, OP.mult)
+        for u in range(2):
+            tt(V("cht", 16 + 8 * u, 24 + 8 * u), V("cht", 48 + 8 * u, 56 + 8 * u), V("mym", 0, 8), OP.add)
         cp(V("pl", 48, 64), V("cht", 16, 32))
         if t + 1 < R:
-            products(t, 0)
             ts(V("ff"), IND(V("sps"), LH), 0.5, OP.is_gt)
             ts(V("nf"), IND(V("sps"), LH), 0.5, OP.is_lt)
-            tt(V("ho", 0, 2), V("psh", t + 1, 1024, 512), V("nf", 0, 2), OP.mult)
-        cr, pr = "cr%d" % t, "pr%d" % t
-        pick(V(cr), V(pr), V(cc_), V(pc_), V("pl", 32, 48))
-        for b in range(4):
-            mm(V("psd", 512 * b, 512 * b + M), V("qe", 128 * b, 128 * b + 128), V("se", 128 * b, 128 * b + 128), V(cr), V(pr), False, True)
-        for b in range(4):
-            o, i_ = V("ht", b, 1024, 4), V("psd", 512 * b, 512 * b + M)
-            if b % 2:
-                ts(o, i_, 0.5, OP.mult)
-            else:
-                scale(o, i_, 0.5)
+            tt(V("ho", 0, 2), V("hp", 0, 2), V("nf", 0, 2), OP.mult)
         for u in range(2):
-            quant(V(ct, M + 128 * u, M + 128 * u + 128), V(pt, M + 128 * u, M + 128 * u + 128), V("ht", 512 * u, 512 * u + 512))
+            pick(V(cr, 128 * u, 128 * u + 128), V(pr, 128 * u, 128 * u + 128), V(cc_), V(pc_), V("pl", 32 + 8 * u, 40 + 8 * u))
+        unpack(cr, pr, False, 128)
+        for u in range(2):
+            for b in range(4):
+                o, i_ = V("ht", 512 * u + b, 512 * u + 512, 4), V("ps", 2048 * u + 512 * b, 2048 * u + 512 * b + 128)
+                if b % 2:
+                    ts(o, i_, 0.5, OP.mult)
+                else:
+                    scale(o, i_, 0.5)
+            quant(V(ct, M * u + 128, M * u + M), V(pt, M * u + 128, M * u + M), V("ht", 512 * u, 512 * u + 512))
         if t + 1 < R:
             heights(t + 1)
         for u in range(2):
-            pick(V("ct%d" % (t + 1), 128 * u, 128 * u + 128), V("pt%d" % (t + 1), 128 * u, 128 * u + 128), V(ct), V(pt), V("pl", 48 + 8 * u, 56 + 8 * u))
+            w_ = M if t + 1 < R else 128
+            pick(V("ct%d" % (t + 1), w_ * u, w_ * u + 128), V("pt%d" % (t + 1), w_ * u, w_ * u + 128), V(ct, M * u, M * u + M), V(pt, M * u, M * u + M),
+                 V("pl", 48 + 8 * u, 56 + 8 * u))
 
     ct, pt = "ct%d" % R, "pt%d" % R
-    mm(V("psy", 0, M), V("qw"), V("sw"), V(ct, 0, M), V(pt, 0, M), True, True)
-    dma("s", T.oc[:], ap(V(ct, 0, M)).bitcast(dt.uint8), "dout", ins=[V(ct, 0, M)])
+    for u in range(2):
+        mm(V("ps", 2048 * u, 2048 * u + 128), V("qw"), V("sw"), V(ct, 128 * u, 128 * u + 128), V(pt, 128 * u, 128 * u + 128), True, True)
+        cp(V("yo", 128 * u, 128 * u + 128), V("ps", 2048 * u, 2048 * u + 128), "v" if u else "a")
+        dma("s", T.oc[:, 512 * u:512 * u + 512], ap(V(ct, 128 * u, 128 * u + 128)).bitcast(dt.uint8), "dout", ins=[V(ct, 128 * u, 128 * u + 128)])
+        dma("s", T.y[:, 128 * u:128 * u + 128], T.yo[:, 128 * u:128 * u + 128], "dout", ins=[V("yo", 128 * u, 128 * u + 128)])
     for k in range(4):
-        dma("a", T.osc[4 * k:4 * k + 4, :], T[pt][32 * k:32 * k + 4, 0:M], "dout", ins=[V(pt, 0, M)])
-    cp(V("yo"), V("psy", 0, M))
-    dma("s", T.y[:], T.yo[:], "dout", ins=[V("yo")])
+        dma("s", T.osc[4 * k:4 * k + 4, :], T[pt][32 * k:32 * k + 4, 0:M], "dout", ins=[V(pt, 0, M)])
     issue()
     for s_ in SEMAPHORES:
         if count[s_]:

from concourse.bass import DstId, RemoteDMATransfer
from concourse.mybir import dt, AluOpType, AxisListType, ActivationFunctionType

N, M, K, J, R = 8, 256, 64, 3, 3
H = K // 2
F32, I32, U16, BF, CODE, PLANE = "float32", "int32", "uint16", "bfloat16", "float8_e4m3fn_x4", "uint8"
NA = 7
ND = 16 - NA
NS = 6
NC = 2
DUMMY = 2200
BIG = 2.0 ** 90
ROUND32 = 1.5 * 2.0 ** 28
MKW = 4128
HOP, FAR, LOCAL, CYCLE = 0.235, 1.4, 1.3, 0.00083
PIECES_R = ((0, 128, "v"), (128, 256, "a"))
PIECES_W = ((0, 128, "v"), (128, 256, "v"))

SCRATCH = {}


def _sb(name, n, d):
    SCRATCH[name] = ("sbuf", [128, n], d)


for _n, _w, _d in [
    ("xs", 1024, BF), ("us", 512, BF), ("ws", 512, BF), ("nbs", 48, I32), ("nbo", 16, U16), ("nbl", 48, U16),
    ("qu", 128, CODE), ("su", 128, PLANE), ("qw", 128, CODE), ("sw", 128, PLANE),
    ("et", 2048, BF), ("qe", 512, CODE), ("se", 512, PLANE), ("io128", 128, F32),
    ("ci", 48, I32), ("cf", 32, F32), ("jr", 48, I32), ("tmpi", 160, I32), ("lst", 48, U16),
    ("mk", MKW, BF), ("eqn", 2048, BF), ("z128", 128, BF), ("qd", 64, F32), ("mt3", 768, BF), ("rs24", 192, BF), ("rst", 512, BF), ("sv", 256, F32),
    ("qn", 160, F32), ("xx", 96, F32), ("on", 48, U16), ("ni", 192, I32),
    ("hs", 12, F32), ("tbh", 448, F32), ("tbp", 224, F32), ("tbs", 224, F32), ("gn", 768, F32), ("tn", 768, F32), ("sn", 384, F32),
    ("gm", 512, F32), ("tt", 512, F32), ("sp", 544, F32), ("mg", 512, BF), ("mt", 512, BF), ("oo", 32, U16), ("o2", 32, U16),
    ("o3", 16, U16), ("o4", 16, U16), ("ow", 16, U16), ("yb", 64, F32), ("rf", 256, F32), ("rt2", 256, F32), ("mgs", 256, BF),
    ("gs", 256, F32), ("tts", 256, F32), ("sps", 256, F32),
    ("ja", 256 * (NA + 1), BF), ("acc", 24, F32), ("qi", 64, I32), ("nn", 32, F32), ("nt", 32 * R, F32),
    ("s1", 128, F32), ("sz", 16, F32), ("th0", 512, BF), ("th1", 512, BF), ("ctb", 224, BF), ("pf2", 224, F32),
    ("vo", 16, U16), ("lw", 2480, F32), ("lt", 160, F32), ("zo", 32, F32), ("pl", 80, U16), ("ht", 1024, BF), ("yo", 256, F32),
]:
    _sb(_n, _w, _d)
ALIAS = {}
for _b, _d, _names in (
        ("kc", F32, [("th", 16), ("c128", 32), ("cn", 32), ("mym", 16), ("dum", 16), ("odd", 32), ("nodd", 32), ("zero", 16), ("eq8", 16),
                     ("my8", 16), ("sv3", 48), ("sn3", 48), ("bm", 48), ("h1", 112)]),
        ("wk", F32, [("so", 48), ("so2", 48), ("cs", 16), ("own", 48), ("ff", 16), ("nf", 16), ("ho", 16), ("hp", 16),
                     ("dd", 32), ("ds", 32), ("hm", 48), ("h0", 112), ("hz", 128), ("w1", 32), ("w2", 32), ("cv", 16),
                     ("gw", 64), ("tw", 64), ("szh", 16), ("bb", 64), ("bt", 80), ("pfb", 48), ("df", 48), ("se0", 48), ("se1", 32),
                     ("fl", 32), ("k0", 64), ("k1", 64), ("k2", 64), ("tv", 64), ("qf", 96), ("cht", 64)]),
        ("wb", BF, [("zb", 256), ("ob", 256), ("mw", 64), ("nw", 64), ("jd", 256 * ND), ("js", 256 * ND)])):
    _o = 0
    for _n, _w in _names:
        ALIAS[_n] = (_b, _o, _w)
        _o += _w
    _sb(_b, _o, _d)
for _t in range(R):
    _sb("qh%d" % _t, 16, F32)
    _sb("hl%d" % _t, 128, BF)
    for _s, _w in (("a", 160), ("b", 128), ("r", 256)):
        _sb("c%s%d" % (_s, _t), _w, CODE)
        _sb("p%s%d" % (_s, _t), _w, PLANE)
for _t in range(R + 1):
    _sb("ct%d" % _t, 512, CODE)
    _sb("pt%d" % _t, 512, PLANE)
SCRATCH["ps"] = ("psum", [128, 4096], F32)

SEMAPHORES = ["kv", "ka", "kt", "kg", "ls", "dx", "du", "dw", "dn", "dm", "dh", "dout", "an"] + \
    ["%s%d" % (_s, _t) for _s in ("ah", "az", "aa", "ab") for _t in range(R)]

OP = AluOpType
ACT = ActivationFunctionType


def rank_program(g, core, T, topo):
    rank = T.rank_of(core)
    if rank is None:
        return
    cores = list(T.cores)
    queues = {"v": g.vector, "a": g.scalar, "t": g.tensor, "g": g, "s": g.sync}
    own_sem = {"v": "kv", "a": "ka", "t": "kt", "g": "kg"}
    count = {s: 0 for s in SEMAPHORES}
    known = {q: {} for q in queues}
    hist = {}
    ops = []

    def V(name, c0=0, c1=None, s=1, p0=0, p1=128):
        if name in ALIAS:
            b, o, w = ALIAS[name]
            return (b, o + c0, o + (w if c1 is None else c1), s, p0, p1)
        return (name, c0, SCRATCH[name][1][1] if c1 is None else c1, s, p0, p1)

    def on(x, p0, p1):
        return x[:4] + (p0, p1)

    def IND(win, off):
        return ("*", win, off)

    def ap(x):
        if not isinstance(x, tuple):
            return x
        if x[0] == "*":
            return ap(x[1]).indirect(ap(x[2]))
        name, c0, c1, s, p0, p1 = x
        return T[name][p0:p1, c0:c1] if s == 1 else T[name][p0:p1, c0:c1:s]

    def flat(xs):
        o = []
        for x in xs:
            if isinstance(x, tuple):
                o += [x[1], x[2]] if x[0] == "*" else [x]
        return o

    def meet(a, b):
        if a[2] <= b[1] or b[2] <= a[1] or a[5] <= b[4] or b[5] <= a[4]:
            return False
        return not (a[3] > 1 and a[3] == b[3] and (a[1] - b[1]) % a[3] != 0)

    def covers(a, b):
        return a[1] <= b[1] and b[2] <= a[2] and a[4] <= b[4] and b[5] <= a[5] and (a[3] == 1 or (a[3] == b[3] and (a[1] - b[1]) % a[3] == 0))

    def size(x):
        return 16 * size(x[2]) if x[0] == "*" else (x[2] - x[1] + x[3] - 1) // x[3]

    def narrow(*xs):
        return all(SCRATCH[x[0]][2] in (BF, U16) for x in xs)

    def add(q, call, outs, ins, cost, lat=HOP, sem=None, chain=False, ahead=0.0):
        outs, ins = flat(outs), flat(ins)
        pre = set()
        for regs, wr in ((ins, False), (outs, True)):
            for x in regs:
                for (y, yw, k) in hist.get(x[0], ()):
                    if (wr or yw) and meet(x, y):
                        pre.add(k)
        k = len(ops)
        for x in outs:
            hist[x[0]] = [e for e in hist.get(x[0], ()) if not covers(x, e[0])]
        for regs, wr in ((ins, False), (outs, True)):
            for x in regs:
                hist.setdefault(x[0], []).append((x, wr, k))
        ops.append({"q": q, "call": call, "pre": sorted(pre), "cost": cost, "lat": lat, "sem": sem, "ahead": ahead, "chain": chain})

    def vcost(out, x, *more, k=1):
        if x[0] == "*":
            return 0.05 + 1.56 * CYCLE * size(x)
        return CYCLE * max(64, k * size(x) * (0.5 if k == 1 and narrow(out, x, *more) else 1))

    def acost(x):
        return 0.065 + 1.56 * CYCLE * size(x) if x[0] == "*" else 0.055 + CYCLE * size(x)

    def wait(q, sem, val):
        if known[q].get(sem, 0) < val:
            queues[q].wait_ge(T.sem[sem], val)
            known[q][sem] = val

    def issue():
        n = len(ops)
        post = [[] for _ in range(n)]
        for k, o in enumerate(ops):
            for j in o["pre"]:
                post[j].append(k)

        def gap(j, k):
            return 0.0 if ops[k]["chain"] and ops[j]["q"] == "t" else ops[j]["lat"]
        left = [0.0] * n
        for k in range(n - 1, -1, -1):
            left[k] = ops[k]["ahead"] + ops[k]["cost"] + max([gap(k, j) + left[j] for j in post[k]] + [ops[k]["lat"]])
        need = [len(o["pre"]) for o in ops]
        ready = [0.0] * n
        cand = {q: [] for q in queues}
        free = {q: 0.0 for q in queues}
        for k in range(n):
            if not need[k]:
                cand[ops[k]["q"]].append(k)
        done = []
        while len(done) < n:
            best = None
            for q, cs_ in cand.items():
                if not cs_:
                    continue
                top = max(cs_, key=lambda k: (left[k], -k))
                at = max(free[q], ready[top])
                fit = [k for k in cs_ if max(free[q], ready[k]) + ops[k]["cost"] <= at + 0.01]
                k = min(fit, key=lambda k: (max(free[q], ready[k]), -left[k], k)) if fit else top
                at = max(free[q], ready[k])
                if best is None or at < best[0]:
                    best = (at, k)
            at, k = best
            o = ops[k]
            cand[o["q"]].remove(k)
            free[o["q"]] = at + o["cost"]
            done.append(k)
            for j in post[k]:
                ready[j] = max(ready[j], at + o["cost"] + gap(k, j))
                need[j] -= 1
                if not need[j]:
                    cand[ops[j]["q"]].append(j)
        sig = {}
        for k in done:
            o = ops[k]
            want = {}
            for j in o["pre"]:
                if not (o["chain"] and ops[j]["q"] == "t"):
                    s_, v_ = sig[j]
                    want[s_] = max(want.get(s_, 0), v_)
            for s_, v_ in want.items():
                wait(o["q"], s_, v_)
            if o["sem"] is None:
                s_ = own_sem[o["q"]]
                o["call"]().then_inc(T.sem[s_], 1)
                count[s_] += 1
                sig[k] = (s_, count[s_])
            else:
                sig[k] = o["call"]()

    def cp(out, in_, q="v"):
        if q == "v":
            add("v", lambda: g.vector.tensor_copy(ap(out), ap(in_)), [out], [in_], vcost(out, in_))
        else:
            add("a", lambda: g.scalar.activation(ap(out), ap(in_), ACT.Copy), [out], [in_], acost(in_))

    def scale(out, in_, s):
        add("a", lambda: g.scalar.activation(ap(out), ap(in_), ACT.Copy, scale=ap(s)), [out], [in_, s], acost(in_))

    def tt(out, a, b, op):
        add("v", lambda: g.vector.tensor_tensor(ap(out), ap(a), ap(b), op), [out], [a, b], vcost(out, a, k=2))

    def ts(out, a, s1, op0, s2=None, op1=None):
        if op1 is None:
            add("v", lambda: g.vector.tensor_scalar(ap(out), ap(a), ap(s1), None, op0), [out], [a, s1], vcost(out, a))
        else:
            add("v", lambda: g.vector.tensor_scalar(ap(out), ap(a), ap(s1), ap(s2), op0, op1), [out], [a, s1, s2], vcost(out, a))

    def red(out, a, op):
        add("v", lambda: g.vector.tensor_reduce(ap(out), ap(a), AxisListType.X, op), [out], [a], vcost(out, a))

    def scan(out, d0, d1, op0, op1, first=0.0):
        add("v", lambda: g.vector.tensor_tensor_scan(ap(out), ap(d0), ap(d1), ap(first), op0, op1), [out], [d0, d1, first], vcost(out, d0, d1))

    def tr(out, a):
        add("v", lambda: g.vector.transpose(ap(out), ap(a)), [out], [a], vcost(out, a))

    def fill(out, c):
        add("v", lambda: g.vector.memset(ap(out), c), [out], [], vcost(out, out))

    def sign(out, a, bias, accum=None):
        add("a", lambda: g.scalar.activation(ap(out), ap(a), ACT.Sign, bias=ap(bias), accum_out=ap(accum)), [out, accum], [a, bias], acost(a) + 0.02)

    def total_of(out, a, accum):
        add("a", lambda: g.scalar.activation(ap(out), ap(a), ACT.Copy, accum_out=ap(accum)), [out, accum], [a], acost(a) + 0.02)

    def shift(out, a, bias):
        add("a", lambda: g.scalar.activation(ap(out), ap(a), ACT.Identity, bias=ap(bias)), [out], [a, bias], acost(a))

    def iota(out, pattern, base, mult):
        if SCRATCH[out[0]][2] == I32:
            add("g", lambda: g.iota(ap(out), pattern, base, mult), [out], [], 0.13 + 2 * CYCLE * size(out))
        else:
            add("g", lambda: g.iota(ap(out), pattern, base, mult, allow_small_or_imprecise_dtypes=True), [out], [], 0.13 + 2 * CYCLE * size(out))

    def quant(c, s, a):
        add("v", lambda: g.vector.quantize_mx(ap(c), ap(s), ap(a)), [c, s], [a], 0.012 + 0.00022 * size(a))

    def mm(out, lc, ls_, rc, rs, start, stop, ahead=0.0):
        add("t", lambda: g.tensor.matmul_mx(ap(out), ap(lc), ap(ls_), ap(rc), ap(rs), start, stop), [out], [lc, ls_, rc, rs],
            0.0006 * (size(rc) + 16), chain=not start, ahead=ahead)

    def pick(oc_, op_, wc, wp, off):
        add("v", lambda: g.vector.tensor_copy(ap(oc_).bitcast(dt.uint32), ap(wc).bitcast(dt.uint32).indirect(ap(off))), [oc_], [wc, off],
            vcost(oc_, IND(wc, off)))
        cp(op_, IND(wp, off), "a")

    def dma(q, out, in_, sem, outs=(), ins=(), total=None, lat=LOCAL):
        def call():
            queues[q].dma_start(out, in_).then_inc(T.sem[sem], 16)
            count[sem] += 16
            return sem, total or count[sem]
        add(q, call, list(outs), list(ins), 0.05, lat, sem)

    def bits(m):
        return bin(m).count("1")

    def dst(c):
        rid, pid, _ = topo.addr(c)
        return DstId(rid=rid, pnc=pid)

    def split(src):
        i0 = cores.index(src)
        others = [cores[(i0 + k) % N] for k in range(1, N)]
        near_ = [c for c in others if topo.chip(c) == topo.chip(src)]
        far = [c for c in others if topo.chip(c) != topo.chip(src)]
        mf_ = topo.mask(src, far[0])
        for c in far:
            mf_ &= topo.mask(src, c)
        mn = topo.mask(src, near_[0]) & ~mf_
        return near_, far, mn, mf_

    def allgather(src, buf, w, sem, lat=FAR, cost=0.1):
        def call():
            near_, far, mn, mf_ = split(core)
            land = ap(V(buf, w * rank, w * rank + w))
            g.remote_dma_fused([RemoteDMATransfer(dst_ids=[dst(c) for c in cs_], dma_engine_mask=m, remote_sem=T.sem[sem],
                                                  srcs=[ap(src)], dsts=[land for _ in cs_]) for cs_, m in ((far, mf_), (near_, mn))],
                               local_sem=T.sem.ls)
            count["ls"] += bits(mf_) + bits(mn)
            for c in cores:
                if c != core:
                    n2, f2, mn2, mf2 = split(c)
                    count[sem] += bits(mn2) if core in n2 else bits(mf2)
            return sem, count[sem]
        others = [V(buf, a, b) for a, b in ((0, w * rank), (w * rank + w, w * N)) if a < b]
        add("g", call, others, [src], cost, lat, sem)

    def spread(moves, cb, pb, sem, lands, reads):
        def call():
            _, _, mn, mf_ = split(core)
            en = [e for e in topo.engines(core, moves[1][0]) if mf_ >> e & 1]
            masks = [mn, sum(1 << e for e in en[:len(en) // 2]), sum(1 << e for e in en[len(en) // 2:])]
            for b_, view in ((cb, lambda x: ap(x).bitcast(dt.uint8)), (pb, ap)):
                g.remote_dma_fused([RemoteDMATransfer(dst_ids=[dst(c)], dma_engine_mask=m, remote_sem=T.sem[sem],
                                                      srcs=[view(V(b_, a, a + H))], dsts=[view(V(b_, b, b + H))])
                                    for (c, a, b), m in zip(moves, masks)], local_sem=T.sem.ls)
            count["ls"] += 2 * sum(bits(m) for m in masks)
            count[sem] += 2 * sum(bits(m) for m in masks)
            return sem, count[sem]
        add("g", call, [V(b_, a, a + H) for b_ in (cb, pb) for a in lands], [V(b_, *reads) for b_ in (cb, pb)], 0.2, FAR + 0.2, sem)

    me = topo.chip(core)
    half = rank % 2
    near = [c for c in cores if c != core and topo.chip(c) == me][0]
    mate = sorted([c for c in cores if topo.mates(topo.chip(c), me)], key=lambda c: cores.index(c) % 2 != half)
    plane = sorted([c for c in cores if topo.same_plane(topo.chip(c), me)], key=lambda c: cores.index(c) % 2 != half)
    set_c = [k for k in range(N) if topo.chip(cores[k]) not in (me, topo.chip(mate[0]))]
    assert set_c == list(range(set_c[0], set_c[0] + len(set_c))) and cores.index(near) // 2 == rank // 2
    assert len(mate) == 2 and len(plane) == 2 and cores.index(mate[0]) // 2 == cores.index(mate[1]) // 2

    def turn(place, src, nc):
        tr(place(0, 0), src)
        pairs = [(a, b) for a in range(4) for b in range(4) if (a - b) % 2]
        for a, b in pairs[:nc]:
            cp(on(place(a, b), 32 * b, 32 * b + 32), on(place(0, 0), 32 * a, 32 * a + 32), "a")
        tr(on(place(0, 2), 64, 128), on(src, 0, 64))
        tr(on(place(2, 0), 0, 64), on(src, 64, 128))
        for a, b in pairs[nc:]:
            tr(on(place(a, b), 32 * b, 32 * b + 32), on(src, 32 * a, 32 * a + 32))

    def table(tb, src):
        turn(lambda a, b: V(tb, 96 + 32 * (a - b), 128 + 32 * (a - b)), src, NC)

    dma("a", T.nbs[0:16, :], T.nb[:], "dn", [V("nbs", p1=16)], total=32)
    dma("a", T.nbs[16:32, :], T.nb[:], "dn", [V("nbs", p0=16, p1=32)], total=32)
    dma("s", T.xs[:], T.x[:], "dx", [V("xs")], lat=2.0)
    dma("s", T.us[:], T.u[:], "du", [V("us")], lat=1.9)

    CI = {n: V("ci", k, k + 1) for k, n in enumerate(
        ["p", "i", "g", "h", "lo", "hi", "r", "e", "i1", "i2", "i3", "ne", "t2", "t3", "t7", "t8", "t9",
         "s0", "s1", "s2", "s3", "s4", "s5", "n3", "n4", "n5", "n6"])}
    CF = {n: V("cf", k, k + 1) for k, n in enumerate(
        ["p", "i", "g", "h", "lo", "hi", "r", "coff", "base", "sO", "cC", "t0", "t1", "coff2", "bin"])}
    LO, LY, L3, LQ, LF, LH, LD = [V("lst", a, b) for a, b in ((2, 5), (6, 7), (10, 13), (22, 23), (26, 27), (28, 29), (40, 42))]
    AND, SHR = OP.bitwise_and, OP.logical_shift_right
    io32 = V("io128", 0, 32)
    iota(CI["p"], [[0, 1]], 0, 1)
    iota(V("jr"), [[1, 48]], 0, 0)
    iota(V("io128"), [[1, 128]], 0, 0)
    iota(V("sv3"), [[1, 16], [0, 3]], 0, 0)
    iota(V("sv", 0, 128), [[1, 8], [16, 16]], 1, 0)
    P = CI["p"]
    ts(CI["i"], P, 15, AND)
    ts(CI["g"], P, 4, SHR)
    ts(CI["h"], P, 4, SHR, 1, AND)
    ts(CI["lo"], P, 5, SHR, 1, AND)
    ts(CI["hi"], P, 6, SHR)
    ts(CI["r"], P, 31, AND)
    cp(V("cf", 0, 7), V("ci", 0, 7))
    ts(CI["e"], P, 1, AND)
    ts(V("mk", 0, 31), V("io128", 0, 31), CF["i"], OP.is_lt)
    ts(V("eq8", 0, 8), V("io128", 0, 16, 2), CF["i"], OP.not_equal, -BIG, OP.mult)
    fill(V("z128"), 0.0)
    for k in range(16):
        if k % 2:
            shift(V("eqn", 128 * k, 128 * k + 128), V("z128"), V("eq8", k % 8, k % 8 + 1))
        else:
            ts(V("eqn", 128 * k, 128 * k + 128), V("z128"), V("eq8", k % 8, k % 8 + 1), OP.add)
    fill(V("mk", 31, 32), 1.0)
    for b_ in ("xx", "tbp", "tbs", "qd", "ctb", "h0", "hz", "tv", "nn", "zo", "zero", "k0"):
        fill(V(b_), 0.0)
    for c_ in (0, 224):
        fill(V("tbh", c_, c_ + 224), 0.0)
    for c_ in (271, 543):
        fill(V("sp", c_, c_ + 1), 0.0)
    w_ = 32
    while w_ < MKW:
        n_ = min(w_, MKW - w_, 256)
        cp(V("mk", w_, w_ + n_), V("mk", 0, n_), "a")
        w_ += n_
    ts(CF["t0"], CI["hi"], -64.0, OP.mult, 96.0, OP.add)
    tt(CI["ne"], CI["e"], CI["h"], OP.not_equal)
    ts(CI["t2"], CI["h"], -32.0, OP.mult, 96.0, OP.add)
    tt(CI["t3"], CI["i"], CI["e"], OP.subtract)
    ts(CF["coff"], CI["lo"], -32.0, OP.mult, CF["t0"], OP.add)
    tt(CI["t2"], CI["t2"], CI["ne"], OP.mult)
    tt(CI["t3"], CI["t3"], CI["h"], OP.add)
    tt(CF["sO"], CI["t2"], CI["t3"], OP.add)
    ts(LO, V("jr", 0, 3), 16.0, OP.mult, CF["sO"], OP.add)
    ts(CI["n3"], CI["t3"], 5.0, OP.min)
    ts(CI["n4"], CI["t3"], 3.0, OP.is_ge, 3.0, OP.mult)
    ts(CI["n5"], CI["e"], 3.0, OP.mult)
    tt(CI["n3"], CI["n3"], CI["n4"], OP.add)
    tt(CI["n3"], CI["n3"], CI["n5"], OP.add)
    cp(LY, CI["n3"])
    ts(CI["n6"], P, 7, AND)
    ts(V("lst", 40, 41), CI["n6"], 0.0, OP.add)
    ts(V("lst", 41, 42), CI["n6"], 8.0, OP.add)
    ts(CF["coff2"], CF["coff"], 2.0, OP.mult)
    ts(V("tmpi", 96, 99), V("jr", 0, 3), 16.0, OP.mult, CF["i"], OP.add)
    ts(L3, V("tmpi", 96, 99), -1.0, OP.add, 1.0 / 3, OP.mult)
    ts(CF["t1"], P, 32.0, OP.mult)
    ts(V("sn3"), V("sv3"), 128.0, OP.mult, CF["p"], OP.add)
    ts(V("sv3"), V("sv3"), CF["t1"], OP.add)
    cp(V("h1", 6, 112, 7), V("sv3", 0, 48, 3))
    fill(V("h1", 5, 112, 7), 0.0)
    for b_, n_, hi_, lo_ in (("rs24", 24, 2 * BIG, -2 * BIG), ("rst", 16, 1.0, 0.0)):
        fill(V(b_), hi_)
        fill(V(b_, 0, None, n_), lo_)
    ts(CI["i2"], P, 2, SHR, 1, AND)
    fill(V("cn"), -4095.0 / 32)
    fill(V("ob"), 1.0)
    ts(CF["base"], P, 16.0, OP.mult)
    ts(CF["bin"], P, 16.0, OP.mult, float(NA), OP.add)
    ts(V("th"), V("io128", 0, 16), CF["base"], OP.add, -1.0, OP.mult)
    ts(V("th"), V("th"), 0.5, OP.add)
    ts(CI["i1"], P, 1, SHR, 1, AND)
    ts(CI["i3"], P, 3, SHR, 1, AND)
    ts(CI["s0"], CI["h"], -1.0, OP.mult, 3.0, OP.add)
    ts(V("tmpi", 104, 112), V("jr", 0, 8), 1, SHR, 1, AND)
    ts(V("tmpi", 112, 120), V("jr", 0, 8), 2, SHR)
    ts(V("tmpi", 120, 128), V("jr", 0, 8), 1, AND)
    tt(CI["s0"], CI["s0"], CI["ne"], OP.mult)
    tt(CI["s1"], CI["i1"], CI["lo"], OP.not_equal)
    tt(CI["s2"], CI["i2"], CI["hi"], OP.not_equal)
    ts(CI["s3"], CI["i3"], 32.0, OP.mult, 15.0, OP.add)
    ts(CI["s4"], CI["e"], 16.0, OP.mult)
    ts(V("tmpi", 104, 112), V("tmpi", 104, 112), CF["lo"], OP.not_equal, 32.0, OP.mult)
    ts(V("tmpi", 112, 120), V("tmpi", 112, 120), CF["hi"], OP.not_equal, 64.0, OP.mult)
    ts(V("tmpi", 120, 128), V("tmpi", 120, 128), 128.0, OP.mult, CF["r"], OP.add)
    tt(CI["s0"], CI["s0"], CI["i1"], OP.add)
    ts(CI["s1"], CI["s1"], 64.0, OP.mult)
    ts(CI["s2"], CI["s2"], 128.0, OP.mult)
    tt(CI["s3"], CI["s3"], CI["s4"], OP.add)
    ts(CI["s5"], CI["h"], 16.0, OP.mult, 15.0, OP.add)
    ts(CI["t7"], CI["e"], 32.0, OP.mult)
    tt(V("tmpi", 104, 112), V("tmpi", 104, 112), V("tmpi", 112, 120), OP.add)
    ts(V("tmpi", 120, 128), V("tmpi", 120, 128), float(M * rank), OP.add)
    ts(LQ, CI["s0"], 2.0, OP.mult, float(half), OP.add)
    for k, o_ in enumerate((1 - half, 16 + half, 17 - half)):
        ts(V("lst", 30 + 2 * k, 31 + 2 * k), CI["s0"], 2.0, OP.mult, float(o_), OP.add)
    tt(CI["s1"], CI["s1"], CI["s2"], OP.add)
    tt(CI["s5"], CI["s5"], CI["t7"], OP.add)
    tt(V("my8", 0, 8), V("tmpi", 104, 112), V("tmpi", 120, 128), OP.add)
    tt(CI["s1"], CI["s1"], CI["s3"], OP.add)
    cp(LH, CI["s5"])
    cp(LF, CI["s1"])
    ts(V("mym"), V("jr", 0, 16), 16.0, OP.mult, CF["i"], OP.add)
    ts(CI["t8"], CI["g"], float(set_c[0]), OP.is_ge, float(K), OP.mult)
    ts(CI["t9"], CI["g"], float(set_c[-1]), OP.is_le)
    ts(V("sv", 128, 256), V("sv", 0, 128), 128.0, OP.is_gt, 128.0, OP.mult)
    tt(V("sv", 0, 128), V("sv", 0, 128), V("sv", 128, 256), OP.add)
    ts(V("sv", 128, 256), V("sv", 0, 128), 8.0, OP.add)
    ts(V("dum"), V("mym"), float(DUMMY), OP.add)
    tt(CF["cC"], CI["t8"], CI["t9"], OP.mult)
    fill(V("c128"), 128.0)
    ts(V("odd"), io32, 2.0, OP.mult, 1.0, OP.add)
    ts(V("nodd"), io32, -2.0, OP.mult, -1.0, OP.add)
    fill(V("bt", 0, 1), 0.0)
    fill(V("k0", 3, 64, 4), 1.0)
    fill(V("qn", 48, 64), 0.0)
    ts(V("pfb", 0, 1), P, float(32 - NS), OP.mult, 128.0 * NS, OP.add)
    ts(V("pfb", 33, 34), P, float(-NS), OP.mult, 128.0 * NS, OP.add)
    for b in range(4):
        fill(V("et", 512 * b, 512 * b + 512), 0.0)
        ts(V("et", 512 * b + b, 512 * b + 512, 4), V("io128"), CF["p"], OP.is_equal)
        quant(V("qe", 128 * b, 128 * b + 128), V("se", 128 * b, 128 * b + 128), V("et", 512 * b, 512 * b + 512))

    for a in range(4):
        for e in range(2):
            cp(V("so", e, 12, 2, 32 * a, 32 * a + 32), V("nbs", 2 * a + e, 48, 8, 0, 32))
    tt(V("so", 16, 20), V("so", 0, 4), V("so", 4, 8), OP.min)
    tt(V("so", 20, 24), V("so", 0, 4), V("so", 4, 8), OP.max)
    tt(V("so", 24, 28), V("so", 20, 24), V("so", 8, 12), OP.min)
    tt(V("so", 32, 44, 3), V("so", 16, 20), V("so", 8, 12), OP.min)
    tt(V("so", 34, 44, 3), V("so", 20, 24), V("so", 8, 12), OP.max)
    tt(V("so", 33, 44, 3), V("so", 16, 20), V("so", 24, 28), OP.max)
    cp(V("nbo"), IND(V("so", 32, 44), LY))
    allgather(V("nbo", 0, 6), "nbl", 6, "an", FAR, 1.1)
    dma("s", ap(V("nbl", 6 * rank, 6 * rank + 6)), ap(V("nbo", 0, 6)), "dm", [V("nbl", 6 * rank, 6 * rank + 6)], [V("nbo", 0, 6)])
    for u in range(2):
        quant(V("ct0", M * u, M * u + 128), V("pt0", M * u, M * u + 128), V("xs", 512 * u, 512 * u + 512))
    quant(V("qu"), V("su"), V("us"))

    def products(t, c0):
        for u in range(2):
            mm(V("ps", 2048 * u, 2048 * u + 128), V("ct%d" % t, c0 + M * u, c0 + M * u + 128), V("pt%d" % t, c0 + M * u, c0 + M * u + 128),
               V("qu"), V("su"), True, True)

    def unpack(c, s, first, w):
        for u in range(2):
            for b in range(4):
                mm(V("ps", 2048 * u + 512 * b, 2048 * u + 512 * b + 128), V("qe", 128 * b, 128 * b + 128), V("se", 128 * b, 128 * b + 128),
                   V(c, w * u, w * u + 128), V(s, w * u, w * u + 128), first, not first, 0.0 if first else 0.1 * (7 - 4 * u - b))

    def heights(t):
        if t == 0:
            products(0, 0)
            cp(V("hs", 0, 2), V("ps", 0, 2049, 2048))
        else:
            products(t - 1, 128)
            for u in range(2):
                ts(V("hs", 4 * t + u, 4 * t + u + 1), V("ps", 2048 * u + t, 2048 * u + t + 1), V("ff", u, u + 1), OP.mult, V("ho", u, u + 1), OP.add)
        mine, own = V("hs", 4 * t, 4 * t + 2), V("qh%d" % t, 2 * rank, 2 * rank + 2)
        allgather(mine, "qh%d" % t, 2, "ah%d" % t, FAR if t else FAR + 0.4)
        dma("s", ap(own), ap(mine), "dh", [own], [mine])

    heights(0)
    dma("s", T.ws[:], T.w[:], "dw", [V("ws")], [V("hs", 0, 2)], lat=2.0)
    quant(V("qw"), V("sw"), V("ws"))

    for k in range(4):
        cp(V("mt3", 192 * k, 192 * k + 192), IND(V("eqn"), V("nbl", 12 * k, 12 * k + 12)), "a")
    cp(V("ni", 0, 48), V("nbl"))
    ts(V("ni", 48, 96), V("ni", 0, 48), 127, AND)
    ts(V("ni", 96, 144), V("ni", 0, 48), 96, AND)
    ts(V("ni", 144, 192), V("ni", 0, 48), 5, SHR, 32, AND)
    ts(V("qf", 0, 48), V("ni", 48, 96), CF["coff2"], OP.add)
    tt(V("hm"), V("ni", 96, 144), V("ni", 144, 192), OP.add)
    tt(V("qf", 0, 48), V("qf", 0, 48), V("hm"), OP.add)
    cp(V("on"), V("qf", 0, 48))
    cp(V("qn", 0, 48), V("nbl"))
    tr(V("xx", 16, 80), V("qn", 0, 64))
    tr(V("qn", 64, 160), V("xx"))
    cp(V("tmpi", 0, 48), IND(V("qn"), LO))
    ops[-1]["ahead"] = 2.0
    ts(V("tmpi", 48, 96), V("tmpi", 0, 48), 127, AND)
    ts(V("qi", 0, 48), V("tmpi", 0, 48), 7, SHR)
    tt(V("bm"), V("tmpi", 0, 48), V("sn3"), OP.is_lt)
    ts(V("so2"), V("tmpi", 48, 96), 32.0, OP.mult)
    tt(V("so"), V("qi", 0, 48), V("sv3"), OP.subtract)
    tt(V("so2"), V("so2"), V("so"), OP.add)
    scale(V("bm"), V("bm"), -BIG)
    for j in range(J):
        cp(V("h1", 4 - 2 * j, 112, 7), V("so2", j, 48, 3), "a")
        if j < J - 1:
            scale(V("h1", 3 - 2 * j, 112, 7), V("so2", j, 48, 3), -1.0)

    def lookup(src, c0, s, d, pieces):
        for a, b, q in pieces:
            x = V(src, c0 + s * (a // 16), c0 + s * (b // 16 - 1) + 1, s)
            o2, oo = V("o2", 16 * d + a // 16, 16 * d + b // 16), V("oo", 16 * d + a // 16, 16 * d + b // 16)
            mg, mt, gm, tt_ = [V(n_, 256 * d + a, 256 * d + b) for n_ in ("mg", "mt", "gm", "tt")]
            cp(o2, x)
            ts(oo, x, 1.0 / 32, OP.mult, CF["coff"], OP.add)
            cp(mg, IND(V("mk"), o2), "a")
            cp(gm, IND(V("tbp"), oo), q)
            tr(mt, mg)
            tr(tt_, gm)
            scan(V("sp", 272 * d + a, 272 * d + b), mt, tt_, OP.mult, OP.add)

    def pointers(src, c0, s):
        for k in range(2):
            tt(V("dd", 16 * k, 16 * k + 16), V(src, c0, c0 + 15 * s + 1, s), V(src, c0 + s, c0 + 16 * s + 1, s), OP.subtract)
        table("tbp", V("dd"))

    def walk(out, x, d):
        o2, oo = V("ow", 4 * d, 4 * d + 2), V("ow", 4 * d + 2, 4 * d + 4)
        mg, mt, gm, tt_ = [V(n_, 32 * d, 32 * d + 32) for n_ in ("mw", "nw", "gw", "tw")]
        cp(o2, x)
        ts(oo, x, 1.0 / 32, OP.mult, CF["coff"], OP.add)
        cp(mg, IND(V("mk"), o2), "a")
        cp(gm, IND(V("tbp"), oo))
        tr(mt, mg)
        tr(tt_, gm)
        scan(out, mt, tt_, OP.mult, OP.add)

    for t in range(R):
        ct, pt, qh, hl = "ct%d" % t, "pt%d" % t, "qh%d" % t, "hl%d" % t
        cp(V("qd", 0, 64, 2), IND(V(qh), LD))
        tt(V("hm"), IND(V(qh), L3), V("bm"), OP.add)
        turn(lambda a, b: V("tbh", 192 + 64 * (a - b), 256 + 64 * (a - b)), V("qd"), 1)
        for k in range(2):
            gn, tn, mt3 = [V(n_, 384 * k, 384 * k + 384) for n_ in ("gn", "tn", "mt3")]
            tt(gn, IND(V("tbh"), V("on", 24 * k, 24 * k + 24)), mt3, OP.add)
            tr(tn, gn)
            scan(V("sn", 192 * k, 192 * k + 192), V("rs24"), V("tn", 384 * k, 384 * k + 384, 2), OP.min, OP.max)
        top = V("sn", 23, 384, 24)
        tt(V("h0", 6, 112, 7), V(qh), top, OP.is_le)
        for j in range(J):
            tt(V("h0", 5 - 2 * j, 112, 7), V("hm", j, 48, 3), top, OP.is_lt)
        for j in range(J - 1):
            tt(V("h0", 4 - 2 * j, 112, 7), V("sn", 8 * j + 7, 384, 24), top, OP.is_lt)
        scan(V("hz", 0, 112), V("h0"), V("h1"), OP.mult, OP.add)
        for step in range(6):
            src = ("hz", 6, 7) if step == 0 else ("sp", 272 + 15, 16)
            pointers(*src)
            lookup(*src, 0, PIECES_R)
            lookup("sp", 15, 16, 1, PIECES_W)
        pointers("sp", 272 + 15, 16)
        walk(V("w1"), V("sp", 272 + 32 * rank + 15, 272 + 32 * rank + 32, 16), 0)
        walk(V("w2"), V("w1", 15, 32, 16), 1)
        ts(V("cv", 0, 2), V("w2", 15, 32, 16), ROUND32, OP.add, ROUND32, OP.subtract)
        ts(V("cv", 2, 4), V("w2", 15, 32, 16), 128.0, OP.mult)
        for u in range(2):
            ts(V("yb", 32 * u, 32 * u + 32), V("cn"), V("cv", u, u + 1), OP.mult, V("cv", 2 + u, 3 + u), OP.add)
        turn(lambda a, b: V("rf", 64 * (a ^ b), 64 * (a ^ b) + 64), V("yb"), 1)
        ts(V("zb"), V("rf"), CF["base"], OP.subtract)
        for k in range(NA + 1):
            sign(V("ja", 256 * k, 256 * k + 256), V("rf"), V("th", k, k + 1), V("acc", k, k + 1))
        ts(V("jd", 0, 256), V("rf"), CF["bin"], OP.is_equal, 2.0, OP.mult)
        for k in range(1, ND):
            ts(V("jd", 256 * k, 256 * k + 256), V("zb"), float(NA + k), OP.is_equal, 2.0, OP.mult)
        for k in range(ND):
            scan(V("js", 256 * k, 256 * k + 256), V("ob"), V("jd", 256 * k, 256 * k + 256), OP.mult, OP.add)
        cp(V(hl, 16 * rank + NA, 16 * rank + 16), V("js", 255, 256 * ND, 256))
        tt(V(hl, 16 * rank, 16 * rank + NA), V("acc", 0, NA), V("acc", 1, NA + 1), OP.subtract)
        allgather(V(hl, 16 * rank, 16 * rank + 16), hl, 16, "az%d" % t)
        tr(V("rt2"), V("rf"))
        fill(V("lw", 0, 112), 0.0)
        cp(V("qi", 0, 8), V("rt2", 0, 256, 32))
        ts(V("qi", 8, 16), V("qi", 0, 8), 4, SHR)
        ts(V("qi", 24, 32), V("qi", 0, 8), 15, AND)
        ts(V("qf", 48, 56), V("qi", 24, 32), 15.0, OP.add)
        for e in range(2):
            ts(V("o3", e, 16, 2), V("qi", 8, 16), CF["coff"], OP.add)
        for u in range(2):
            cp(V("nn", 4 * u, 4 * u + 4), V("rt2", 32 * u, 256, 64))
        tt(V("qf", 56, 64), V("rt2", 0, 256, 32), V("my8", 0, 8), OP.not_equal)
        tr(V("nt", 32 * t, 32 * t + 32, 1, 0, 32), V("nn", p1=32))
        tt(V("qf", 48, 56), V("qf", 48, 56), V("qf", 56, 64), OP.mult)
        dma("s", T.rt[0:1, M * t:M * t + M], ap(V("nt", 32 * t, 32 * t + 32, 1, 0, 8)), "dout", ins=[V("nt", 32 * t, 32 * t + 32, 1, 0, 32)])
        for e in range(2):
            ts(V("o4", e, 16, 2), V("qf", 48, 56), 16.0, OP.add)
        for k in range(2):
            cp(V("mgs", 128 * k, 128 * k + 128), IND(V("mk", 0, 64), V("o4", 8 * k, 8 * k + 8)), "a")
        for k in range(16):
            if k < 16 - NS:
                red(V("sz", k, k + 1), V(hl, k, 128, 16), OP.add)
            else:
                total_of(V("s1", 8 * k, 8 * k + 8), V(hl, k, 128, 16), V("sz", k, k + 1))
        ts(V("szh"), V("sz"), 0.5, OP.mult)
        for k in range(16):
            if k < 16 - NS:
                ts(V("th0", k, 512, 16), V("odd"), V("sz", k, k + 1), OP.is_lt, 2.0, OP.mult)
            else:
                sign(V("th0", k, 512, 16), V("nodd"), V("sz", k, k + 1))
        scan(V("th1"), V("rst"), V("th0"), OP.mult, OP.add)
        table("ctb", V("th1", 15, 512, 16))
        scan(V("pf2"), V("ob", 0, 224), V("ctb"), OP.mult, OP.add, 128.0 * NS)
        total = V("pf2", 223, 224)
        ts(V("bb", 0, 32), V("c128"), total, OP.is_ge)
        ts(V("bb", 32, 64), V("c128"), total, OP.is_ge, total, OP.mult)
        tr(V("pfb", 1, 33), V("pf2", 95, 127))
        tr(V("bt", 1, 33), V("bb", 0, 32))
        tr(V("bt", 33, 65), V("bb", 32, 64))
        tt(V("df", 0, 33), V("pfb", 0, 33), V("pfb", 1, 34), OP.subtract)
        red(V("cs", 0, 1), V("bt", 1, 33), OP.add)
        scan(V("se0", 0, 33), V("bt", 0, 33), V("df", 0, 33), OP.mult, OP.add)
        scan(V("se1"), V("bt", 0, 32), V("df", 1, 33), OP.mult, OP.add)
        red(V("cs", 1, 2), V("bt", 33, 65), OP.max)
        GT, EQ = V("k0", 1, 64, 4), V("fl", 0, 16)
        ts(GT, V("szh"), V("cs", 0, 1), OP.add, 32.0, OP.is_gt)
        ts(EQ, V("szh"), V("cs", 0, 1), OP.add, 32.0, OP.is_equal)
        ts(V("cs", 2, 3), V("se0", 32, 33), -0.5, OP.mult, V("se1", 31, 32), OP.add)
        ts(V("cs", 3, 4), V("se0", 32, 33), V("se1", 31, 32), OP.subtract, 0.5, OP.mult)
        ts(V("fl", 16, 32), V("szh"), V("cs", 0, 1), OP.add, 32.0, OP.is_lt)
        ts(V("k0", 2, 64, 4), V("szh"), V("cs", 0, 1), OP.add, 32.0, OP.is_ge)
        scan(V("k1", 0, 64, 4), GT, EQ, OP.add, OP.subtract, V("cs", 2, 3))
        scan(V("k1", 1, 64, 4), EQ, V("zero"), OP.add, OP.add, V("cs", 3, 4))
        tt(V("k1", 2, 64, 4), V("fl", 16, 32), V("dum"), OP.mult)
        ts(V("k1", 3, 64, 4), EQ, V("cs", 1, 2), OP.mult, 0.5, OP.mult)
        scan(V("k2"), V("k0"), V("k1"), OP.mult, OP.add)
        val = V("k2", 3, 64, 4)
        ts(V("vo"), val, 15.0, OP.add)
        add("v", lambda: g.vector.tensor_copy(ap(IND(V("lw"), V("vo"))), ap(V("sv"))), [V("lw")], [V("sv"), V("vo")], 0.05 + 3.8 * CYCLE * 256)
        tr(V("lt", 0, 64), V("lw", 16, 80))
        tr(V("lt", 64, 160), V("lw", 0, 96))
        for k, a0 in enumerate((32 * (rank // 2), 32 * (cores.index(mate[0]) // 2))):
            for a in range(4):
                cp(V("zo", 16 * k, 16 * k + 10, 1, 32 * a, 32 * a + 32), V("lt", 0, 160, 16, a0, a0 + 32), "a" if a % 2 else "v")
        ts(V("pl", 0, 16), IND(V("zo", 0, 16), LQ), -1.0, OP.add)
        ca, pa, cc_, pc_, cr, pr = ["%s%s%d" % (x, s_, t) for s_ in "abr" for x in "cp"]
        pick(V(ca, 0, K), V(pa, 0, K), V(ct, 0, M + 128), V(pt, 0, M + 128), V("pl", 0, 4))
        spread([(near, H * (1 - half), 2 * H), (mate[0], H * half, 3 * H), (mate[1], H * (1 - half), 4 * H)], ca, pa, "aa%d" % t, (2 * H, 3 * H, 4 * H), (0, K))
        if t + 1 < R:
            if t:
                products(t, 0)
            cp(V("hp", 0, 2), V("ps", t + 1, 2048 + t + 2, 2048))
        unpack(ct, pt, True, M)
        for k in range(3):
            ts(V("own", 16 * k, 16 * k + 16), IND(V("zo"), V("lst", 30 + 2 * k, 31 + 2 * k)), 0.5, OP.is_gt, float(H * (2 + k - half)), OP.mult)
        c0 = 2 * half
        tt(V("cht", 0, 2), V("own", c0, c0 + 2), V("mym", c0, c0 + 2), OP.add)
        tt(V("cht", 2, 4), V("own", 16 + c0, 18 + c0), V("own", 32 + c0, 34 + c0), OP.add)
        tt(V("cht", 4, 6), V("cht", 0, 2), V("cht", 2, 4), OP.add)
        cp(V("pl", 16, 18), V("cht", 4, 6))
        o_ = H * half
        pick(V(cc_, o_, o_ + H), V(pc_, o_, o_ + H), V(ca), V(pa), V("pl", 16, 18))
        spread([(near, o_, o_), (plane[0], o_, K + o_), (plane[1], o_, K + o_)], cc_, pc_, "ab%d" % t, (H - o_, K, K + H), (o_, o_ + H))
        ts(V("tv", 48, 64), val, 64.5, OP.is_lt)
        ts(V("tv", 32, 48), val, CF["cC"], OP.add)
        tt(V("tv", 0, 16), V("tv", 32, 48), V("tv", 48, 64), OP.mult)
        for k in range(2):
            tt(V("ds", 16 * k, 16 * k + 16), V("tv", 0, 16), V("tv", 1, 17), OP.subtract)
        table("tbs", V("ds"))
        for k in range(2):
            gs, tts, sps, mgs = [V(n_, 128 * k, 128 * k + 128) for n_ in ("gs", "tts", "sps", "mgs")]
            tt(gs, IND(V("tbs"), V("o3", 8 * k, 8 * k + 8)), mgs, OP.mult)
            tr(tts, gs)
            scan(sps, V("rst", 0, 128), tts, OP.mult, OP.add)
        ts(V("pl", 32, 48), IND(V("sps"), LF), -1.0, OP.add)
        ts(V("cht", 48, 64), IND(V("sps"), LF), 0.5, OP.is_gt, 128.0, OP.mult)
        for u in range(2):
            tt(V("cht", 16 + 8 * u, 24 + 8 * u), V("cht", 48 + 8 * u, 56 + 8 * u), V("mym", 0, 8), OP.add)
        cp(V("pl", 48, 64), V("cht", 16, 32))
        if t + 1 < R:
            ts(V("ff"), IND(V("sps"), LH), 0.5, OP.is_gt)
            ts(V("nf"), IND(V("sps"), LH), 0.5, OP.is_lt)
            tt(V("ho", 0, 2), V("hp", 0, 2), V("nf", 0, 2), OP.mult)
        for u in range(2):
            pick(V(cr, 128 * u, 128 * u + 128), V(pr, 128 * u, 128 * u + 128), V(cc_), V(pc_), V("pl", 32 + 8 * u, 40 + 8 * u))
        unpack(cr, pr, False, 128)
        for u in range(2):
            for b in range(4):
                o, i_ = V("ht", 512 * u + b, 512 * u + 512, 4), V("ps", 2048 * u + 512 * b, 2048 * u + 512 * b + 128)
                if b % 2:
                    ts(o, i_, 0.5, OP.mult)
                else:
                    scale(o, i_, 0.5)
            quant(V(ct, M * u + 128, M * u + M), V(pt, M * u + 128, M * u + M), V("ht", 512 * u, 512 * u + 512))
        if t + 1 < R:
            heights(t + 1)
        for u in range(2):
            w_ = M if t + 1 < R else 128
            pick(V("ct%d" % (t + 1), w_ * u, w_ * u + 128), V("pt%d" % (t + 1), w_ * u, w_ * u + 128), V(ct, M * u, M * u + M), V(pt, M * u, M * u + M),
                 V("pl", 48 + 8 * u, 56 + 8 * u))

    ct, pt = "ct%d" % R, "pt%d" % R
    for u in range(2):
        mm(V("ps", 2048 * u, 2048 * u + 128), V("qw"), V("sw"), V(ct, 128 * u, 128 * u + 128), V(pt, 128 * u, 128 * u + 128), True, True)
        cp(V("yo", 128 * u, 128 * u + 128), V("ps", 2048 * u, 2048 * u + 128), "v" if u else "a")
        dma("s", T.oc[:, 512 * u:512 * u + 512], ap(V(ct, 128 * u, 128 * u + 128)).bitcast(dt.uint8), "dout", ins=[V(ct, 128 * u, 128 * u + 128)])
        dma("s", T.y[:, 128 * u:128 * u + 128], T.yo[:, 128 * u:128 * u + 128], "dout", ins=[V("yo", 128 * u, 128 * u + 128)])
    for k in range(4):
        dma("s", T.osc[4 * k:4 * k + 4, :], T[pt][32 * k:32 * k + 4, 0:M], "dout", ins=[V(pt, 0, M)])
    issue()
    for s_ in SEMAPHORES:
        if count[s_]:
            wait("g", s_, count[s_])
